import numpy as np
import ml_dtypes


def mxq(x, axis, fmt="e4m3"):
    dtype, down = {"e4m3": (ml_dtypes.float8_e4m3fn, 7), "e5m2": (ml_dtypes.float8_e5m2, 14)}[fmt]
    v = np.moveaxis(np.asarray(x, np.float32).astype(ml_dtypes.bfloat16).astype(np.float64), axis, -1)
    blocks = v.reshape(v.shape[:-1] + (-1, 32))
    amax = np.abs(blocks).max(-1, keepdims=True)
    byte = np.maximum(np.where(amax > 0, np.frexp(amax)[1] - 1 + 127, 0) - down, 1)
    scale = np.exp2(byte - 127.0)
    codes = (blocks / scale).astype(np.float32).astype(dtype).astype(np.float64)
    return np.moveaxis((codes * scale).reshape(v.shape), -1, axis)


WIDE = False


def mx_kscale(k):
    if not WIDE:
        return np.ones(k)
    levels = np.array([10, -10, 5, -5, 0])
    if k % 512:
        return np.exp2(np.random.permutation(np.resize(levels, k // 32))).repeat(32)
    a = np.empty((k // 512, 16))
    for p in range(k // 512):
        a[p, :8] = np.random.permutation(np.resize(levels, 8))
        for g in range(8):
            far = levels[np.abs(levels - a[p, g]) >= 10]
            a[p, g + 8] = far[np.random.randint(len(far))]
    return np.exp2(a.ravel()).repeat(32)


def f64(x):
    return np.asarray(x).astype(np.float64)


def striped(idx):
    return np.tile(idx.reshape(-1, 16).T, (8, 1)).astype(np.uint16)


def unstriped(offs):
    return offs[:16].T.reshape(-1).astype(np.int64)


E2M1 = np.array([0.0, 0.5, 1.0, 1.5, 2.0, 3.0, 4.0, 6.0, -0.0, -0.5, -1.0, -1.5, -2.0, -3.0, -4.0, -6.0])


def pack_weight(w, fmt):
    k, n = w.shape
    w = f64(np.asarray(w, np.float32).astype(ml_dtypes.bfloat16)).reshape(k // 32, 32, n)
    amax = np.abs(w).max(1)
    if fmt == "e4m3":
        byte = np.frexp(amax)[1] - 1 + 127 - 7
    else:
        mant, ex = np.frexp(amax / 6.0)
        byte = np.where(mant > 0.5, ex, ex - 1) + 127
    byte = np.clip(np.where(amax > 0, byte, 1), 1, 254)
    scaled = (w * np.exp2(127.0 - byte)[:, None, :]).reshape(k, n).astype(np.float32)
    by_word = np.ascontiguousarray(scaled.reshape(k // 512, 128, 4, n).transpose(0, 1, 3, 2))
    if fmt == "e4m3":
        words = by_word.astype(ml_dtypes.float8_e4m3fn).view(np.uint8)
    else:
        c = by_word.astype(ml_dtypes.float4_e2m1fn).view(np.uint8) & 0xF
        words = (c[..., 0::2] | (c[..., 1::2] << 4)).reshape(k // 512, 128, 2 * n)
    return np.ascontiguousarray(words), np.ascontiguousarray(byte.astype(np.uint8).reshape(k // 512, 16, n))


def unpack_weight(words, scales, fmt):
    g, _, n = scales.shape
    words = np.ascontiguousarray(words).reshape(g, 128, n, -1)
    if fmt == "e4m3":
        vals = words.view(ml_dtypes.float8_e4m3fn).astype(np.float64)
    else:
        nib = np.empty((g, 128, n, 4), np.uint8)
        nib[..., 0::2] = words & 0xF
        nib[..., 1::2] = words >> 4
        vals = E2M1[nib]
    vals = vals * np.repeat(np.exp2(scales.astype(np.float64) - 127.0), 8, axis=1)[..., None]
    return vals.transpose(0, 1, 3, 2).reshape(g * 512, n)


def gelu(v):
    return 0.5 * v * (1.0 + np.tanh(np.sqrt(2.0 / np.pi) * (v + 0.044715 * v**3)))


K, K2, H, N, T, T2, S, P = 1024, 512, 1024, 384, 2048, 2048, 1024, 1024

def setup_inputs():
    n = np.random.standard_normal
    s = mx_kscale(K)[:, None]
    s2 = mx_kscale(K2)[:, None]
    u = mx_kscale(H)[:, None]
    tab_words, tab_scales = pack_weight(n((K, T)) * s, "e4m3")
    wrx_words, wrx_scales = pack_weight(n((K, H)) / np.sqrt(K) / s * u.T, "e2m1")
    wdem_words, wdem_scales = pack_weight(n((H, N)) / np.sqrt(H) / u, "e4m3")
    return {
        "tab_words": tab_words, "tab_scales": tab_scales,
        "offs": striped(np.random.permutation(T)[:P]),
        "offs2": striped(np.random.permutation(T2)[:S]),
        "offs3": striped(np.random.permutation(T2)[:P]),
        "xs": (np.round(16 * n((K2, S))) / 16 * s2).astype(np.float32),
        "base": (np.round(16 * n((K2, T2))) / 16 * s2).astype(np.float32),
        "wtx": (0.9 * n((K2, H)) / np.sqrt(K2) / s2 * u.T).astype(np.float32),
        "cub": (0.1 * np.exp(0.3 * n(H)) / u[:, 0] ** 2).astype(np.float32),
        "wrx_words": wrx_words, "wrx_scales": wrx_scales,
        "wdem_words": wdem_words, "wdem_scales": wdem_scales,
        "bdem": (0.3 * n(N)).astype(np.float32),
    }

def reference(tab_words, tab_scales, offs, offs2, offs3, xs, base, wtx, cub,
              wrx_words, wrx_scales, wdem_words, wdem_scales, bdem):
    v = unpack_weight(tab_words, tab_scales, "e4m3")[:, unstriped(offs)]
    wrx = unpack_weight(wrx_words, wrx_scales, "e2m1")
    wdem = unpack_weight(wdem_words, wdem_scales, "e4m3")
    page = f64(base).copy()
    page[:, unstriped(offs2)] = f64(xs)
    a = mxq(f64(wtx), 0, "e4m3").T @ mxq(page, 0, "e4m3")
    x = a[:, unstriped(offs3)]
    b = wrx.T @ v
    leak = x + f64(cub)[:, None] * (x * x * x)
    resid = b - leak
    y = wdem.T @ mxq(resid, 0, "e4m3")
    return y + f64(bdem)[:, None]

@@ -1,0 +1,264 @@
+from contextlib import ExitStack
+
+import concourse.mybir as mybir
+
+K, K2, H, N, T, T2, S, J = 1024, 512, 1024, 384, 2048, 2048, 1024, 1024
+FLOPS = 2 * (K2 * H * T2 + K * H * J + H * N * J)
+
+F32 = mybir.dt.float32
+BF16 = mybir.dt.bfloat16
+I32 = mybir.dt.int32
+U32 = mybir.dt.uint32
+U16 = mybir.dt.uint16
+U8 = mybir.dt.uint8
+FP8X4 = mybir.dt.float8_e4m3fn_x4
+FP4X4 = mybir.dt.float4_e2m1fn_x4
+ACT = mybir.ActivationFunctionType
+ALU = mybir.AluOpType
+
+P = 128
+PACK = 4
+BANK = 512
+QUADS = 4
+ALIGN = 64
+B_COLS = 128
+Y_COLS = 256
+
+
+def tile_list_duplex_cancel_filter_kernel(
+    tc, tab_words, tab_scales, offs, offs2, offs3, xs, base, wtx, cub,
+    wrx_words, wrx_scales, wdem_words, wdem_scales, bdem, out,
+):
+    nc = tc.nc
+    with ExitStack() as ctx:
+        lists = ctx.enter_context(tc.tile_pool(name="lists", bufs=1))
+        sb = ctx.enter_context(tc.tile_pool(name="sb", bufs=1))
+        psum = ctx.enter_context(tc.psum_pool(name="psum", bufs=4))
+
+        def tile(shape, dtype, name, tag=None, bufs=1):
+            return sb.tile(shape, dtype, name=name, tag=tag or name, bufs=bufs, align_bytes=ALIGN)
+
+        def zeroed_plane(width, name):
+            plane = tile([P, width], U8, name)
+            nc.vector.memset(plane[:].bitcast(I32), 0)
+            return plane
+
+        def load_packed_planes(plane, scales):
+            for q in range(QUADS):
+                nc.sync.dma_start(
+                    out=plane[32 * q : 32 * q + 8, :].bitcast(I32),
+                    in_=scales[:, 4 * q : 4 * q + 4, :].bitcast(I32),
+                )
+
+        def move_second_plane(dst, packed):
+            for q in range(QUADS):
+                nc.sync.dma_start(
+                    out=dst[32 * q : 32 * q + 4, :].bitcast(I32),
+                    in_=packed[32 * q + 4 : 32 * q + 8, :].bitcast(I32),
+                )
+
+        idx = lists.tile([P, J // 16], U16, name="idx")
+        idx2 = lists.tile([P, S // 16], U16, name="idx2")
+        idx3 = lists.tile([P, J // 16], U16, name="idx3")
+
+        tab_planes = zeroed_plane(T, "tab_planes")
+        wrx_planes_raw = zeroed_plane(H, "wrx_planes_raw")
+        wdem_planes = zeroed_plane(N, "wdem_planes")
+        v_plane1 = zeroed_plane(J, "v_plane1")
+        wrx_plane1 = zeroed_plane(H, "wrx_plane1")
+
+        base_rows = base.rearrange("(p t) c -> p t c", t=PACK)
+        xs_rows = xs.rearrange("(p t) c -> p t c", t=PACK)
+        page = [tile([P, T2], F32, f"page{t}", tag="row", bufs=6) for t in range(PACK)]
+        xs_pieces = [(0, 0, S // 2), (0, S // 2, S)] + [(t, 0, S) for t in range(1, PACK)]
+        xs_tiles = [tile([P, hi - lo], F32, f"xs{t}_{lo}") for t, lo, hi in xs_pieces]
+        wtx_raw = tile([P, 2, PACK, BANK], F32, "wtx_raw", tag="wide")
+
+        nc.sync.dma_start(idx2[:], offs2)
+        for (t, lo, hi), xs_tile in zip(xs_pieces, xs_tiles):
+            if lo == 0:
+                nc.sync.dma_start(out=page[t][:], in_=base_rows[:, t, :])
+            nc.sync.dma_start(out=xs_tile[:], in_=xs_rows[:, t, lo:hi])
+            if t == 0 and hi == S:
+                for g in range(2):
+                    nc.sync.dma_start(
+                        out=wtx_raw[:, g, :, :],
+                        in_=wtx[:, BANK * g : BANK * (g + 1)].rearrange("(p j) c -> p j c", j=PACK),
+                    )
+
+        wrx_raw = tile([P, 2, 2 * H], U8, "wrx_raw")
+        nc.sync.dma_start(
+            out=wrx_raw[:].bitcast(I32), in_=wrx_words.rearrange("a p c -> p a c").bitcast(I32)
+        )
+        load_packed_planes(wrx_planes_raw, wrx_scales)
+        nc.sync.dma_start(idx[:], offs)
+        load_packed_planes(tab_planes, tab_scales)
+        tab = [tile([P, T], U32, f"tab{a}") for a in range(2)]
+        for a in range(2):
+            nc.sync.dma_start(
+                out=tab[a][:].bitcast(I32),
+                in_=tab_words[a].rearrange("p n i -> p (n i)").bitcast(I32),
+            )
+        nc.sync.dma_start(idx3[:], offs3)
+        cub_cols = tile([P, 2, PACK], F32, "cub_cols")
+        nc.sync.dma_start(out=cub_cols[:], in_=cub.rearrange("(g p t) -> p g t", g=2, t=PACK))
+        wdem = tile([P, 2, N], U32, "wdem")
+        nc.sync.dma_start(
+            out=wdem[:].bitcast(I32), in_=wdem_words.rearrange("a p c i -> p a (c i)").bitcast(I32)
+        )
+        load_packed_planes(wdem_planes, wdem_scales)
+        bias_cols = tile([P, N // P], F32, "bias_cols")
+        with nc.allow_non_contiguous_dma(reason="one bias value to a partition"):
+            nc.sync.dma_start(out=bias_cols[:], in_=bdem.rearrange("(n p) -> p n", p=P))
+
+        wtx_bf = tile([P, 2, PACK * BANK], BF16, "wtx_bf")
+        wtx_codes = tile([P, H], U32, "wtx_codes")
+        wtx_plane = tile([P, H], U8, "wtx_plane")
+        for g in range(2):
+            nc.scalar.activation(
+                out=wtx_bf[:, g, :].rearrange("p (t m j) -> p m j t", t=PACK, j=PACK),
+                in_=wtx_raw[:, g, :, :].rearrange("p j (m t) -> p m j t", t=PACK),
+                func=ACT.Identity,
+            )
+            cols = slice(BANK * g, BANK * (g + 1))
+            nc.vector.quantize_mx(
+                out=wtx_codes[:, cols].bitcast(FP8X4), scales=wtx_plane[:, cols], in_=wtx_bf[:, g, :]
+            )
+
+        page_bf = tile([P, T2, PACK], BF16, "page_bf", tag="wide")
+        for (t, lo, hi), xs_tile in zip(xs_pieces, xs_tiles):
+            nc.vector.tensor_copy(page[t][:].indirect(idx2[:, lo // 16 : hi // 16]), xs_tile[:])
+            if hi == S:
+                step = BANK if t == PACK - 1 else T2
+                for c0 in range(0, T2, step):
+                    nc.scalar.copy(out=page_bf[:, c0 : c0 + step, t], in_=page[t][:, c0 : c0 + step])
+
+        v = [tile([P, J], U32, f"v{a}") for a in range(2)]
+        page_plane = tile([P, T2], U8, "page_plane")
+        page_codes = []
+        for a, chunks in enumerate(((0,), (1, 2, 3))):
+            nc.vector.tensor_copy(v[a][:], tab[a][:].indirect(idx[:]))
+            codes = tile([P, len(chunks) * BANK], U32, f"page_codes{a}", tag=f"tab{a}")
+            for n, c in enumerate(chunks):
+                part = codes[:, n * BANK : (n + 1) * BANK]
+                nc.vector.quantize_mx(
+                    out=part.bitcast(FP8X4),
+                    scales=page_plane[:, c * BANK : (c + 1) * BANK],
+                    in_=page_bf[:, c * BANK : (c + 1) * BANK, :].rearrange("p c t -> p (c t)"),
+                )
+                page_codes.append(part)
+
+        wrx = tile([P, 2, 2 * H], U8, "wrx", tag="wide")
+        nc.vector.tensor_copy(
+            out=wrx[:].rearrange("p a c -> p (a c)").bitcast(U16).rearrange("p (h t m) -> p h t m", t=PACK, m=P),
+            in_=wrx_raw[:].rearrange("p a c -> p (a c)").bitcast(U16).rearrange("p (h m t) -> p h t m", t=PACK, m=P),
+        )
+        v_planes = tile([P, J], U8, "v_planes", tag="wrx_raw")
+        nc.vector.tensor_copy(v_planes[:], tab_planes[:].indirect(idx[:]))
+        move_second_plane(v_plane1, v_planes)
+        wrx_planes = tile([P, H], U8, "wrx_planes", tag="tab_planes")
+        nc.vector.tensor_copy(
+            out=wrx_planes[:].rearrange("p (g t m) -> p g t m", t=PACK, m=P),
+            in_=wrx_planes_raw[:].rearrange("p (g m t) -> p g t m", t=PACK, m=P),
+        )
+        move_second_plane(wrx_plane1, wrx_planes)
+        v_plane = (v_planes, v_plane1)
+        wrx_plane = (wrx_planes, wrx_plane1)
+
+        tiles = 2 * PACK
+        resid_codes = [tile([P, J], U32, f"resid_codes{g}") for g in range(2)]
+        resid_plane = [tile([P, J], U8, f"resid_plane{g}") for g in range(2)]
+        leak = [tile([P, PACK, J], F32, f"leak{g}") for g in range(2)]
+        out_rows = out.rearrange("(n p) j -> p n j", p=P)
+
+        def project(i):
+            a_rows = tile([P, T2], F32, f"a{i}", tag="row", bufs=6)
+            rows = slice(P * i, P * (i + 1))
+            for c in range(T2 // BANK):
+                cols = slice(BANK * c, BANK * (c + 1))
+                acc = psum.tile([P, BANK], F32, name="acc", tag="acc")
+                nc.tensor.matmul_mx(
+                    out=acc[:],
+                    lhsT=wtx_codes[:, rows].bitcast(FP8X4), lhsT_scale=wtx_plane[:, rows],
+                    rhs=page_codes[c].bitcast(FP8X4), rhs_scale=page_plane[:, cols],
+                    start=True, stop=True,
+                )
+                nc.scalar.copy(out=a_rows[:, cols], in_=acc[:])
+            return a_rows
+
+        def make_leak(i, a_rows, lo, hi):
+            g, t = divmod(i, PACK)
+            x = tile([P, hi - lo], F32, "x", bufs=3)
+            gain = tile([P, hi - lo], F32, "gain", bufs=3)
+            nc.vector.tensor_copy(x[:], a_rows[:].indirect(idx3[:, lo // 16 : hi // 16]))
+            nc.scalar.activation(out=gain[:], in_=x[:], func=ACT.Square)
+            nc.scalar.activation(
+                out=gain[:], in_=gain[:], func=ACT.Identity, scale=cub_cols[:, g, t : t + 1], bias=1.0
+            )
+            nc.vector.tensor_tensor(leak[g][:, t, lo:hi], gain[:], x[:], ALU.mult)
+
+        def make_resid(g, j0):
+            resid = tile([P, Y_COLS, PACK], BF16, "resid", bufs=3)
+            for lo in range(0, Y_COLS, B_COLS):
+                cols = slice(j0 + lo, j0 + lo + B_COLS)
+                b = psum.tile([P, PACK, B_COLS], F32, name="b", tag="b")
+                for t in range(PACK):
+                    r0 = P * (PACK * g + t)
+                    for a in range(2):
+                        nc.tensor.matmul_mx(
+                            out=b[:, t, :],
+                            lhsT=wrx[:, a, 2 * r0 : 2 * (r0 + P)].bitcast(FP4X4),
+                            lhsT_scale=wrx_plane[a][:, r0 : r0 + P],
+                            rhs=v[a][:, cols].bitcast(FP8X4), rhs_scale=v_plane[a][:, cols],
+                            start=(a == 0), stop=(a == 1),
+                        )
+                nc.vector.tensor_tensor(
+                    resid[:, lo : lo + B_COLS, :].rearrange("p (c i) t -> p c t i", i=4),
+                    b[:].rearrange("p t (c i) -> p c t i", i=4),
+                    leak[g][:, :, cols].rearrange("p t (c i) -> p c t i", i=4),
+                    ALU.subtract,
+                )
+            cols = slice(j0, j0 + Y_COLS)
+            nc.vector.quantize_mx(
+                out=resid_codes[g][:, cols].bitcast(FP8X4),
+                scales=resid_plane[g][:, cols],
+                in_=resid[:].rearrange("p c t -> p (c t)"),
+            )
+
+        def filter_out(j0):
+            cols = slice(j0, j0 + Y_COLS)
+            last = j0 + Y_COLS == J
+            staged = tile([P, N // P, Y_COLS], F32, "staged", bufs=4)
+            for n in range(N // P):
+                rows = slice(P * n, P * (n + 1))
+                y = psum.tile([P, Y_COLS], F32, name="y", tag="acc")
+                for g in range(2):
+                    nc.tensor.matmul_mx(
+                        out=y[:],
+                        lhsT=wdem[:, g, rows].bitcast(FP8X4), lhsT_scale=wdem_planes[4 * g : P, rows],
+                        rhs=resid_codes[g][:, cols].bitcast(FP8X4), rhs_scale=resid_plane[g][:, cols],
+                        start=(g == 0), stop=(g == 1),
+                    )
+                if last and n == 1:
+                    nc.vector.tensor_scalar(
+                        staged[:, n, :], y[:], bias_cols[:, n : n + 1], None, ALU.add
+                    )
+                else:
+                    nc.scalar.activation(
+                        out=staged[:, n, :], in_=y[:], func=ACT.Identity, bias=bias_cols[:, n : n + 1]
+                    )
+            nc.sync.dma_start(out=out_rows[:, :, cols], in_=staged[:])
+
+        ahead = 2
+        a_tiles = [project(i) for i in range(ahead)]
+        for i in range(tiles):
+            if i + ahead < tiles:
+                a_tiles.append(project(i + ahead))
+            pieces = ((0, J // 2), (J // 2, J)) if i == tiles - 1 else ((0, J),)
+            for lo, hi in pieces:
+                make_leak(i, a_tiles[i], lo, hi)
+            if i % PACK == PACK - 1:
+                for j0 in range(0, J, Y_COLS):
+                    make_resid(i // PACK, j0)
+                    if i == tiles - 1:
+                        filter_out(j0)

@@ -40,7 +40,7 @@ def tile_list_duplex_cancel_filter_kernel(
 
         def zeroed_plane(width, name):
             plane = tile([P, width], U8, name)
-            nc.vector.memset(plane[:].bitcast(I32), 0)
+            nc.gpsimd.memset(plane[:].bitcast(I32), 0)
             return plane
 
         def load_packed_planes(plane, scales):
@@ -50,22 +50,40 @@ def tile_list_duplex_cancel_filter_kernel(
                     in_=scales[:, 4 * q : 4 * q + 4, :].bitcast(I32),
                 )
 
-        def move_second_plane(dst, packed):
-            for q in range(QUADS):
-                nc.sync.dma_start(
-                    out=dst[32 * q : 32 * q + 4, :].bitcast(I32),
-                    in_=packed[32 * q + 4 : 32 * q + 8, :].bitcast(I32),
-                )
+        def load_scale_rows(scales, name):
+            rows = tile([P, scales.shape[2]], U8, name)
+            nc.sync.dma_start(
+                out=rows[0:32, :].bitcast(I32), in_=scales.rearrange("a q c -> (a q) c").bitcast(I32)
+            )
+            nc.vector.memset(rows[32:64, :].bitcast(I32), 0)
+            nc.vector.memset(rows[64:128, :].bitcast(I32), 0)
+            return rows
+
+        def spread_scale_rows(planes, rows):
+            for a in range(2):
+                for q in range(QUADS):
+                    nc.sync.dma_start(
+                        out=planes[a][32 * q : 32 * q + 4, :].bitcast(I32),
+                        in_=rows[16 * a + 4 * q : 16 * a + 4 * q + 4, :].bitcast(I32),
+                    )
 
         idx = lists.tile([P, J // 16], U16, name="idx")
         idx2 = lists.tile([P, S // 16], U16, name="idx2")
         idx3 = lists.tile([P, J // 16], U16, name="idx3")
 
-        tab_planes = zeroed_plane(T, "tab_planes")
-        wrx_planes_raw = zeroed_plane(H, "wrx_planes_raw")
+        nc.sync.dma_start(idx[:], offs)
+        tab_rows = load_scale_rows(tab_scales, "tab_rows")
+        wrx_rows_raw = load_scale_rows(wrx_scales, "wrx_rows_raw")
         wdem_planes = zeroed_plane(N, "wdem_planes")
-        v_plane1 = zeroed_plane(J, "v_plane1")
-        wrx_plane1 = zeroed_plane(H, "wrx_plane1")
+        v_plane = [zeroed_plane(J, f"v_plane{a}") for a in range(2)]
+        wrx_plane = [zeroed_plane(H, f"wrx_plane{a}") for a in range(2)]
+        v_rows = tile([P, J], U8, "v_rows")
+        nc.vector.tensor_copy(v_rows[:], tab_rows[:].indirect(idx[:]))
+        wrx_rows = tile([P, H], U8, "wrx_rows")
+        nc.vector.tensor_copy(
+            out=wrx_rows[:].rearrange("p (g t m) -> p g t m", t=PACK, m=P),
+            in_=wrx_rows_raw[:].rearrange("p (g m t) -> p g t m", t=PACK, m=P),
+        )
 
         base_rows = base.rearrange("(p t) c -> p t c", t=PACK)
         xs_rows = xs.rearrange("(p t) c -> p t c", t=PACK)
@@ -90,11 +108,8 @@ def tile_list_duplex_cancel_filter_kernel(
         nc.sync.dma_start(
             out=wrx_raw[:].bitcast(I32), in_=wrx_words.rearrange("a p c -> p a c").bitcast(I32)
         )
-        load_packed_planes(wrx_planes_raw, wrx_scales)
-        nc.sync.dma_start(idx[:], offs)
-        load_packed_planes(tab_planes, tab_scales)
         tab = [tile([P, T], U32, f"tab{a}") for a in range(2)]
-        for a in range(2):
+        for a in (1, 0):
             nc.sync.dma_start(
                 out=tab[a][:].bitcast(I32),
                 in_=tab_words[a].rearrange("p n i -> p (n i)").bitcast(I32),
@@ -110,6 +125,8 @@ def tile_list_duplex_cancel_filter_kernel(
         bias_cols = tile([P, N // P], F32, "bias_cols")
         with nc.allow_non_contiguous_dma(reason="one bias value to a partition"):
             nc.sync.dma_start(out=bias_cols[:], in_=bdem.rearrange("(n p) -> p n", p=P))
+        spread_scale_rows(v_plane, v_rows)
+        spread_scale_rows(wrx_plane, wrx_rows)
 
         wtx_bf = tile([P, 2, PACK * BANK], BF16, "wtx_bf")
         wtx_codes = tile([P, H], U32, "wtx_codes")
@@ -128,137 +145,177 @@ def tile_list_duplex_cancel_filter_kernel(
         page_bf = tile([P, T2, PACK], BF16, "page_bf", tag="wide")
         for (t, lo, hi), xs_tile in zip(xs_pieces, xs_tiles):
             nc.vector.tensor_copy(page[t][:].indirect(idx2[:, lo // 16 : hi // 16]), xs_tile[:])
-            if hi == S:
-                step = BANK if t == PACK - 1 else T2
-                for c0 in range(0, T2, step):
+            if hi == S and t < 2:
+                nc.scalar.copy(out=page_bf[:, :, t], in_=page[t][:])
+            elif hi == S:
+                split = T2 - BANK
+                step = BANK if t == PACK - 1 else split
+                for c0 in range(0, split, step):
                     nc.scalar.copy(out=page_bf[:, c0 : c0 + step, t], in_=page[t][:, c0 : c0 + step])
-
-        v = [tile([P, J], U32, f"v{a}") for a in range(2)]
-        page_plane = tile([P, T2], U8, "page_plane")
-        page_codes = []
-        for a, chunks in enumerate(((0,), (1, 2, 3))):
-            nc.vector.tensor_copy(v[a][:], tab[a][:].indirect(idx[:]))
-            codes = tile([P, len(chunks) * BANK], U32, f"page_codes{a}", tag=f"tab{a}")
-            for n, c in enumerate(chunks):
-                part = codes[:, n * BANK : (n + 1) * BANK]
-                nc.vector.quantize_mx(
-                    out=part.bitcast(FP8X4),
-                    scales=page_plane[:, c * BANK : (c + 1) * BANK],
-                    in_=page_bf[:, c * BANK : (c + 1) * BANK, :].rearrange("p c t -> p (c t)"),
+                nc.gpsimd.tensor_scalar(
+                    page_bf[:, split:, t], page[t][:, split:], 1.0, 0.0, ALU.mult, ALU.add
                 )
-                page_codes.append(part)
+
+        half = J // 2
+        v1_first = tile([P, half], U32, "v1_first")
+        nc.vector.tensor_copy(v1_first[:], tab[1][:].indirect(idx[:, : half // 16]))
+        v0 = tile([P, J], U32, "v0")
+        nc.vector.tensor_copy(v0[:], tab[0][:].indirect(idx[:]))
+        page_plane = tile([P, T2], U8, "page_plane")
+        page_codes = tile([P, T2], U32, "page_codes", tag="tab0")
+        chunk_order = (0, 3, 1, 2)
+        for c in chunk_order:
+            cols = slice(c * BANK, (c + 1) * BANK)
+            nc.vector.quantize_mx(
+                out=page_codes[:, cols].bitcast(FP8X4),
+                scales=page_plane[:, cols],
+                in_=page_bf[:, cols, :].rearrange("p c t -> p (c t)"),
+            )
+        v1 = [v1_first]
 
         wrx = tile([P, 2, 2 * H], U8, "wrx", tag="wide")
         nc.vector.tensor_copy(
             out=wrx[:].rearrange("p a c -> p (a c)").bitcast(U16).rearrange("p (h t m) -> p h t m", t=PACK, m=P),
             in_=wrx_raw[:].rearrange("p a c -> p (a c)").bitcast(U16).rearrange("p (h m t) -> p h t m", t=PACK, m=P),
         )
-        v_planes = tile([P, J], U8, "v_planes", tag="wrx_raw")
-        nc.vector.tensor_copy(v_planes[:], tab_planes[:].indirect(idx[:]))
-        move_second_plane(v_plane1, v_planes)
-        wrx_planes = tile([P, H], U8, "wrx_planes", tag="tab_planes")
-        nc.vector.tensor_copy(
-            out=wrx_planes[:].rearrange("p (g t m) -> p g t m", t=PACK, m=P),
-            in_=wrx_planes_raw[:].rearrange("p (g m t) -> p g t m", t=PACK, m=P),
-        )
-        move_second_plane(wrx_plane1, wrx_planes)
-        v_plane = (v_planes, v_plane1)
-        wrx_plane = (wrx_planes, wrx_plane1)
 
         tiles = 2 * PACK
-        resid_codes = [tile([P, J], U32, f"resid_codes{g}") for g in range(2)]
         resid_plane = [tile([P, J], U8, f"resid_plane{g}") for g in range(2)]
         leak = [tile([P, PACK, J], F32, f"leak{g}") for g in range(2)]
         out_rows = out.rearrange("(n p) j -> p n j", p=P)
 
         def project(i):
-            a_rows = tile([P, T2], F32, f"a{i}", tag="row", bufs=6)
+            if i == 1:
+                a_rows = tile([P, T2], F32, f"a{i}", tag="wtx_bf")
+            else:
+                a_rows = tile([P, T2], F32, f"a{i}", tag="row", bufs=6)
             rows = slice(P * i, P * (i + 1))
-            for c in range(T2 // BANK):
+            for c in chunk_order:
                 cols = slice(BANK * c, BANK * (c + 1))
                 acc = psum.tile([P, BANK], F32, name="acc", tag="acc")
                 nc.tensor.matmul_mx(
                     out=acc[:],
                     lhsT=wtx_codes[:, rows].bitcast(FP8X4), lhsT_scale=wtx_plane[:, rows],
-                    rhs=page_codes[c].bitcast(FP8X4), rhs_scale=page_plane[:, cols],
+                    rhs=page_codes[:, cols].bitcast(FP8X4), rhs_scale=page_plane[:, cols],
                     start=True, stop=True,
                 )
-                nc.scalar.copy(out=a_rows[:, cols], in_=acc[:])
+                if i in () and c == chunk_order[-1]:
+                    nc.vector.tensor_copy(out=a_rows[:, cols], in_=acc[:])
+                else:
+                    nc.scalar.copy(out=a_rows[:, cols], in_=acc[:])
             return a_rows
 
         def make_leak(i, a_rows, lo, hi):
             g, t = divmod(i, PACK)
             x = tile([P, hi - lo], F32, "x", bufs=3)
-            gain = tile([P, hi - lo], F32, "gain", bufs=3)
+            if i == tiles - 2:
+                gain = tile([P, hi - lo], F32, "last_pool_gain")
+            else:
+                gain = tile([P, hi - lo], F32, "gain", bufs=3)
             nc.vector.tensor_copy(x[:], a_rows[:].indirect(idx3[:, lo // 16 : hi // 16]))
             nc.scalar.activation(out=gain[:], in_=x[:], func=ACT.Square)
-            nc.scalar.activation(
-                out=gain[:], in_=gain[:], func=ACT.Identity, scale=cub_cols[:, g, t : t + 1], bias=1.0
-            )
-            nc.vector.tensor_tensor(leak[g][:, t, lo:hi], gain[:], x[:], ALU.mult)
-
-        def make_resid(g, j0):
-            resid = tile([P, Y_COLS, PACK], BF16, "resid", bufs=3)
-            for lo in range(0, Y_COLS, B_COLS):
-                cols = slice(j0 + lo, j0 + lo + B_COLS)
-                b = psum.tile([P, PACK, B_COLS], F32, name="b", tag="b")
-                for t in range(PACK):
-                    r0 = P * (PACK * g + t)
-                    for a in range(2):
-                        nc.tensor.matmul_mx(
-                            out=b[:, t, :],
-                            lhsT=wrx[:, a, 2 * r0 : 2 * (r0 + P)].bitcast(FP4X4),
-                            lhsT_scale=wrx_plane[a][:, r0 : r0 + P],
-                            rhs=v[a][:, cols].bitcast(FP8X4), rhs_scale=v_plane[a][:, cols],
-                            start=(a == 0), stop=(a == 1),
-                        )
-                nc.vector.tensor_tensor(
-                    resid[:, lo : lo + B_COLS, :].rearrange("p (c i) t -> p c t i", i=4),
-                    b[:].rearrange("p t (c i) -> p c t i", i=4),
-                    leak[g][:, :, cols].rearrange("p t (c i) -> p c t i", i=4),
-                    ALU.subtract,
+            if i in (7,):
+                nc.scalar.activation(
+                    out=gain[:], in_=gain[:], func=ACT.Identity, scale=cub_cols[:, g, t : t + 1], bias=1.0
                 )
-            cols = slice(j0, j0 + Y_COLS)
+            else:
+                nc.gpsimd.tensor_scalar(
+                    gain[:], gain[:], cub_cols[:, g, t : t + 1], 1.0, ALU.mult, ALU.add
+                )
+            if i in (0, 1, 6, 7):
+                nc.vector.tensor_tensor(leak[g][:, t, lo:hi], gain[:], x[:], ALU.mult)
+            else:
+                nc.gpsimd.tensor_tensor(leak[g][:, t, lo:hi], gain[:], x[:], ALU.mult)
+
+        def project_received(g, j0, tag):
+            cols = slice(j0, j0 + B_COLS)
+            b = psum.tile([P, PACK, B_COLS], F32, name="b", tag=tag)
+            words = (v0[:, cols], v1[j0 // half][:, j0 % half : j0 % half + B_COLS])
+            for t in range(PACK):
+                r0 = P * (PACK * g + t)
+                for a in range(2):
+                    nc.tensor.matmul_mx(
+                        out=b[:, t, :],
+                        lhsT=wrx[:, a, 2 * r0 : 2 * (r0 + P)].bitcast(FP4X4),
+                        lhsT_scale=wrx_plane[a][:, r0 : r0 + P],
+                        rhs=words[a].bitcast(FP8X4), rhs_scale=v_plane[a][:, cols],
+                        start=(a == 0), stop=(a == 1),
+                    )
+            return b
+
+        def subtract(g, j0, resid, b):
+            cols = slice(j0, j0 + B_COLS)
+            nc.vector.tensor_tensor(
+                resid.rearrange("p (c i) t -> p c t i", i=4),
+                b[:].rearrange("p t (c i) -> p c t i", i=4),
+                leak[g][:, :, cols].rearrange("p t (c i) -> p c t i", i=4),
+                ALU.subtract,
+            )
+
+        def quantise_resid(g, resid, codes, cols):
             nc.vector.quantize_mx(
-                out=resid_codes[g][:, cols].bitcast(FP8X4),
+                out=codes[:, cols].bitcast(FP8X4),
                 scales=resid_plane[g][:, cols],
                 in_=resid[:].rearrange("p c t -> p (c t)"),
             )
 
-        def filter_out(j0):
-            cols = slice(j0, j0 + Y_COLS)
-            last = j0 + Y_COLS == J
-            staged = tile([P, N // P, Y_COLS], F32, "staged", bufs=4)
-            for n in range(N // P):
-                rows = slice(P * n, P * (n + 1))
-                y = psum.tile([P, Y_COLS], F32, name="y", tag="acc")
-                for g in range(2):
-                    nc.tensor.matmul_mx(
-                        out=y[:],
-                        lhsT=wdem[:, g, rows].bitcast(FP8X4), lhsT_scale=wdem_planes[4 * g : P, rows],
-                        rhs=resid_codes[g][:, cols].bitcast(FP8X4), rhs_scale=resid_plane[g][:, cols],
-                        start=(g == 0), stop=(g == 1),
-                    )
-                if last and n == 1:
-                    nc.vector.tensor_scalar(
-                        staged[:, n, :], y[:], bias_cols[:, n : n + 1], None, ALU.add
-                    )
-                else:
-                    nc.scalar.activation(
-                        out=staged[:, n, :], in_=y[:], func=ACT.Identity, bias=bias_cols[:, n : n + 1]
-                    )
-            nc.sync.dma_start(out=out_rows[:, :, cols], in_=staged[:])
+        def filter_out(cols, tag, last):
+            width = cols.stop - cols.start
+            staged = tile([P, N // P, width], F32, "staged", bufs=4)
+            for group in ((0,), (1,), (2,)) if last else ((0, 1), (2,)):
+                y = psum.tile([P, len(group), width], F32, name="y", tag=tag)
+                for s, n in enumerate(group):
+                    rows = slice(P * n, P * (n + 1))
+                    for g in range(2):
+                        nc.tensor.matmul_mx(
+                            out=y[:, s, :],
+                            lhsT=wdem[:, g, rows].bitcast(FP8X4), lhsT_scale=wdem_planes[4 * g : P, rows],
+                            rhs=resid_codes[g][:, cols].bitcast(FP8X4), rhs_scale=resid_plane[g][:, cols],
+                            start=(g == 0), stop=(g == 1),
+                        )
+                for s, n in enumerate(group):
+                    if last and n == 1:
+                        nc.vector.tensor_scalar(
+                            staged[:, n, :], y[:, s, :], bias_cols[:, n : n + 1], None, ALU.add
+                        )
+                    else:
+                        nc.scalar.activation(
+                            out=staged[:, n, :], in_=y[:, s, :], func=ACT.Identity, bias=bias_cols[:, n : n + 1]
+                        )
+                    if last:
+                        queue = nc.scalar if n == 2 else nc.sync
+                        queue.dma_start(out=out_rows[:, n, cols], in_=staged[:, n, :])
+            if not last:
+                nc.sync.dma_start(out=out_rows[:, :, cols], in_=staged[:])
 
-        ahead = 2
-        a_tiles = [project(i) for i in range(ahead)]
+        a_tiles = [project(i) for i in range(1)]
         for i in range(tiles):
-            if i + ahead < tiles:
-                a_tiles.append(project(i + ahead))
+            if len(a_tiles) < tiles:
+                a_tiles.append(project(len(a_tiles)))
+            if i == -1 and len(a_tiles) < tiles:
+                a_tiles.append(project(len(a_tiles)))
             pieces = ((0, J // 2), (J // 2, J)) if i == tiles - 1 else ((0, J),)
             for lo, hi in pieces:
                 make_leak(i, a_tiles[i], lo, hi)
-            if i % PACK == PACK - 1:
-                for j0 in range(0, J, Y_COLS):
-                    make_resid(i // PACK, j0)
-                    if i == tiles - 1:
-                        filter_out(j0)
+            if i == 1:
+                v1_second = tile([P, half], U32, "v1_second", tag="wtx_bf")
+                nc.vector.tensor_copy(v1_second[:], tab[1][:].indirect(idx[:, half // 16 :]))
+                v1.append(v1_second)
+
+        resid0 = tile([P, J, PACK], BF16, "resid0")
+        for j0 in range(0, J, B_COLS):
+            subtract(0, j0, resid0[:, j0 : j0 + B_COLS, :], project_received(0, j0, "b"))
+        resid_codes = [
+            tile([P, J], U32, "resid_codes0", tag="last_pool_gain"),
+            tile([P, J], U32, "resid_codes1"),
+        ]
+        quantise_resid(0, resid0, resid_codes[0], slice(0, J))
+        widths = (256, 256, 256, 256)
+        starts = [sum(widths[:n]) for n in range(len(widths))]
+        b_banks = [project_received(1, j0, "b" if j0 < J // 2 else "acc") for j0 in range(0, J, B_COLS)]
+        for j0, width in zip(starts, widths):
+            resid = tile([P, width, PACK], BF16, "resid1", bufs=3)
+            for lo in range(0, width, B_COLS):
+                subtract(1, j0 + lo, resid[:, lo : lo + B_COLS, :], b_banks[(j0 + lo) // B_COLS])
+            quantise_resid(1, resid, resid_codes[1], slice(j0, j0 + width))
+            filter_out(slice(j0, j0 + width), "acc" if j0 == J // 2 else "b", j0 + width == J)

@@ -17,12 +17,21 @@ ACT = mybir.ActivationFunctionType
 ALU = mybir.AluOpType
 
 P = 128
-PACK = 4
+LANES = 4
+PASSES = 2
 BANK = 512
-QUADS = 4
+QUADRANT = 32
+BLOCKS = 16
 ALIGN = 64
-B_COLS = 128
+LINE = 4
+ROW_TILES = PASSES * LANES
+HALF = J // 2
+B_COLS = BANK // LANES
 Y_COLS = 256
+PSUM_RING = 4
+ROW_RING = 6
+LEAK_RING = 3
+VECTOR_FIRST = 3
 
 
 def tile_list_duplex_cancel_filter_kernel(
@@ -33,7 +42,7 @@ def tile_list_duplex_cancel_filter_kernel(
     with ExitStack() as ctx:
         lists = ctx.enter_context(tc.tile_pool(name="lists", bufs=1))
         sb = ctx.enter_context(tc.tile_pool(name="sb", bufs=1))
-        psum = ctx.enter_context(tc.psum_pool(name="psum", bufs=4))
+        psum = ctx.enter_context(tc.psum_pool(name="psum", bufs=PSUM_RING))
 
         def tile(shape, dtype, name, tag=None, bufs=1):
             return sb.tile(shape, dtype, name=name, tag=tag or name, bufs=bufs, align_bytes=ALIGN)
@@ -42,13 +51,6 @@ def tile_list_duplex_cancel_filter_kernel(
             plane = tile([P, width], U8, name)
             nc.gpsimd.memset(plane[:].bitcast(I32), 0)
             return plane
-
-        def load_packed_planes(plane, scales):
-            for q in range(QUADS):
-                nc.sync.dma_start(
-                    out=plane[32 * q : 32 * q + 8, :].bitcast(I32),
-                    in_=scales[:, 4 * q : 4 * q + 4, :].bitcast(I32),
-                )
 
         def load_scale_rows(scales, name):
             rows = tile([P, scales.shape[2]], U8, name)
@@ -60,11 +62,12 @@ def tile_list_duplex_cancel_filter_kernel(
             return rows
 
         def spread_scale_rows(planes, rows):
-            for a in range(2):
-                for q in range(QUADS):
+            for a in range(PASSES):
+                for quad in range(P // QUADRANT):
+                    first = BLOCKS * a + 4 * quad
                     nc.sync.dma_start(
-                        out=planes[a][32 * q : 32 * q + 4, :].bitcast(I32),
-                        in_=rows[16 * a + 4 * q : 16 * a + 4 * q + 4, :].bitcast(I32),
+                        out=planes[a][QUADRANT * quad : QUADRANT * quad + 4, :].bitcast(I32),
+                        in_=rows[first : first + 4, :].bitcast(I32),
                     )
 
         idx = lists.tile([P, J // 16], U16, name="idx")
@@ -75,66 +78,71 @@ def tile_list_duplex_cancel_filter_kernel(
         tab_rows = load_scale_rows(tab_scales, "tab_rows")
         wrx_rows_raw = load_scale_rows(wrx_scales, "wrx_rows_raw")
         wdem_planes = zeroed_plane(N, "wdem_planes")
-        v_plane = [zeroed_plane(J, f"v_plane{a}") for a in range(2)]
-        wrx_plane = [zeroed_plane(H, f"wrx_plane{a}") for a in range(2)]
+        v_plane = [zeroed_plane(J, f"v_plane{a}") for a in range(PASSES)]
+        wrx_plane = [zeroed_plane(H, f"wrx_plane{a}") for a in range(PASSES)]
         v_rows = tile([P, J], U8, "v_rows")
         nc.vector.tensor_copy(v_rows[:], tab_rows[:].indirect(idx[:]))
         wrx_rows = tile([P, H], U8, "wrx_rows")
         nc.vector.tensor_copy(
-            out=wrx_rows[:].rearrange("p (g t m) -> p g t m", t=PACK, m=P),
-            in_=wrx_rows_raw[:].rearrange("p (g m t) -> p g t m", t=PACK, m=P),
+            out=wrx_rows[:].rearrange("p (g t m) -> p g t m", t=LANES, m=P),
+            in_=wrx_rows_raw[:].rearrange("p (g m t) -> p g t m", t=LANES, m=P),
         )
 
-        base_rows = base.rearrange("(p t) c -> p t c", t=PACK)
-        xs_rows = xs.rearrange("(p t) c -> p t c", t=PACK)
-        page = [tile([P, T2], F32, f"page{t}", tag="row", bufs=6) for t in range(PACK)]
-        xs_pieces = [(0, 0, S // 2), (0, S // 2, S)] + [(t, 0, S) for t in range(1, PACK)]
+        base_lanes = base.rearrange("(p t) c -> p t c", t=LANES)
+        xs_lanes = xs.rearrange("(p t) c -> p t c", t=LANES)
+        page = [tile([P, T2], F32, f"page{t}", tag="row", bufs=ROW_RING) for t in range(LANES)]
+        xs_pieces = [(t, lo, lo + S // 2) for t in range(2) for lo in (0, S // 2)]
+        xs_pieces = xs_pieces + [(t, 0, S) for t in range(2, LANES)]
         xs_tiles = [tile([P, hi - lo], F32, f"xs{t}_{lo}") for t, lo, hi in xs_pieces]
-        wtx_raw = tile([P, 2, PACK, BANK], F32, "wtx_raw", tag="wide")
+        wtx_raw = tile([P, PASSES, LANES, BANK], F32, "wtx_raw", tag="wide")
 
         nc.sync.dma_start(idx2[:], offs2)
         for (t, lo, hi), xs_tile in zip(xs_pieces, xs_tiles):
             if lo == 0:
-                nc.sync.dma_start(out=page[t][:], in_=base_rows[:, t, :])
-            nc.sync.dma_start(out=xs_tile[:], in_=xs_rows[:, t, lo:hi])
+                nc.sync.dma_start(out=page[t][:], in_=base_lanes[:, t, :])
+            nc.sync.dma_start(out=xs_tile[:], in_=xs_lanes[:, t, lo:hi])
             if t == 0 and hi == S:
-                for g in range(2):
+                for g in range(PASSES):
                     nc.sync.dma_start(
                         out=wtx_raw[:, g, :, :],
-                        in_=wtx[:, BANK * g : BANK * (g + 1)].rearrange("(p j) c -> p j c", j=PACK),
+                        in_=wtx[:, BANK * g : BANK * (g + 1)].rearrange("(p i) c -> p i c", i=LANES),
                     )
 
-        wrx_raw = tile([P, 2, 2 * H], U8, "wrx_raw")
+        wrx_raw = tile([P, PASSES, 2 * H], U8, "wrx_raw")
         nc.sync.dma_start(
             out=wrx_raw[:].bitcast(I32), in_=wrx_words.rearrange("a p c -> p a c").bitcast(I32)
         )
-        tab = [tile([P, T], U32, f"tab{a}") for a in range(2)]
+        tab = [tile([P, T], U32, f"tab{a}") for a in range(PASSES)]
         for a in (1, 0):
             nc.sync.dma_start(
                 out=tab[a][:].bitcast(I32),
                 in_=tab_words[a].rearrange("p n i -> p (n i)").bitcast(I32),
             )
         nc.sync.dma_start(idx3[:], offs3)
-        cub_cols = tile([P, 2, PACK], F32, "cub_cols")
-        nc.sync.dma_start(out=cub_cols[:], in_=cub.rearrange("(g p t) -> p g t", g=2, t=PACK))
-        wdem = tile([P, 2, N], U32, "wdem")
+        cub_cols = tile([P, PASSES, LANES], F32, "cub_cols")
+        nc.sync.dma_start(out=cub_cols[:], in_=cub.rearrange("(g p t) -> p g t", g=PASSES, t=LANES))
+        wdem = tile([P, PASSES, N], U32, "wdem")
         nc.sync.dma_start(
             out=wdem[:].bitcast(I32), in_=wdem_words.rearrange("a p c i -> p a (c i)").bitcast(I32)
         )
-        load_packed_planes(wdem_planes, wdem_scales)
+        for quad in range(P // QUADRANT):
+            nc.sync.dma_start(
+                out=wdem_planes[QUADRANT * quad : QUADRANT * quad + 4 * PASSES, :].bitcast(I32),
+                in_=wdem_scales[:, 4 * quad : 4 * quad + 4, :].bitcast(I32),
+            )
         bias_cols = tile([P, N // P], F32, "bias_cols")
         with nc.allow_non_contiguous_dma(reason="one bias value to a partition"):
             nc.sync.dma_start(out=bias_cols[:], in_=bdem.rearrange("(n p) -> p n", p=P))
         spread_scale_rows(v_plane, v_rows)
         spread_scale_rows(wrx_plane, wrx_rows)
 
-        wtx_bf = tile([P, 2, PACK * BANK], BF16, "wtx_bf")
+        wtx_bf = tile([P, PASSES, LANES * BANK], BF16, "wtx_bf")
         wtx_codes = tile([P, H], U32, "wtx_codes")
         wtx_plane = tile([P, H], U8, "wtx_plane")
-        for g in range(2):
+        for g in range(PASSES):
             nc.scalar.activation(
-                out=wtx_bf[:, g, :].rearrange("p (t m j) -> p m j t", t=PACK, j=PACK),
-                in_=wtx_raw[:, g, :, :].rearrange("p j (m t) -> p m j t", t=PACK),
+                out=wtx_bf[:, g, :].rearrange("p (t m i) -> p m i t", t=LANES, i=LANES),
+                in_=wtx_raw[:, g, :, :].rearrange("p i (m t) -> p m i t", t=LANES),
                 func=ACT.Identity,
             )
             cols = slice(BANK * g, BANK * (g + 1))
@@ -142,56 +150,53 @@ def tile_list_duplex_cancel_filter_kernel(
                 out=wtx_codes[:, cols].bitcast(FP8X4), scales=wtx_plane[:, cols], in_=wtx_bf[:, g, :]
             )
 
-        page_bf = tile([P, T2, PACK], BF16, "page_bf", tag="wide")
+        page_bf = tile([P, T2, LANES], BF16, "page_bf", tag="wide")
+        split = T2 - BANK
         for (t, lo, hi), xs_tile in zip(xs_pieces, xs_tiles):
             nc.vector.tensor_copy(page[t][:].indirect(idx2[:, lo // 16 : hi // 16]), xs_tile[:])
             if hi == S and t < 2:
                 nc.scalar.copy(out=page_bf[:, :, t], in_=page[t][:])
             elif hi == S:
-                split = T2 - BANK
-                step = BANK if t == PACK - 1 else split
+                step = BANK if t == LANES - 1 else split
                 for c0 in range(0, split, step):
                     nc.scalar.copy(out=page_bf[:, c0 : c0 + step, t], in_=page[t][:, c0 : c0 + step])
                 nc.gpsimd.tensor_scalar(
                     page_bf[:, split:, t], page[t][:, split:], 1.0, 0.0, ALU.mult, ALU.add
                 )
 
-        half = J // 2
-        v1_first = tile([P, half], U32, "v1_first")
-        nc.vector.tensor_copy(v1_first[:], tab[1][:].indirect(idx[:, : half // 16]))
+        v1_first = tile([P, HALF], U32, "v1_first")
+        nc.vector.tensor_copy(v1_first[:], tab[1][:].indirect(idx[:, : HALF // 16]))
         v0 = tile([P, J], U32, "v0")
         nc.vector.tensor_copy(v0[:], tab[0][:].indirect(idx[:]))
         page_plane = tile([P, T2], U8, "page_plane")
         page_codes = tile([P, T2], U32, "page_codes", tag="tab0")
-        chunk_order = (0, 3, 1, 2)
-        for c in chunk_order:
-            cols = slice(c * BANK, (c + 1) * BANK)
+        page_pieces = [slice(c0, c0 + BANK) for c0 in (0, split, *range(BANK, split, BANK))]
+        for cols in page_pieces:
             nc.vector.quantize_mx(
                 out=page_codes[:, cols].bitcast(FP8X4),
                 scales=page_plane[:, cols],
                 in_=page_bf[:, cols, :].rearrange("p c t -> p (c t)"),
             )
-        v1 = [v1_first]
 
-        wrx = tile([P, 2, 2 * H], U8, "wrx", tag="wide")
+        wrx = tile([P, PASSES, 2 * H], U8, "wrx", tag="wide")
+        wrx_to = wrx[:].rearrange("p a c -> p (a c)").bitcast(U16)
+        wrx_from = wrx_raw[:].rearrange("p a c -> p (a c)").bitcast(U16)
         nc.vector.tensor_copy(
-            out=wrx[:].rearrange("p a c -> p (a c)").bitcast(U16).rearrange("p (h t m) -> p h t m", t=PACK, m=P),
-            in_=wrx_raw[:].rearrange("p a c -> p (a c)").bitcast(U16).rearrange("p (h m t) -> p h t m", t=PACK, m=P),
+            out=wrx_to.rearrange("p (h t m) -> p h t m", t=LANES, m=P),
+            in_=wrx_from.rearrange("p (h m t) -> p h t m", t=LANES, m=P),
         )
 
-        tiles = 2 * PACK
-        resid_plane = [tile([P, J], U8, f"resid_plane{g}") for g in range(2)]
-        leak = [tile([P, PACK, J], F32, f"leak{g}") for g in range(2)]
+        resid_plane = [tile([P, J], U8, f"resid_plane{g}") for g in range(PASSES)]
+        leak = [tile([P, LANES, J], F32, f"leak{g}") for g in range(PASSES)]
         out_rows = out.rearrange("(n p) j -> p n j", p=P)
 
-        def project(i):
+        def project_page(i):
             if i == 1:
                 a_rows = tile([P, T2], F32, f"a{i}", tag="wtx_bf")
             else:
-                a_rows = tile([P, T2], F32, f"a{i}", tag="row", bufs=6)
+                a_rows = tile([P, T2], F32, f"a{i}", tag="row", bufs=ROW_RING)
             rows = slice(P * i, P * (i + 1))
-            for c in chunk_order:
-                cols = slice(BANK * c, BANK * (c + 1))
+            for cols in page_pieces:
                 acc = psum.tile([P, BANK], F32, name="acc", tag="acc")
                 nc.tensor.matmul_mx(
                     out=acc[:],
@@ -199,88 +204,83 @@ def tile_list_duplex_cancel_filter_kernel(
                     rhs=page_codes[:, cols].bitcast(FP8X4), rhs_scale=page_plane[:, cols],
                     start=True, stop=True,
                 )
-                if i in () and c == chunk_order[-1]:
-                    nc.vector.tensor_copy(out=a_rows[:, cols], in_=acc[:])
-                else:
-                    nc.scalar.copy(out=a_rows[:, cols], in_=acc[:])
+                nc.scalar.copy(out=a_rows[:, cols], in_=acc[:])
             return a_rows
 
         def make_leak(i, a_rows, lo, hi):
-            g, t = divmod(i, PACK)
-            x = tile([P, hi - lo], F32, "x", bufs=3)
-            if i == tiles - 2:
-                gain = tile([P, hi - lo], F32, "last_pool_gain")
+            g, t = divmod(i, LANES)
+            x = tile([P, hi - lo], F32, "x", bufs=LEAK_RING)
+            if i == ROW_TILES - 2 and hi == J:
+                gain = tile([P, hi - lo], F32, "last_gpsimd_gain")
             else:
-                gain = tile([P, hi - lo], F32, "gain", bufs=3)
+                gain = tile([P, hi - lo], F32, "gain", bufs=LEAK_RING)
             nc.vector.tensor_copy(x[:], a_rows[:].indirect(idx3[:, lo // 16 : hi // 16]))
             nc.scalar.activation(out=gain[:], in_=x[:], func=ACT.Square)
-            if i in (7,):
+            cub_col = cub_cols[:, g, t : t + 1]
+            if i >= ROW_TILES - 2:
                 nc.scalar.activation(
-                    out=gain[:], in_=gain[:], func=ACT.Identity, scale=cub_cols[:, g, t : t + 1], bias=1.0
+                    out=gain[:], in_=gain[:], func=ACT.Identity, scale=cub_col, bias=1.0
                 )
             else:
-                nc.gpsimd.tensor_scalar(
-                    gain[:], gain[:], cub_cols[:, g, t : t + 1], 1.0, ALU.mult, ALU.add
-                )
-            if i in (0, 1, 6, 7):
-                nc.vector.tensor_tensor(leak[g][:, t, lo:hi], gain[:], x[:], ALU.mult)
-            else:
-                nc.gpsimd.tensor_tensor(leak[g][:, t, lo:hi], gain[:], x[:], ALU.mult)
+                nc.gpsimd.tensor_scalar(gain[:], gain[:], cub_col, 1.0, ALU.mult, ALU.add)
+            on_vector = i < VECTOR_FIRST or i == ROW_TILES - 1
+            engine = nc.vector if on_vector else nc.gpsimd
+            engine.tensor_tensor(leak[g][:, t, lo:hi], gain[:], x[:], ALU.mult)
 
         def project_received(g, j0, tag):
             cols = slice(j0, j0 + B_COLS)
-            b = psum.tile([P, PACK, B_COLS], F32, name="b", tag=tag)
-            words = (v0[:, cols], v1[j0 // half][:, j0 % half : j0 % half + B_COLS])
-            for t in range(PACK):
-                r0 = P * (PACK * g + t)
-                for a in range(2):
+            b = psum.tile([P, LANES, B_COLS], F32, name="b", tag=tag)
+            words = (v0[:, cols], v1[j0 // HALF][:, j0 % HALF : j0 % HALF + B_COLS])
+            for t in range(LANES):
+                r0 = P * (LANES * g + t)
+                for a in range(PASSES):
                     nc.tensor.matmul_mx(
                         out=b[:, t, :],
                         lhsT=wrx[:, a, 2 * r0 : 2 * (r0 + P)].bitcast(FP4X4),
                         lhsT_scale=wrx_plane[a][:, r0 : r0 + P],
                         rhs=words[a].bitcast(FP8X4), rhs_scale=v_plane[a][:, cols],
-                        start=(a == 0), stop=(a == 1),
+                        start=(a == 0), stop=(a == PASSES - 1),
                     )
             return b
 
         def subtract(g, j0, resid, b):
-            cols = slice(j0, j0 + B_COLS)
             nc.vector.tensor_tensor(
-                resid.rearrange("p (c i) t -> p c t i", i=4),
-                b[:].rearrange("p t (c i) -> p c t i", i=4),
-                leak[g][:, :, cols].rearrange("p t (c i) -> p c t i", i=4),
+                resid.rearrange("p (c i) t -> p c t i", i=LINE),
+                b[:].rearrange("p t (c i) -> p c t i", i=LINE),
+                leak[g][:, :, j0 : j0 + B_COLS].rearrange("p t (c i) -> p c t i", i=LINE),
                 ALU.subtract,
             )
 
-        def quantise_resid(g, resid, codes, cols):
+        def quantise_resid(g, resid, cols):
             nc.vector.quantize_mx(
-                out=codes[:, cols].bitcast(FP8X4),
+                out=resid_codes[g][:, cols].bitcast(FP8X4),
                 scales=resid_plane[g][:, cols],
                 in_=resid[:].rearrange("p c t -> p (c t)"),
             )
 
-        def filter_out(cols, tag, last):
-            width = cols.stop - cols.start
-            staged = tile([P, N // P, width], F32, "staged", bufs=4)
+        def filter_and_store(cols, tag):
+            last = cols.stop == J
+            staged = tile([P, N // P, Y_COLS], F32, "staged", bufs=J // Y_COLS)
             for group in ((0,), (1,), (2,)) if last else ((0, 1), (2,)):
-                y = psum.tile([P, len(group), width], F32, name="y", tag=tag)
-                for s, n in enumerate(group):
+                y = psum.tile([P, len(group), Y_COLS], F32, name="y", tag=tag)
+                for place, n in enumerate(group):
                     rows = slice(P * n, P * (n + 1))
-                    for g in range(2):
+                    for g in range(PASSES):
                         nc.tensor.matmul_mx(
-                            out=y[:, s, :],
-                            lhsT=wdem[:, g, rows].bitcast(FP8X4), lhsT_scale=wdem_planes[4 * g : P, rows],
-                            rhs=resid_codes[g][:, cols].bitcast(FP8X4), rhs_scale=resid_plane[g][:, cols],
-                            start=(g == 0), stop=(g == 1),
+                            out=y[:, place, :],
+                            lhsT=wdem[:, g, rows].bitcast(FP8X4),
+                            lhsT_scale=wdem_planes[4 * g : P, rows],
+                            rhs=resid_codes[g][:, cols].bitcast(FP8X4),
+                            rhs_scale=resid_plane[g][:, cols],
+                            start=(g == 0), stop=(g == PASSES - 1),
                         )
-                for s, n in enumerate(group):
+                for place, n in enumerate(group):
+                    bias = bias_cols[:, n : n + 1]
                     if last and n == 1:
-                        nc.vector.tensor_scalar(
-                            staged[:, n, :], y[:, s, :], bias_cols[:, n : n + 1], None, ALU.add
-                        )
+                        nc.vector.tensor_scalar(staged[:, n, :], y[:, place, :], bias, None, ALU.add)
                     else:
                         nc.scalar.activation(
-                            out=staged[:, n, :], in_=y[:, s, :], func=ACT.Identity, bias=bias_cols[:, n : n + 1]
+                            out=staged[:, n, :], in_=y[:, place, :], func=ACT.Identity, bias=bias
                         )
                     if last:
                         queue = nc.scalar if n == 2 else nc.sync
@@ -288,34 +288,35 @@ def tile_list_duplex_cancel_filter_kernel(
             if not last:
                 nc.sync.dma_start(out=out_rows[:, :, cols], in_=staged[:])
 
-        a_tiles = [project(i) for i in range(1)]
-        for i in range(tiles):
-            if len(a_tiles) < tiles:
-                a_tiles.append(project(len(a_tiles)))
-            if i == -1 and len(a_tiles) < tiles:
-                a_tiles.append(project(len(a_tiles)))
-            pieces = ((0, J // 2), (J // 2, J)) if i == tiles - 1 else ((0, J),)
+        v1 = [v1_first]
+        a_tiles = [project_page(0)]
+        for i in range(ROW_TILES):
+            if i + 1 < ROW_TILES:
+                a_tiles.append(project_page(i + 1))
+            pieces = ((0, HALF), (HALF, J)) if i >= ROW_TILES - 2 else ((0, J),)
             for lo, hi in pieces:
                 make_leak(i, a_tiles[i], lo, hi)
             if i == 1:
-                v1_second = tile([P, half], U32, "v1_second", tag="wtx_bf")
-                nc.vector.tensor_copy(v1_second[:], tab[1][:].indirect(idx[:, half // 16 :]))
+                v1_second = tile([P, HALF], U32, "v1_second", tag="wtx_bf")
+                nc.vector.tensor_copy(v1_second[:], tab[1][:].indirect(idx[:, HALF // 16 :]))
                 v1.append(v1_second)
 
-        resid0 = tile([P, J, PACK], BF16, "resid0")
+        resid0 = tile([P, J, LANES], BF16, "resid0")
         for j0 in range(0, J, B_COLS):
             subtract(0, j0, resid0[:, j0 : j0 + B_COLS, :], project_received(0, j0, "b"))
         resid_codes = [
-            tile([P, J], U32, "resid_codes0", tag="last_pool_gain"),
+            tile([P, J], U32, "resid_codes0", tag="last_gpsimd_gain"),
             tile([P, J], U32, "resid_codes1"),
         ]
-        quantise_resid(0, resid0, resid_codes[0], slice(0, J))
-        widths = (256, 256, 256, 256)
-        starts = [sum(widths[:n]) for n in range(len(widths))]
-        b_banks = [project_received(1, j0, "b" if j0 < J // 2 else "acc") for j0 in range(0, J, B_COLS)]
-        for j0, width in zip(starts, widths):
-            resid = tile([P, width, PACK], BF16, "resid1", bufs=3)
-            for lo in range(0, width, B_COLS):
-                subtract(1, j0 + lo, resid[:, lo : lo + B_COLS, :], b_banks[(j0 + lo) // B_COLS])
-            quantise_resid(1, resid, resid_codes[1], slice(j0, j0 + width))
-            filter_out(slice(j0, j0 + width), "acc" if j0 == J // 2 else "b", j0 + width == J)
+        quantise_resid(0, resid0, slice(0, J))
+
+        b_banks = [
+            project_received(1, j0, "b" if j0 < HALF else "acc") for j0 in range(0, J, B_COLS)
+        ]
+        for j0 in range(0, J, Y_COLS):
+            resid1 = tile([P, Y_COLS, LANES], BF16, "resid1", bufs=3)
+            for lo in range(0, Y_COLS, B_COLS):
+                subtract(1, j0 + lo, resid1[:, lo : lo + B_COLS, :], b_banks[(j0 + lo) // B_COLS])
+            cols = slice(j0, j0 + Y_COLS)
+            quantise_resid(1, resid1, cols)
+            filter_and_store(cols, "acc" if j0 == HALF else "b")

@@ -31,7 +31,8 @@ Y_COLS = 256
 PSUM_RING = 4
 ROW_RING = 6
 LEAK_RING = 3
-VECTOR_FIRST = 3
+VECTOR_FIRST = 2
+VECTOR_BANK_TILE = 5
 
 
 def tile_list_duplex_cancel_filter_kernel(
@@ -204,7 +205,10 @@ def tile_list_duplex_cancel_filter_kernel(
                     rhs=page_codes[:, cols].bitcast(FP8X4), rhs_scale=page_plane[:, cols],
                     start=True, stop=True,
                 )
-                nc.scalar.copy(out=a_rows[:, cols], in_=acc[:])
+                if i == VECTOR_BANK_TILE and cols == page_pieces[-1]:
+                    nc.vector.tensor_copy(out=a_rows[:, cols], in_=acc[:])
+                else:
+                    nc.scalar.copy(out=a_rows[:, cols], in_=acc[:])
             return a_rows
 
         def make_leak(i, a_rows, lo, hi):

@@ -28,11 +28,22 @@ ROW_TILES = PASSES * LANES
 HALF = J // 2
 B_COLS = BANK // LANES
 Y_COLS = 256
+A_RING = 3
 PSUM_RING = 4
 ROW_RING = 6
 LEAK_RING = 3
 VECTOR_FIRST = 2
 VECTOR_BANK_TILE = 5
+GAIN = "GGGGGSSS"
+PROD = "GGGGGGGG"
+VPROD = ()
+QAT = {512: (0, 256), 768: (512,), 1024: (768,)}
+PIN = "tab1"
+HALVES = (6, 7)
+VBANK = ((3, 3), (4, 3), (5, 3), (6, 3))
+FILL = (1, 2)
+SUB0_AFTER = 8
+G_COLS = 512
 
 
 def tile_list_duplex_cancel_filter_kernel(
@@ -47,6 +58,9 @@ def tile_list_duplex_cancel_filter_kernel(
 
         def tile(shape, dtype, name, tag=None, bufs=1):
             return sb.tile(shape, dtype, name=name, tag=tag or name, bufs=bufs, align_bytes=ALIGN)
+
+        def bank(shape, tag):
+            return psum.tile(shape, F32, name=tag, tag=tag, bufs=A_RING if tag == "acc" else 8 - A_RING)
 
         def zeroed_plane(width, name):
             plane = tile([P, width], U8, name)
@@ -84,7 +98,7 @@ def tile_list_duplex_cancel_filter_kernel(
         v_rows = tile([P, J], U8, "v_rows")
         nc.vector.tensor_copy(v_rows[:], tab_rows[:].indirect(idx[:]))
         wrx_rows = tile([P, H], U8, "wrx_rows")
-        nc.vector.tensor_copy(
+        nc.gpsimd.tensor_copy(
             out=wrx_rows[:].rearrange("p (g t m) -> p g t m", t=LANES, m=P),
             in_=wrx_rows_raw[:].rearrange("p (g m t) -> p g t m", t=LANES, m=P),
         )
@@ -97,6 +111,7 @@ def tile_list_duplex_cancel_filter_kernel(
         xs_tiles = [tile([P, hi - lo], F32, f"xs{t}_{lo}") for t, lo, hi in xs_pieces]
         wtx_raw = tile([P, PASSES, LANES, BANK], F32, "wtx_raw", tag="wide")
 
+        wrx_raw = tile([P, PASSES, 2 * H], U8, "wrx_raw")
         nc.sync.dma_start(idx2[:], offs2)
         for (t, lo, hi), xs_tile in zip(xs_pieces, xs_tiles):
             if lo == 0:
@@ -108,11 +123,12 @@ def tile_list_duplex_cancel_filter_kernel(
                         out=wtx_raw[:, g, :, :],
                         in_=wtx[:, BANK * g : BANK * (g + 1)].rearrange("(p i) c -> p i c", i=LANES),
                     )
+            if t == 1 and hi == S:
+                nc.sync.dma_start(
+                    out=wrx_raw[:].bitcast(I32),
+                    in_=wrx_words.rearrange("a p c -> p a c").bitcast(I32),
+                )
 
-        wrx_raw = tile([P, PASSES, 2 * H], U8, "wrx_raw")
-        nc.sync.dma_start(
-            out=wrx_raw[:].bitcast(I32), in_=wrx_words.rearrange("a p c -> p a c").bitcast(I32)
-        )
         tab = [tile([P, T], U32, f"tab{a}") for a in range(PASSES)]
         for a in (1, 0):
             nc.sync.dma_start(
@@ -151,8 +167,16 @@ def tile_list_duplex_cancel_filter_kernel(
                 out=wtx_codes[:, cols].bitcast(FP8X4), scales=wtx_plane[:, cols], in_=wtx_bf[:, g, :]
             )
 
+        wrx = tile([P, PASSES, 2 * H], U8, "wrx")
+        wrx_to = wrx[:].rearrange("p a c -> p (a c)").bitcast(U16)
+        wrx_from = wrx_raw[:].rearrange("p a c -> p (a c)").bitcast(U16)
+        nc.gpsimd.tensor_copy(
+            out=wrx_to.rearrange("p (h t m) -> p h t m", t=LANES, m=P),
+            in_=wrx_from.rearrange("p (h m t) -> p h t m", t=LANES, m=P),
+        )
+
         page_bf = tile([P, T2, LANES], BF16, "page_bf", tag="wide")
-        split = T2 - BANK
+        split = T2 - G_COLS
         for (t, lo, hi), xs_tile in zip(xs_pieces, xs_tiles):
             nc.vector.tensor_copy(page[t][:].indirect(idx2[:, lo // 16 : hi // 16]), xs_tile[:])
             if hi == S and t < 2:
@@ -160,80 +184,79 @@ def tile_list_duplex_cancel_filter_kernel(
             elif hi == S:
                 step = BANK if t == LANES - 1 else split
                 for c0 in range(0, split, step):
-                    nc.scalar.copy(out=page_bf[:, c0 : c0 + step, t], in_=page[t][:, c0 : c0 + step])
+                    c1 = min(c0 + step, split)
+                    nc.scalar.copy(out=page_bf[:, c0:c1, t], in_=page[t][:, c0:c1])
                 nc.gpsimd.tensor_scalar(
                     page_bf[:, split:, t], page[t][:, split:], 1.0, 0.0, ALU.mult, ALU.add
                 )
 
-        v1_first = tile([P, HALF], U32, "v1_first")
-        nc.vector.tensor_copy(v1_first[:], tab[1][:].indirect(idx[:, : HALF // 16]))
         v0 = tile([P, J], U32, "v0")
         nc.vector.tensor_copy(v0[:], tab[0][:].indirect(idx[:]))
         page_plane = tile([P, T2], U8, "page_plane")
         page_codes = tile([P, T2], U32, "page_codes", tag="tab0")
-        page_pieces = [slice(c0, c0 + BANK) for c0 in (0, split, *range(BANK, split, BANK))]
+        page_pieces = [slice(c0, c0 + BANK) for c0 in (0, T2 - BANK, *range(BANK, T2 - BANK, BANK))]
         for cols in page_pieces:
             nc.vector.quantize_mx(
                 out=page_codes[:, cols].bitcast(FP8X4),
                 scales=page_plane[:, cols],
                 in_=page_bf[:, cols, :].rearrange("p c t -> p (c t)"),
             )
+        v1 = []
 
-        wrx = tile([P, PASSES, 2 * H], U8, "wrx", tag="wide")
-        wrx_to = wrx[:].rearrange("p a c -> p (a c)").bitcast(U16)
-        wrx_from = wrx_raw[:].rearrange("p a c -> p (a c)").bitcast(U16)
-        nc.vector.tensor_copy(
-            out=wrx_to.rearrange("p (h t m) -> p h t m", t=LANES, m=P),
-            in_=wrx_from.rearrange("p (h m t) -> p h t m", t=LANES, m=P),
-        )
+        def gather_v1(tag):
+            half = len(v1)
+            words = tile([P, HALF], U32, f"v1_{half}", tag=tag)
+            lo = HALF * half // 16
+            nc.vector.tensor_copy(words[:], tab[1][:].indirect(idx[:, lo : lo + HALF // 16]))
+            v1.append(words)
 
-        resid_plane = [tile([P, J], U8, f"resid_plane{g}") for g in range(PASSES)]
-        leak = [tile([P, LANES, J], F32, f"leak{g}") for g in range(PASSES)]
+        leak = [tile([P, 2, LANES, HALF], F32, f"leak{g}") for g in range(PASSES)]
         out_rows = out.rearrange("(n p) j -> p n j", p=P)
 
         def project_page(i):
-            if i == 1:
-                a_rows = tile([P, T2], F32, f"a{i}", tag="wtx_bf")
+            if i in (1, 7):
+                a_rows = tile([P, T2], F32, f"a{i}", tag="wtx_bf" if i == 1 else "tab1")
             else:
                 a_rows = tile([P, T2], F32, f"a{i}", tag="row", bufs=ROW_RING)
             rows = slice(P * i, P * (i + 1))
-            for cols in page_pieces:
-                acc = psum.tile([P, BANK], F32, name="acc", tag="acc")
+            for q, cols in enumerate(page_pieces):
+                acc = bank([P, BANK], "b" if i < LANES and (LANES * i + q) % 8 >= A_RING else "acc")
                 nc.tensor.matmul_mx(
                     out=acc[:],
                     lhsT=wtx_codes[:, rows].bitcast(FP8X4), lhsT_scale=wtx_plane[:, rows],
                     rhs=page_codes[:, cols].bitcast(FP8X4), rhs_scale=page_plane[:, cols],
                     start=True, stop=True,
                 )
-                if i == VECTOR_BANK_TILE and cols == page_pieces[-1]:
+                if (i, q) in VBANK:
                     nc.vector.tensor_copy(out=a_rows[:, cols], in_=acc[:])
                 else:
                     nc.scalar.copy(out=a_rows[:, cols], in_=acc[:])
             return a_rows
 
-        def make_leak(i, a_rows, lo, hi):
+        def gather_x(i):
+            x = tile([P, J], F32, f"x{i}", tag=("xs2_0", "xs3_0", "wrx_raw", "x")[i % 4])
+            nc.vector.tensor_copy(x[:], a_tiles[i][:].indirect(idx3[:]))
+            x_tiles.append(x)
+
+        def make_leak(i, halves):
             g, t = divmod(i, LANES)
-            x = tile([P, hi - lo], F32, "x", bufs=LEAK_RING)
-            if i == ROW_TILES - 2 and hi == J:
-                gain = tile([P, hi - lo], F32, "last_gpsimd_gain")
-            else:
-                gain = tile([P, hi - lo], F32, "gain", bufs=LEAK_RING)
-            nc.vector.tensor_copy(x[:], a_rows[:].indirect(idx3[:, lo // 16 : hi // 16]))
-            nc.scalar.activation(out=gain[:], in_=x[:], func=ACT.Square)
+            x = x_tiles[i][:].rearrange("p (h j) -> p h j", j=HALF)[:, halves, :]
+            y = leak[g][:, halves, t, :]
+            nc.scalar.activation(out=y, in_=x, func=ACT.Square)
             cub_col = cub_cols[:, g, t : t + 1]
-            if i >= ROW_TILES - 2:
-                nc.scalar.activation(
-                    out=gain[:], in_=gain[:], func=ACT.Identity, scale=cub_col, bias=1.0
-                )
+            if GAIN[i] == "S":
+                gain = y
+                nc.scalar.activation(out=y, in_=y, func=ACT.Identity, scale=cub_col, bias=1.0)
             else:
-                nc.gpsimd.tensor_scalar(gain[:], gain[:], cub_col, 1.0, ALU.mult, ALU.add)
-            on_vector = i < VECTOR_FIRST or i == ROW_TILES - 1
-            engine = nc.vector if on_vector else nc.gpsimd
-            engine.tensor_tensor(leak[g][:, t, lo:hi], gain[:], x[:], ALU.mult)
+                gain_tile = tile([P, 2, HALF], F32, "gain")
+                gain = gain_tile[:, halves, :]
+                nc.gpsimd.tensor_scalar(gain, y, cub_col, 1.0, ALU.mult, ALU.add)
+            engine = nc.vector if (i, halves.start) in VPROD else nc.gpsimd
+            engine.tensor_tensor(y, gain, x, ALU.mult)
 
         def project_received(g, j0, tag):
             cols = slice(j0, j0 + B_COLS)
-            b = psum.tile([P, LANES, B_COLS], F32, name="b", tag=tag)
+            b = bank([P, LANES, B_COLS], tag)
             words = (v0[:, cols], v1[j0 // HALF][:, j0 % HALF : j0 % HALF + B_COLS])
             for t in range(LANES):
                 r0 = P * (LANES * g + t)
@@ -251,22 +274,15 @@ def tile_list_duplex_cancel_filter_kernel(
             nc.vector.tensor_tensor(
                 resid.rearrange("p (c i) t -> p c t i", i=LINE),
                 b[:].rearrange("p t (c i) -> p c t i", i=LINE),
-                leak[g][:, :, j0 : j0 + B_COLS].rearrange("p t (c i) -> p c t i", i=LINE),
+                leak[g][:, j0 // HALF, :, j0 % HALF : j0 % HALF + B_COLS].rearrange("p t (c i) -> p c t i", i=LINE),
                 ALU.subtract,
             )
 
-        def quantise_resid(g, resid, cols):
-            nc.vector.quantize_mx(
-                out=resid_codes[g][:, cols].bitcast(FP8X4),
-                scales=resid_plane[g][:, cols],
-                in_=resid[:].rearrange("p c t -> p (c t)"),
-            )
-
-        def filter_and_store(cols, tag):
+        def filter_and_store(cols, tag, codes, plane):
             last = cols.stop == J
             staged = tile([P, N // P, Y_COLS], F32, "staged", bufs=J // Y_COLS)
             for group in ((0,), (1,), (2,)) if last else ((0, 1), (2,)):
-                y = psum.tile([P, len(group), Y_COLS], F32, name="y", tag=tag)
+                y = bank([P, len(group), Y_COLS], tag)
                 for place, n in enumerate(group):
                     rows = slice(P * n, P * (n + 1))
                     for g in range(PASSES):
@@ -274,8 +290,8 @@ def tile_list_duplex_cancel_filter_kernel(
                             out=y[:, place, :],
                             lhsT=wdem[:, g, rows].bitcast(FP8X4),
                             lhsT_scale=wdem_planes[4 * g : P, rows],
-                            rhs=resid_codes[g][:, cols].bitcast(FP8X4),
-                            rhs_scale=resid_plane[g][:, cols],
+                            rhs=codes[:, g, :].bitcast(FP8X4),
+                            rhs_scale=plane[:, g, :],
                             start=(g == 0), stop=(g == PASSES - 1),
                         )
                 for place, n in enumerate(group):
@@ -292,35 +308,44 @@ def tile_list_duplex_cancel_filter_kernel(
             if not last:
                 nc.sync.dma_start(out=out_rows[:, :, cols], in_=staged[:])
 
-        v1 = [v1_first]
+        def finish(j0):
+            codes = tile([P, PASSES, Y_COLS], U32, f"codes{j0}")
+            plane = tile([P, PASSES, Y_COLS], U8, f"plane{j0}")
+            nc.vector.quantize_mx(
+                out=codes[:].rearrange("p g c -> p (g c)").bitcast(FP8X4),
+                scales=plane[:].rearrange("p g c -> p (g c)"),
+                in_=resid[j0 // Y_COLS].rearrange("p g c t -> p (g c t)"),
+            )
+            filter_and_store(slice(j0, j0 + Y_COLS), "b", codes, plane)
+
+        x_tiles = []
         a_tiles = [project_page(0)]
-        for i in range(ROW_TILES):
-            if i + 1 < ROW_TILES:
-                a_tiles.append(project_page(i + 1))
-            pieces = ((0, HALF), (HALF, J)) if i >= ROW_TILES - 2 else ((0, J),)
-            for lo, hi in pieces:
-                make_leak(i, a_tiles[i], lo, hi)
+        gather_v1("wide")
+        for i in range(5):
+            a_tiles.append(project_page(i + 1))
+            gather_x(i)
+            make_leak(i, slice(0, 2))
             if i == 1:
-                v1_second = tile([P, HALF], U32, "v1_second", tag="wtx_bf")
-                nc.vector.tensor_copy(v1_second[:], tab[1][:].indirect(idx[:, HALF // 16 :]))
-                v1.append(v1_second)
+                gather_v1("wtx_bf")
+        a_tiles.append(project_page(6))
+        a_tiles.append(project_page(7))
+        for i in range(5, ROW_TILES):
+            gather_x(i)
+        make_leak(5, slice(0, 2))
+        for h in range(2):
+            for i in (6, 7):
+                make_leak(i, slice(h, h + 1))
 
-        resid0 = tile([P, J, LANES], BF16, "resid0")
-        for j0 in range(0, J, B_COLS):
-            subtract(0, j0, resid0[:, j0 : j0 + B_COLS, :], project_received(0, j0, "b"))
-        resid_codes = [
-            tile([P, J], U32, "resid_codes0", tag="last_gpsimd_gain"),
-            tile([P, J], U32, "resid_codes1"),
-        ]
-        quantise_resid(0, resid0, slice(0, J))
-
-        b_banks = [
-            project_received(1, j0, "b" if j0 < HALF else "acc") for j0 in range(0, J, B_COLS)
-        ]
-        for j0 in range(0, J, Y_COLS):
-            resid1 = tile([P, Y_COLS, LANES], BF16, "resid1", bufs=3)
-            for lo in range(0, Y_COLS, B_COLS):
-                subtract(1, j0 + lo, resid1[:, lo : lo + B_COLS, :], b_banks[(j0 + lo) // B_COLS])
-            cols = slice(j0, j0 + Y_COLS)
-            quantise_resid(1, resid1, cols)
-            filter_and_store(cols, "acc" if j0 == HALF else "b")
+        resid_all = tile([P, J // Y_COLS, PASSES, Y_COLS, LANES], BF16, "resid", tag=PIN)
+        resid = [resid_all[:, c] for c in range(J // Y_COLS)]
+        for g in range(PASSES):
+            banks = [
+                project_received(g, j0, "b" if j0 < B_COLS * (8 - A_RING) else "acc")
+                for j0 in range(0, J, B_COLS)
+            ]
+            for j0 in range(0, J, B_COLS):
+                lo = j0 % Y_COLS
+                subtract(g, j0, resid[j0 // Y_COLS][:, g, lo : lo + B_COLS, :], banks[j0 // B_COLS])
+                if g == 1 and j0 + B_COLS in QAT:
+                    for c0 in QAT[j0 + B_COLS]:
+                        finish(c0)

@@ -36,14 +36,22 @@ VECTOR_FIRST = 2
 VECTOR_BANK_TILE = 5
 GAIN = "GGGGGSSS"
 PROD = "GGGGGGGG"
+FTAG = ("wtx_bf1", "wtx_bf0")
+AHEAD = 1
+AFROM = 0
+XS0 = 256
+NFIRST = 1
+CUTS = (0, 256, 512, 768, 896, 1024)
+BT = 4
+NF = 1
 VPROD = ()
 QAT = {512: (0, 256), 768: (512,), 1024: (768,)}
 PIN = "tab1"
 HALVES = (6, 7)
-VBANK = ((3, 3), (4, 3), (5, 3), (6, 3))
-FILL = (1, 2)
+VBANK = ((4, 0), (5, 0), (6, 0), (7, 0))
+FILL = (0, 2)
 SUB0_AFTER = 8
-G_COLS = 512
+G_COLS = 640
 
 
 def tile_list_duplex_cancel_filter_kernel(
@@ -67,13 +75,13 @@ def tile_list_duplex_cancel_filter_kernel(
             nc.gpsimd.memset(plane[:].bitcast(I32), 0)
             return plane
 
-        def load_scale_rows(scales, name):
+        def load_scale_rows(scales, name, engine):
             rows = tile([P, scales.shape[2]], U8, name)
             nc.sync.dma_start(
                 out=rows[0:32, :].bitcast(I32), in_=scales.rearrange("a q c -> (a q) c").bitcast(I32)
             )
-            nc.vector.memset(rows[32:64, :].bitcast(I32), 0)
-            nc.vector.memset(rows[64:128, :].bitcast(I32), 0)
+            engine.memset(rows[32:64, :].bitcast(I32), 0)
+            engine.memset(rows[64:128, :].bitcast(I32), 0)
             return rows
 
         def spread_scale_rows(planes, rows):
@@ -90,47 +98,53 @@ def tile_list_duplex_cancel_filter_kernel(
         idx3 = lists.tile([P, J // 16], U16, name="idx3")
 
         nc.sync.dma_start(idx[:], offs)
-        tab_rows = load_scale_rows(tab_scales, "tab_rows")
-        wrx_rows_raw = load_scale_rows(wrx_scales, "wrx_rows_raw")
-        wdem_planes = zeroed_plane(N, "wdem_planes")
-        v_plane = [zeroed_plane(J, f"v_plane{a}") for a in range(PASSES)]
-        wrx_plane = [zeroed_plane(H, f"wrx_plane{a}") for a in range(PASSES)]
+        tab_rows = load_scale_rows(tab_scales, "tab_rows", nc.vector)
         v_rows = tile([P, J], U8, "v_rows")
         nc.vector.tensor_copy(v_rows[:], tab_rows[:].indirect(idx[:]))
-        wrx_rows = tile([P, H], U8, "wrx_rows")
-        nc.gpsimd.tensor_copy(
-            out=wrx_rows[:].rearrange("p (g t m) -> p g t m", t=LANES, m=P),
-            in_=wrx_rows_raw[:].rearrange("p (g m t) -> p g t m", t=LANES, m=P),
-        )
 
         base_lanes = base.rearrange("(p t) c -> p t c", t=LANES)
         xs_lanes = xs.rearrange("(p t) c -> p t c", t=LANES)
         page = [tile([P, T2], F32, f"page{t}", tag="row", bufs=ROW_RING) for t in range(LANES)]
-        xs_pieces = [(t, lo, lo + S // 2) for t in range(2) for lo in (0, S // 2)]
-        xs_pieces = xs_pieces + [(t, 0, S) for t in range(2, LANES)]
+        xs_pieces = [(0, 0, XS0), (0, XS0, S), (1, 0, S), (2, 0, S // 2), (2, S // 2, S), (3, 0, S)]
         xs_tiles = [tile([P, hi - lo], F32, f"xs{t}_{lo}") for t, lo, hi in xs_pieces]
-        wtx_raw = tile([P, PASSES, LANES, BANK], F32, "wtx_raw", tag="wide")
-
+        wtx_raw = [
+            tile([P, LANES, BANK], F32, f"wtx_raw{g}", tag="wide" if g == 0 else None)
+            for g in range(PASSES)
+        ]
         wrx_raw = tile([P, PASSES, 2 * H], U8, "wrx_raw")
+
+        def load_wtx(g):
+            nc.sync.dma_start(
+                out=wtx_raw[g][:],
+                in_=wtx[:, BANK * g : BANK * (g + 1)].rearrange("(p i) c -> p i c", i=LANES),
+            )
+
         nc.sync.dma_start(idx2[:], offs2)
         for (t, lo, hi), xs_tile in zip(xs_pieces, xs_tiles):
             if lo == 0:
                 nc.sync.dma_start(out=page[t][:], in_=base_lanes[:, t, :])
             nc.sync.dma_start(out=xs_tile[:], in_=xs_lanes[:, t, lo:hi])
             if t == 0 and hi == S:
-                for g in range(PASSES):
-                    nc.sync.dma_start(
-                        out=wtx_raw[:, g, :, :],
-                        in_=wtx[:, BANK * g : BANK * (g + 1)].rearrange("(p i) c -> p i c", i=LANES),
-                    )
-            if t == 1 and hi == S:
+                wrx_rows_raw = load_scale_rows(wrx_scales, "wrx_rows_raw", nc.gpsimd)
+            if t == 1:
+                load_wtx(0)
                 nc.sync.dma_start(
                     out=wrx_raw[:].bitcast(I32),
                     in_=wrx_words.rearrange("a p c -> p a c").bitcast(I32),
                 )
+            if t == 2 and lo == 0:
+                load_wtx(1)
+        wdem_planes = zeroed_plane(N, "wdem_planes")
+        v_plane = [zeroed_plane(J, f"v_plane{a}") for a in range(PASSES)]
+        wrx_plane = [zeroed_plane(H, f"wrx_plane{a}") for a in range(PASSES)]
+        wrx_rows = tile([P, H], U8, "wrx_rows")
+        nc.gpsimd.tensor_copy(
+            out=wrx_rows[:].rearrange("p (g t m) -> p g t m", t=LANES, m=P),
+            in_=wrx_rows_raw[:].rearrange("p (g m t) -> p g t m", t=LANES, m=P),
+        )
 
         tab = [tile([P, T], U32, f"tab{a}") for a in range(PASSES)]
-        for a in (1, 0):
+        for a in range(PASSES):
             nc.sync.dma_start(
                 out=tab[a][:].bitcast(I32),
                 in_=tab_words[a].rearrange("p n i -> p (n i)").bitcast(I32),
@@ -153,18 +167,12 @@ def tile_list_duplex_cancel_filter_kernel(
         spread_scale_rows(v_plane, v_rows)
         spread_scale_rows(wrx_plane, wrx_rows)
 
-        wtx_bf = tile([P, PASSES, LANES * BANK], BF16, "wtx_bf")
-        wtx_codes = tile([P, H], U32, "wtx_codes")
-        wtx_plane = tile([P, H], U8, "wtx_plane")
+        wtx_bf = [tile([P, LANES * BANK], BF16, f"wtx_bf{g}") for g in range(PASSES)]
         for g in range(PASSES):
             nc.scalar.activation(
-                out=wtx_bf[:, g, :].rearrange("p (t m i) -> p m i t", t=LANES, i=LANES),
-                in_=wtx_raw[:, g, :, :].rearrange("p i (m t) -> p m i t", t=LANES),
+                out=wtx_bf[g][:].rearrange("p (t m i) -> p m i t", t=LANES, i=LANES),
+                in_=wtx_raw[g][:].rearrange("p i (m t) -> p m i t", t=LANES),
                 func=ACT.Identity,
-            )
-            cols = slice(BANK * g, BANK * (g + 1))
-            nc.vector.quantize_mx(
-                out=wtx_codes[:, cols].bitcast(FP8X4), scales=wtx_plane[:, cols], in_=wtx_bf[:, g, :]
             )
 
         wrx = tile([P, PASSES, 2 * H], U8, "wrx")
@@ -179,9 +187,7 @@ def tile_list_duplex_cancel_filter_kernel(
         split = T2 - G_COLS
         for (t, lo, hi), xs_tile in zip(xs_pieces, xs_tiles):
             nc.vector.tensor_copy(page[t][:].indirect(idx2[:, lo // 16 : hi // 16]), xs_tile[:])
-            if hi == S and t < 2:
-                nc.scalar.copy(out=page_bf[:, :, t], in_=page[t][:])
-            elif hi == S:
+            if hi == S:
                 step = BANK if t == LANES - 1 else split
                 for c0 in range(0, split, step):
                     c1 = min(c0 + step, split)
@@ -192,15 +198,31 @@ def tile_list_duplex_cancel_filter_kernel(
 
         v0 = tile([P, J], U32, "v0")
         nc.vector.tensor_copy(v0[:], tab[0][:].indirect(idx[:]))
+        codes_wp = tile([P, T2 + H], U32, "codes_wp", tag="tab0")
+        page_codes = codes_wp[:, :T2]
+        wtx_codes = [codes_wp[:, T2 + BANK * g : T2 + BANK * (g + 1)] for g in range(PASSES)]
+        wtx_plane = [tile([P, BANK], U8, f"wtx_plane{g}") for g in range(PASSES)]
         page_plane = tile([P, T2], U8, "page_plane")
-        page_codes = tile([P, T2], U32, "page_codes", tag="tab0")
-        page_pieces = [slice(c0, c0 + BANK) for c0 in (0, T2 - BANK, *range(BANK, T2 - BANK, BANK))]
+
+        def quantise_wtx(g, lo, hi):
+            nc.vector.quantize_mx(
+                out=wtx_codes[g][:, lo:hi].bitcast(FP8X4),
+                scales=wtx_plane[g][:, lo:hi],
+                in_=wtx_bf[g][:, LANES * lo : LANES * hi],
+            )
+
+        quantise_wtx(0, 0, P)
+        page_pieces = [slice(c0, c0 + BANK) for c0 in (T2 - BANK, *range(0, T2 - BANK, BANK))]
         for cols in page_pieces:
+            if cols == page_pieces[-1]:
+                quantise_wtx(1, 0, BANK)
             nc.vector.quantize_mx(
                 out=page_codes[:, cols].bitcast(FP8X4),
                 scales=page_plane[:, cols],
                 in_=page_bf[:, cols, :].rearrange("p c t -> p (c t)"),
             )
+        quantise_wtx(0, P, 2 * P)
+        quantise_wtx(0, 2 * P, BANK)
         v1 = []
 
         def gather_v1(tag):
@@ -214,16 +236,17 @@ def tile_list_duplex_cancel_filter_kernel(
         out_rows = out.rearrange("(n p) j -> p n j", p=P)
 
         def project_page(i):
-            if i in (1, 7):
-                a_rows = tile([P, T2], F32, f"a{i}", tag="wtx_bf" if i == 1 else "tab1")
+            if i in (1, 6, 7):
+                a_rows = tile([P, T2], F32, f"a{i}", tag={1: "wtx_bf0", 6: "wtx_bf1", 7: "tab1"}[i])
             else:
                 a_rows = tile([P, T2], F32, f"a{i}", tag="row", bufs=ROW_RING)
-            rows = slice(P * i, P * (i + 1))
+            g, t = divmod(i, LANES)
+            rows = slice(P * t, P * (t + 1))
             for q, cols in enumerate(page_pieces):
-                acc = bank([P, BANK], "b" if i < LANES and (LANES * i + q) % 8 >= A_RING else "acc")
+                acc = bank([P, BANK], "b" if i < BT and q >= A_RING else "acc")
                 nc.tensor.matmul_mx(
                     out=acc[:],
-                    lhsT=wtx_codes[:, rows].bitcast(FP8X4), lhsT_scale=wtx_plane[:, rows],
+                    lhsT=wtx_codes[g][:, rows].bitcast(FP8X4), lhsT_scale=wtx_plane[g][:, rows],
                     rhs=page_codes[:, cols].bitcast(FP8X4), rhs_scale=page_plane[:, cols],
                     start=True, stop=True,
                 )
@@ -234,7 +257,7 @@ def tile_list_duplex_cancel_filter_kernel(
             return a_rows
 
         def gather_x(i):
-            x = tile([P, J], F32, f"x{i}", tag=("xs2_0", "xs3_0", "wrx_raw", "x")[i % 4])
+            x = tile([P, J], F32, f"x{i}", tag=("xs3_0", "xs1_0", "wrx_raw", "x")[i % 4])
             nc.vector.tensor_copy(x[:], a_tiles[i][:].indirect(idx3[:]))
             x_tiles.append(x)
 
@@ -242,12 +265,15 @@ def tile_list_duplex_cancel_filter_kernel(
             g, t = divmod(i, LANES)
             x = x_tiles[i][:].rearrange("p (h j) -> p h j", j=HALF)[:, halves, :]
             y = leak[g][:, halves, t, :]
-            nc.scalar.activation(out=y, in_=x, func=ACT.Square)
             cub_col = cub_cols[:, g, t : t + 1]
             if GAIN[i] == "S":
                 gain = y
-                nc.scalar.activation(out=y, in_=y, func=ACT.Identity, scale=cub_col, bias=1.0)
+                square_tile = tile([P, 2, HALF], F32, "square")
+                square = square_tile[:, halves, :]
+                nc.scalar.activation(out=square, in_=x, func=ACT.Square)
+                nc.scalar.activation(out=y, in_=square, func=ACT.Identity, scale=cub_col, bias=1.0)
             else:
+                nc.scalar.activation(out=y, in_=x, func=ACT.Square)
                 gain_tile = tile([P, 2, HALF], F32, "gain")
                 gain = gain_tile[:, halves, :]
                 nc.gpsimd.tensor_scalar(gain, y, cub_col, 1.0, ALU.mult, ALU.add)
@@ -278,11 +304,12 @@ def tile_list_duplex_cancel_filter_kernel(
                 ALU.subtract,
             )
 
-        def filter_and_store(cols, tag, codes, plane):
+        def filter_and_store(cols, codes, plane):
             last = cols.stop == J
-            staged = tile([P, N // P, Y_COLS], F32, "staged", bufs=J // Y_COLS)
+            width = cols.stop - cols.start
+            staged = tile([P, N // P, width], F32, f"staged{cols.start}")
             for group in ((0,), (1,), (2,)) if last else ((0, 1), (2,)):
-                y = bank([P, len(group), Y_COLS], tag)
+                y = bank([P, len(group), width], "b")
                 for place, n in enumerate(group):
                     rows = slice(P * n, P * (n + 1))
                     for g in range(PASSES):
@@ -308,27 +335,32 @@ def tile_list_duplex_cancel_filter_kernel(
             if not last:
                 nc.sync.dma_start(out=out_rows[:, :, cols], in_=staged[:])
 
-        def finish(j0):
-            codes = tile([P, PASSES, Y_COLS], U32, f"codes{j0}")
-            plane = tile([P, PASSES, Y_COLS], U8, f"plane{j0}")
+        def finish(c):
+            width = CUTS[c + 1] - CUTS[c]
+            codes = tile([P, PASSES, width], U32, f"codes{c}")
+            plane = tile([P, PASSES, width], U8, f"plane{c}")
             nc.vector.quantize_mx(
                 out=codes[:].rearrange("p g c -> p (g c)").bitcast(FP8X4),
                 scales=plane[:].rearrange("p g c -> p (g c)"),
-                in_=resid[j0 // Y_COLS].rearrange("p g c t -> p (g c t)"),
+                in_=resid[c].rearrange("p g c t -> p (g c t)"),
             )
-            filter_and_store(slice(j0, j0 + Y_COLS), "b", codes, plane)
+            filter_and_store(slice(CUTS[c], CUTS[c + 1]), codes, plane)
 
         x_tiles = []
         a_tiles = [project_page(0)]
-        gather_v1("wide")
+        if FILL[0] == 0:
+            gather_v1(None)
         for i in range(5):
-            a_tiles.append(project_page(i + 1))
+            while len(a_tiles) < min(i + 1 + (AHEAD if i >= AFROM else 1), ROW_TILES):
+                a_tiles.append(project_page(len(a_tiles)))
             gather_x(i)
             make_leak(i, slice(0, 2))
-            if i == 1:
-                gather_v1("wtx_bf")
-        a_tiles.append(project_page(6))
-        a_tiles.append(project_page(7))
+            if i + 1 == FILL[0]:
+                gather_v1(FTAG[0])
+            if i + 1 == FILL[1]:
+                gather_v1(FTAG[1])
+        while len(a_tiles) < ROW_TILES:
+            a_tiles.append(project_page(len(a_tiles)))
         for i in range(5, ROW_TILES):
             gather_x(i)
         make_leak(5, slice(0, 2))
@@ -336,16 +368,26 @@ def tile_list_duplex_cancel_filter_kernel(
             for i in (6, 7):
                 make_leak(i, slice(h, h + 1))
 
-        resid_all = tile([P, J // Y_COLS, PASSES, Y_COLS, LANES], BF16, "resid", tag=PIN)
-        resid = [resid_all[:, c] for c in range(J // Y_COLS)]
+        first = CUTS[NF]
+        resid_first = tile([P, PASSES * first * LANES], BF16, "resid_first", tag="wtx_bf1")
+        resid_rest = tile([P, PASSES * (J - first) * LANES], BF16, "resid_rest", tag=PIN)
+        resid = [
+            resid_first[:, PASSES * LANES * lo : PASSES * LANES * hi]
+            if lo < first
+            else resid_rest[:, PASSES * LANES * (lo - first) : PASSES * LANES * (hi - first)]
+            for lo, hi in zip(CUTS, CUTS[1:])
+        ]
+        resid = [r.rearrange("p (g c t) -> p g c t", g=PASSES, t=LANES) for r in resid]
         for g in range(PASSES):
             banks = [
                 project_received(g, j0, "b" if j0 < B_COLS * (8 - A_RING) else "acc")
                 for j0 in range(0, J, B_COLS)
             ]
-            for j0 in range(0, J, B_COLS):
-                lo = j0 % Y_COLS
-                subtract(g, j0, resid[j0 // Y_COLS][:, g, lo : lo + B_COLS, :], banks[j0 // B_COLS])
-                if g == 1 and j0 + B_COLS in QAT:
-                    for c0 in QAT[j0 + B_COLS]:
-                        finish(c0)
+            for c in range(len(CUTS) - 1):
+                for j0 in range(CUTS[c], CUTS[c + 1], B_COLS):
+                    lo = j0 - CUTS[c]
+                    subtract(g, j0, resid[c][:, g, lo : lo + B_COLS, :], banks[j0 // B_COLS])
+                if g == 1 and c == 1:
+                    finish(0)
+                if g == 1 and c >= 1:
+                    finish(c)

@@ -44,6 +44,12 @@ NFIRST = 1
 CUTS = (0, 256, 512, 768, 896, 1024)
 BT = 4
 NF = 1
+G_EARLY = 640
+V1FIRST = 0
+VLAST = 1
+XH = ()
+TAILP = ((5, 0, 2), (6, 0, 1), (7, 0, 1), (6, 1, 2), (7, 1, 2))
+PINI = 6
 VPROD = ()
 QAT = {512: (0, 256), 768: (512,), 1024: (768,)}
 PIN = "tab1"
@@ -144,7 +150,7 @@ def tile_list_duplex_cancel_filter_kernel(
         )
 
         tab = [tile([P, T], U32, f"tab{a}") for a in range(PASSES)]
-        for a in range(PASSES):
+        for a in (1, 0) if V1FIRST else (0, 1):
             nc.sync.dma_start(
                 out=tab[a][:].bitcast(I32),
                 in_=tab_words[a].rearrange("p n i -> p (n i)").bitcast(I32),
@@ -184,10 +190,10 @@ def tile_list_duplex_cancel_filter_kernel(
         )
 
         page_bf = tile([P, T2, LANES], BF16, "page_bf", tag="wide")
-        split = T2 - G_COLS
         for (t, lo, hi), xs_tile in zip(xs_pieces, xs_tiles):
             nc.vector.tensor_copy(page[t][:].indirect(idx2[:, lo // 16 : hi // 16]), xs_tile[:])
             if hi == S:
+                split = T2 - (G_EARLY if t < 2 else G_COLS)
                 step = BANK if t == LANES - 1 else split
                 for c0 in range(0, split, step):
                     c1 = min(c0 + step, split)
@@ -196,6 +202,9 @@ def tile_list_duplex_cancel_filter_kernel(
                     page_bf[:, split:, t], page[t][:, split:], 1.0, 0.0, ALU.mult, ALU.add
                 )
 
+        v1 = [tile([P, HALF], U32, "v1_0")]
+        if V1FIRST:
+            nc.vector.tensor_copy(v1[0][:], tab[1][:].indirect(idx[:, : HALF // 16]))
         v0 = tile([P, J], U32, "v0")
         nc.vector.tensor_copy(v0[:], tab[0][:].indirect(idx[:]))
         codes_wp = tile([P, T2 + H], U32, "codes_wp", tag="tab0")
@@ -223,7 +232,8 @@ def tile_list_duplex_cancel_filter_kernel(
             )
         quantise_wtx(0, P, 2 * P)
         quantise_wtx(0, 2 * P, BANK)
-        v1 = []
+        if not V1FIRST:
+            nc.vector.tensor_copy(v1[0][:], tab[1][:].indirect(idx[:, : HALF // 16]))
 
         def gather_v1(tag):
             half = len(v1)
@@ -236,8 +246,8 @@ def tile_list_duplex_cancel_filter_kernel(
         out_rows = out.rearrange("(n p) j -> p n j", p=P)
 
         def project_page(i):
-            if i in (1, 6, 7):
-                a_rows = tile([P, T2], F32, f"a{i}", tag={1: "wtx_bf0", 6: "wtx_bf1", 7: "tab1"}[i])
+            if i in (1, PINI, 7):
+                a_rows = tile([P, T2], F32, f"a{i}", tag={1: "wtx_bf0", PINI: "wtx_bf1", 7: "tab1"}[i])
             else:
                 a_rows = tile([P, T2], F32, f"a{i}", tag="row", bufs=ROW_RING)
             g, t = divmod(i, LANES)
@@ -258,27 +268,42 @@ def tile_list_duplex_cancel_filter_kernel(
 
         def gather_x(i):
             x = tile([P, J], F32, f"x{i}", tag=("xs3_0", "xs1_0", "wrx_raw", "x")[i % 4])
-            nc.vector.tensor_copy(x[:], a_tiles[i][:].indirect(idx3[:]))
+            if i in XH:
+                for h in range(2):
+                    lo = HALF * h
+                    nc.vector.tensor_copy(
+                        x[:, lo : lo + HALF], a_tiles[i][:].indirect(idx3[:, lo // 16 : (lo + HALF) // 16])
+                    )
+            else:
+                nc.vector.tensor_copy(x[:], a_tiles[i][:].indirect(idx3[:]))
             x_tiles.append(x)
 
-        def make_leak(i, halves):
+        def operands(i, halves):
             g, t = divmod(i, LANES)
             x = x_tiles[i][:].rearrange("p (h j) -> p h j", j=HALF)[:, halves, :]
-            y = leak[g][:, halves, t, :]
-            cub_col = cub_cols[:, g, t : t + 1]
+            return x, leak[g][:, halves, t, :]
+
+        def square(i, halves):
+            x, y = operands(i, halves)
+            nc.scalar.activation(out=y, in_=x, func=ACT.Square)
+
+        def make_gain(i, halves):
+            x, y = operands(i, halves)
+            cub_col = cub_cols[:, i // LANES, i % LANES : i % LANES + 1]
             if GAIN[i] == "S":
-                gain = y
-                square_tile = tile([P, 2, HALF], F32, "square")
-                square = square_tile[:, halves, :]
-                nc.scalar.activation(out=square, in_=x, func=ACT.Square)
-                nc.scalar.activation(out=y, in_=square, func=ACT.Identity, scale=cub_col, bias=1.0)
+                nc.scalar.activation(out=y, in_=y, func=ACT.Identity, scale=cub_col, bias=1.0)
             else:
-                nc.scalar.activation(out=y, in_=x, func=ACT.Square)
-                gain_tile = tile([P, 2, HALF], F32, "gain")
-                gain = gain_tile[:, halves, :]
-                nc.gpsimd.tensor_scalar(gain, y, cub_col, 1.0, ALU.mult, ALU.add)
+                nc.gpsimd.tensor_scalar(y, y, cub_col, 1.0, ALU.mult, ALU.add)
+
+        def multiply(i, halves):
+            x, y = operands(i, halves)
             engine = nc.vector if (i, halves.start) in VPROD else nc.gpsimd
-            engine.tensor_tensor(y, gain, x, ALU.mult)
+            engine.tensor_tensor(y, y, x, ALU.mult)
+
+        def make_leak(i, halves):
+            square(i, halves)
+            make_gain(i, halves)
+            multiply(i, halves)
 
         def project_received(g, j0, tag):
             cols = slice(j0, j0 + B_COLS)
@@ -348,13 +373,15 @@ def tile_list_duplex_cancel_filter_kernel(
 
         x_tiles = []
         a_tiles = [project_page(0)]
-        if FILL[0] == 0:
-            gather_v1(None)
         for i in range(5):
             while len(a_tiles) < min(i + 1 + (AHEAD if i >= AFROM else 1), ROW_TILES):
                 a_tiles.append(project_page(len(a_tiles)))
             gather_x(i)
-            make_leak(i, slice(0, 2))
+            if i in XH:
+                make_leak(i, slice(0, 1))
+                make_leak(i, slice(1, 2))
+            else:
+                make_leak(i, slice(0, 2))
             if i + 1 == FILL[0]:
                 gather_v1(FTAG[0])
             if i + 1 == FILL[1]:
@@ -364,9 +391,15 @@ def tile_list_duplex_cancel_filter_kernel(
         for i in range(5, ROW_TILES):
             gather_x(i)
         make_leak(5, slice(0, 2))
-        for h in range(2):
-            for i in (6, 7):
-                make_leak(i, slice(h, h + 1))
+        halves = (slice(0, 1), slice(1, 2))
+        for i in (6, 7):
+            for cols in halves:
+                square(i, cols)
+            make_gain(i, halves[0])
+            multiply(i, halves[0])
+        for i in (6, 7):
+            make_gain(i, halves[1])
+            multiply(i, halves[1])
 
         first = CUTS[NF]
         resid_first = tile([P, PASSES * first * LANES], BF16, "resid_first", tag="wtx_bf1")

@@ -27,37 +27,15 @@ LINE = 4
 ROW_TILES = PASSES * LANES
 HALF = J // 2
 B_COLS = BANK // LANES
-Y_COLS = 256
-A_RING = 3
-PSUM_RING = 4
+A_BANKS = 3
+B_BANKS = 5
 ROW_RING = 6
-LEAK_RING = 3
-VECTOR_FIRST = 2
-VECTOR_BANK_TILE = 5
-GAIN = "GGGGGSSS"
-PROD = "GGGGGGGG"
-FTAG = ("wtx_bf1", "wtx_bf0")
-AHEAD = 1
-AFROM = 0
-XS0 = 256
-NFIRST = 1
+FIRST_XS = 256
+GPSIMD_COLS = 640
+SCALAR_GAINS_FROM = 5
+VECTOR_PRODUCT = 1
+VECTOR_BANKS_FROM = 5
 CUTS = (0, 256, 512, 768, 896, 1024)
-BT = 4
-NF = 1
-G_EARLY = 640
-V1FIRST = 0
-VLAST = 1
-XH = ()
-TAILP = ((5, 0, 2), (6, 0, 1), (7, 0, 1), (6, 1, 2), (7, 1, 2))
-PINI = 6
-VPROD = ()
-QAT = {512: (0, 256), 768: (512,), 1024: (768,)}
-PIN = "tab1"
-HALVES = (6, 7)
-VBANK = ((4, 0), (5, 0), (6, 0), (7, 0))
-FILL = (0, 2)
-SUB0_AFTER = 8
-G_COLS = 640
 
 
 def tile_list_duplex_cancel_filter_kernel(
@@ -68,13 +46,13 @@ def tile_list_duplex_cancel_filter_kernel(
     with ExitStack() as ctx:
         lists = ctx.enter_context(tc.tile_pool(name="lists", bufs=1))
         sb = ctx.enter_context(tc.tile_pool(name="sb", bufs=1))
-        psum = ctx.enter_context(tc.psum_pool(name="psum", bufs=PSUM_RING))
+        psum = ctx.enter_context(tc.psum_pool(name="psum", bufs=1))
 
         def tile(shape, dtype, name, tag=None, bufs=1):
             return sb.tile(shape, dtype, name=name, tag=tag or name, bufs=bufs, align_bytes=ALIGN)
 
         def bank(shape, tag):
-            return psum.tile(shape, F32, name=tag, tag=tag, bufs=A_RING if tag == "acc" else 8 - A_RING)
+            return psum.tile(shape, F32, name=tag, bufs=A_BANKS if tag == "a_ring" else B_BANKS)
 
         def zeroed_plane(width, name):
             plane = tile([P, width], U8, name)
@@ -99,6 +77,9 @@ def tile_list_duplex_cancel_filter_kernel(
                         in_=rows[first : first + 4, :].bitcast(I32),
                     )
 
+        def entries(offsets, lo, hi):
+            return offsets[:, lo // 16 : hi // 16]
+
         idx = lists.tile([P, J // 16], U16, name="idx")
         idx2 = lists.tile([P, S // 16], U16, name="idx2")
         idx3 = lists.tile([P, J // 16], U16, name="idx3")
@@ -111,12 +92,10 @@ def tile_list_duplex_cancel_filter_kernel(
         base_lanes = base.rearrange("(p t) c -> p t c", t=LANES)
         xs_lanes = xs.rearrange("(p t) c -> p t c", t=LANES)
         page = [tile([P, T2], F32, f"page{t}", tag="row", bufs=ROW_RING) for t in range(LANES)]
-        xs_pieces = [(0, 0, XS0), (0, XS0, S), (1, 0, S), (2, 0, S // 2), (2, S // 2, S), (3, 0, S)]
+        xs_pieces = [(0, 0, FIRST_XS), (0, FIRST_XS, S), (1, 0, S)]
+        xs_pieces = xs_pieces + [(2, 0, S // 2), (2, S // 2, S), (3, 0, S)]
         xs_tiles = [tile([P, hi - lo], F32, f"xs{t}_{lo}") for t, lo, hi in xs_pieces]
-        wtx_raw = [
-            tile([P, LANES, BANK], F32, f"wtx_raw{g}", tag="wide" if g == 0 else None)
-            for g in range(PASSES)
-        ]
+        wtx_raw = [tile([P, LANES, BANK], F32, f"wtx_raw{g}") for g in range(PASSES)]
         wrx_raw = tile([P, PASSES, 2 * H], U8, "wrx_raw")
 
         def load_wtx(g):
@@ -150,7 +129,7 @@ def tile_list_duplex_cancel_filter_kernel(
         )
 
         tab = [tile([P, T], U32, f"tab{a}") for a in range(PASSES)]
-        for a in (1, 0) if V1FIRST else (0, 1):
+        for a in range(PASSES):
             nc.sync.dma_start(
                 out=tab[a][:].bitcast(I32),
                 in_=tab_words[a].rearrange("p n i -> p (n i)").bitcast(I32),
@@ -189,11 +168,11 @@ def tile_list_duplex_cancel_filter_kernel(
             in_=wrx_from.rearrange("p (h m t) -> p h t m", t=LANES, m=P),
         )
 
-        page_bf = tile([P, T2, LANES], BF16, "page_bf", tag="wide")
+        page_bf = tile([P, T2, LANES], BF16, "page_bf", tag="wtx_raw0")
+        split = T2 - GPSIMD_COLS
         for (t, lo, hi), xs_tile in zip(xs_pieces, xs_tiles):
-            nc.vector.tensor_copy(page[t][:].indirect(idx2[:, lo // 16 : hi // 16]), xs_tile[:])
+            nc.vector.tensor_copy(page[t][:].indirect(entries(idx2, lo, hi)), xs_tile[:])
             if hi == S:
-                split = T2 - (G_EARLY if t < 2 else G_COLS)
                 step = BANK if t == LANES - 1 else split
                 for c0 in range(0, split, step):
                     c1 = min(c0 + step, split)
@@ -202,112 +181,97 @@ def tile_list_duplex_cancel_filter_kernel(
                     page_bf[:, split:, t], page[t][:, split:], 1.0, 0.0, ALU.mult, ALU.add
                 )
 
-        v1 = [tile([P, HALF], U32, "v1_0")]
-        if V1FIRST:
-            nc.vector.tensor_copy(v1[0][:], tab[1][:].indirect(idx[:, : HALF // 16]))
         v0 = tile([P, J], U32, "v0")
         nc.vector.tensor_copy(v0[:], tab[0][:].indirect(idx[:]))
-        codes_wp = tile([P, T2 + H], U32, "codes_wp", tag="tab0")
-        page_codes = codes_wp[:, :T2]
-        wtx_codes = [codes_wp[:, T2 + BANK * g : T2 + BANK * (g + 1)] for g in range(PASSES)]
+        codes = tile([P, T2 + H], U32, "codes", tag="tab0")
+        page_codes, wtx_codes = codes[:, :T2], codes[:, T2:]
         wtx_plane = [tile([P, BANK], U8, f"wtx_plane{g}") for g in range(PASSES)]
         page_plane = tile([P, T2], U8, "page_plane")
 
         def quantise_wtx(g, lo, hi):
             nc.vector.quantize_mx(
-                out=wtx_codes[g][:, lo:hi].bitcast(FP8X4),
+                out=wtx_codes[:, BANK * g + lo : BANK * g + hi].bitcast(FP8X4),
                 scales=wtx_plane[g][:, lo:hi],
                 in_=wtx_bf[g][:, LANES * lo : LANES * hi],
             )
 
-        quantise_wtx(0, 0, P)
-        page_pieces = [slice(c0, c0 + BANK) for c0 in (T2 - BANK, *range(0, T2 - BANK, BANK))]
-        for cols in page_pieces:
-            if cols == page_pieces[-1]:
-                quantise_wtx(1, 0, BANK)
+        def quantise_page(cols):
             nc.vector.quantize_mx(
                 out=page_codes[:, cols].bitcast(FP8X4),
                 scales=page_plane[:, cols],
                 in_=page_bf[:, cols, :].rearrange("p c t -> p (c t)"),
             )
+
+        def gather_v1(half, tag):
+            words = tile([P, HALF], U32, f"v1_{half}", tag=tag)
+            lo = HALF * half
+            nc.vector.tensor_copy(words[:], tab[1][:].indirect(entries(idx, lo, lo + HALF)))
+            return words
+
+        page_pieces = [slice(c0, c0 + BANK) for c0 in (T2 - BANK, *range(0, T2 - BANK, BANK))]
+        quantise_wtx(0, 0, P)
+        for cols in page_pieces[:-1]:
+            quantise_page(cols)
+        quantise_wtx(1, 0, BANK)
+        quantise_page(page_pieces[-1])
         quantise_wtx(0, P, 2 * P)
         quantise_wtx(0, 2 * P, BANK)
-        if not V1FIRST:
-            nc.vector.tensor_copy(v1[0][:], tab[1][:].indirect(idx[:, : HALF // 16]))
-
-        def gather_v1(tag):
-            half = len(v1)
-            words = tile([P, HALF], U32, f"v1_{half}", tag=tag)
-            lo = HALF * half // 16
-            nc.vector.tensor_copy(words[:], tab[1][:].indirect(idx[:, lo : lo + HALF // 16]))
-            v1.append(words)
+        v1 = [gather_v1(0, None)]
 
         leak = [tile([P, 2, LANES, HALF], F32, f"leak{g}") for g in range(PASSES)]
         out_rows = out.rearrange("(n p) j -> p n j", p=P)
+        held_tags = {1: "wtx_bf0", ROW_TILES - 2: "wtx_bf1", ROW_TILES - 1: "tab1"}
+        x_tags = ("xs3_0", "xs1_0", "wrx_raw", "wtx_raw1")
 
         def project_page(i):
-            if i in (1, PINI, 7):
-                a_rows = tile([P, T2], F32, f"a{i}", tag={1: "wtx_bf0", PINI: "wtx_bf1", 7: "tab1"}[i])
+            if i in held_tags:
+                a_rows = tile([P, T2], F32, f"a{i}", tag=held_tags[i])
             else:
                 a_rows = tile([P, T2], F32, f"a{i}", tag="row", bufs=ROW_RING)
             g, t = divmod(i, LANES)
-            rows = slice(P * t, P * (t + 1))
-            for q, cols in enumerate(page_pieces):
-                acc = bank([P, BANK], "b" if i < BT and q >= A_RING else "acc")
+            for place, cols in enumerate(page_pieces):
+                acc = bank([P, BANK], "b_ring" if i < LANES and place >= A_BANKS else "a_ring")
                 nc.tensor.matmul_mx(
                     out=acc[:],
-                    lhsT=wtx_codes[g][:, rows].bitcast(FP8X4), lhsT_scale=wtx_plane[g][:, rows],
+                    lhsT=wtx_codes[:, P * i : P * (i + 1)].bitcast(FP8X4),
+                    lhsT_scale=wtx_plane[g][:, P * t : P * (t + 1)],
                     rhs=page_codes[:, cols].bitcast(FP8X4), rhs_scale=page_plane[:, cols],
                     start=True, stop=True,
                 )
-                if (i, q) in VBANK:
+                if i >= VECTOR_BANKS_FROM and place == 0:
                     nc.vector.tensor_copy(out=a_rows[:, cols], in_=acc[:])
                 else:
                     nc.scalar.copy(out=a_rows[:, cols], in_=acc[:])
             return a_rows
 
         def gather_x(i):
-            x = tile([P, J], F32, f"x{i}", tag=("xs3_0", "xs1_0", "wrx_raw", "x")[i % 4])
-            if i in XH:
-                for h in range(2):
-                    lo = HALF * h
-                    nc.vector.tensor_copy(
-                        x[:, lo : lo + HALF], a_tiles[i][:].indirect(idx3[:, lo // 16 : (lo + HALF) // 16])
-                    )
-            else:
-                nc.vector.tensor_copy(x[:], a_tiles[i][:].indirect(idx3[:]))
-            x_tiles.append(x)
+            x = tile([P, J], F32, f"x{i}", tag=x_tags[i] if i < len(x_tags) else None)
+            nc.vector.tensor_copy(x[:], a_tiles[i][:].indirect(idx3[:]))
+            return x
 
-        def operands(i, halves):
+        def leak_operands(i, halves):
             g, t = divmod(i, LANES)
             x = x_tiles[i][:].rearrange("p (h j) -> p h j", j=HALF)[:, halves, :]
             return x, leak[g][:, halves, t, :]
 
         def square(i, halves):
-            x, y = operands(i, halves)
+            x, y = leak_operands(i, halves)
             nc.scalar.activation(out=y, in_=x, func=ACT.Square)
 
-        def make_gain(i, halves):
-            x, y = operands(i, halves)
-            cub_col = cub_cols[:, i // LANES, i % LANES : i % LANES + 1]
-            if GAIN[i] == "S":
+        def gain_and_product(i, halves):
+            x, y = leak_operands(i, halves)
+            g, t = divmod(i, LANES)
+            cub_col = cub_cols[:, g, t : t + 1]
+            if i >= SCALAR_GAINS_FROM:
                 nc.scalar.activation(out=y, in_=y, func=ACT.Identity, scale=cub_col, bias=1.0)
             else:
                 nc.gpsimd.tensor_scalar(y, y, cub_col, 1.0, ALU.mult, ALU.add)
-
-        def multiply(i, halves):
-            x, y = operands(i, halves)
-            engine = nc.vector if (i, halves.start) in VPROD else nc.gpsimd
+            engine = nc.vector if i == VECTOR_PRODUCT else nc.gpsimd
             engine.tensor_tensor(y, y, x, ALU.mult)
 
-        def make_leak(i, halves):
-            square(i, halves)
-            make_gain(i, halves)
-            multiply(i, halves)
-
-        def project_received(g, j0, tag):
+        def project_received(g, j0):
             cols = slice(j0, j0 + B_COLS)
-            b = bank([P, LANES, B_COLS], tag)
+            b = bank([P, LANES, B_COLS], "b_ring" if j0 < B_COLS * B_BANKS else "a_ring")
             words = (v0[:, cols], v1[j0 // HALF][:, j0 % HALF : j0 % HALF + B_COLS])
             for t in range(LANES):
                 r0 = P * (LANES * g + t)
@@ -321,20 +285,29 @@ def tile_list_duplex_cancel_filter_kernel(
                     )
             return b
 
-        def subtract(g, j0, resid, b):
+        def subtract(g, j0, resid_cols, b):
+            half, lo = divmod(j0, HALF)
             nc.vector.tensor_tensor(
-                resid.rearrange("p (c i) t -> p c t i", i=LINE),
+                resid_cols.rearrange("p (c i) t -> p c t i", i=LINE),
                 b[:].rearrange("p t (c i) -> p c t i", i=LINE),
-                leak[g][:, j0 // HALF, :, j0 % HALF : j0 % HALF + B_COLS].rearrange("p t (c i) -> p c t i", i=LINE),
+                leak[g][:, half, :, lo : lo + B_COLS].rearrange("p t (c i) -> p c t i", i=LINE),
                 ALU.subtract,
             )
 
-        def filter_and_store(cols, codes, plane):
-            last = cols.stop == J
+        def filter_and_store(piece):
+            cols = slice(CUTS[piece], CUTS[piece + 1])
             width = cols.stop - cols.start
-            staged = tile([P, N // P, width], F32, f"staged{cols.start}")
+            last = cols.stop == J
+            resid_codes = tile([P, PASSES, width], U32, f"resid_codes{piece}")
+            resid_plane = tile([P, PASSES, width], U8, f"resid_plane{piece}")
+            nc.vector.quantize_mx(
+                out=resid_codes[:].rearrange("p g c -> p (g c)").bitcast(FP8X4),
+                scales=resid_plane[:].rearrange("p g c -> p (g c)"),
+                in_=resid[piece].rearrange("p g c t -> p (g c t)"),
+            )
+            staged = tile([P, N // P, width], F32, f"staged{piece}")
             for group in ((0,), (1,), (2,)) if last else ((0, 1), (2,)):
-                y = bank([P, len(group), width], "b")
+                y = bank([P, len(group), width], "b_ring")
                 for place, n in enumerate(group):
                     rows = slice(P * n, P * (n + 1))
                     for g in range(PASSES):
@@ -342,8 +315,8 @@ def tile_list_duplex_cancel_filter_kernel(
                             out=y[:, place, :],
                             lhsT=wdem[:, g, rows].bitcast(FP8X4),
                             lhsT_scale=wdem_planes[4 * g : P, rows],
-                            rhs=codes[:, g, :].bitcast(FP8X4),
-                            rhs_scale=plane[:, g, :],
+                            rhs=resid_codes[:, g, :].bitcast(FP8X4),
+                            rhs_scale=resid_plane[:, g, :],
                             start=(g == 0), stop=(g == PASSES - 1),
                         )
                 for place, n in enumerate(group):
@@ -360,67 +333,48 @@ def tile_list_duplex_cancel_filter_kernel(
             if not last:
                 nc.sync.dma_start(out=out_rows[:, :, cols], in_=staged[:])
 
-        def finish(c):
-            width = CUTS[c + 1] - CUTS[c]
-            codes = tile([P, PASSES, width], U32, f"codes{c}")
-            plane = tile([P, PASSES, width], U8, f"plane{c}")
-            nc.vector.quantize_mx(
-                out=codes[:].rearrange("p g c -> p (g c)").bitcast(FP8X4),
-                scales=plane[:].rearrange("p g c -> p (g c)"),
-                in_=resid[c].rearrange("p g c t -> p (g c t)"),
-            )
-            filter_and_store(slice(CUTS[c], CUTS[c + 1]), codes, plane)
+        both, halves = slice(0, 2), (slice(0, 1), slice(1, 2))
+        a_tiles, x_tiles = [project_page(0)], []
+        for i in range(SCALAR_GAINS_FROM):
+            a_tiles.append(project_page(i + 1))
+            x_tiles.append(gather_x(i))
+            square(i, both)
+            gain_and_product(i, both)
+            if i == 1:
+                v1.append(gather_v1(1, held_tags[1]))
 
-        x_tiles = []
-        a_tiles = [project_page(0)]
-        for i in range(5):
-            while len(a_tiles) < min(i + 1 + (AHEAD if i >= AFROM else 1), ROW_TILES):
-                a_tiles.append(project_page(len(a_tiles)))
-            gather_x(i)
-            if i in XH:
-                make_leak(i, slice(0, 1))
-                make_leak(i, slice(1, 2))
-            else:
-                make_leak(i, slice(0, 2))
-            if i + 1 == FILL[0]:
-                gather_v1(FTAG[0])
-            if i + 1 == FILL[1]:
-                gather_v1(FTAG[1])
-        while len(a_tiles) < ROW_TILES:
-            a_tiles.append(project_page(len(a_tiles)))
-        for i in range(5, ROW_TILES):
-            gather_x(i)
-        make_leak(5, slice(0, 2))
-        halves = (slice(0, 1), slice(1, 2))
-        for i in (6, 7):
-            for cols in halves:
-                square(i, cols)
-            make_gain(i, halves[0])
-            multiply(i, halves[0])
-        for i in (6, 7):
-            make_gain(i, halves[1])
-            multiply(i, halves[1])
+        for i in range(SCALAR_GAINS_FROM + 1, ROW_TILES):
+            a_tiles.append(project_page(i))
+        for i in range(SCALAR_GAINS_FROM, ROW_TILES):
+            x_tiles.append(gather_x(i))
+        for i in range(SCALAR_GAINS_FROM, ROW_TILES - 2):
+            square(i, both)
+            gain_and_product(i, both)
+        for i in range(ROW_TILES - 2, ROW_TILES):
+            square(i, halves[0])
+            square(i, halves[1])
+            gain_and_product(i, halves[0])
+        for i in range(ROW_TILES - 2, ROW_TILES):
+            gain_and_product(i, halves[1])
 
-        first = CUTS[NF]
-        resid_first = tile([P, PASSES * first * LANES], BF16, "resid_first", tag="wtx_bf1")
-        resid_rest = tile([P, PASSES * (J - first) * LANES], BF16, "resid_rest", tag=PIN)
-        resid = [
-            resid_first[:, PASSES * LANES * lo : PASSES * LANES * hi]
-            if lo < first
-            else resid_rest[:, PASSES * LANES * (lo - first) : PASSES * LANES * (hi - first)]
-            for lo, hi in zip(CUTS, CUTS[1:])
+        values = PASSES * LANES
+        first = CUTS[1]
+        resid_first = tile([P, values * first], BF16, "resid_first", tag=held_tags[ROW_TILES - 2])
+        resid_rest = tile(
+            [P, values * (J - first)], BF16, "resid_rest", tag=held_tags[ROW_TILES - 1]
+        )
+        resid = [resid_first[:]] + [
+            resid_rest[:, values * (lo - first) : values * (hi - first)]
+            for lo, hi in zip(CUTS[1:], CUTS[2:])
         ]
         resid = [r.rearrange("p (g c t) -> p g c t", g=PASSES, t=LANES) for r in resid]
         for g in range(PASSES):
-            banks = [
-                project_received(g, j0, "b" if j0 < B_COLS * (8 - A_RING) else "acc")
-                for j0 in range(0, J, B_COLS)
-            ]
-            for c in range(len(CUTS) - 1):
-                for j0 in range(CUTS[c], CUTS[c + 1], B_COLS):
-                    lo = j0 - CUTS[c]
-                    subtract(g, j0, resid[c][:, g, lo : lo + B_COLS, :], banks[j0 // B_COLS])
-                if g == 1 and c == 1:
-                    finish(0)
-                if g == 1 and c >= 1:
-                    finish(c)
+            b_banks = [project_received(g, j0) for j0 in range(0, J, B_COLS)]
+            for piece in range(len(resid)):
+                for j0 in range(CUTS[piece], CUTS[piece + 1], B_COLS):
+                    lo = j0 - CUTS[piece]
+                    subtract(g, j0, resid[piece][:, g, lo : lo + B_COLS, :], b_banks[j0 // B_COLS])
+                if g == PASSES - 1 and piece == 1:
+                    filter_and_store(0)
+                if g == PASSES - 1 and piece >= 1:
+                    filter_and_store(piece)

@@ -31,11 +31,10 @@ A_BANKS = 3
 B_BANKS = 5
 ROW_RING = 6
 FIRST_XS = 256
-GPSIMD_COLS = 640
+GPSIMD_COLS = (384, 640)
 SCALAR_GAINS_FROM = 5
-VECTOR_PRODUCT = 1
-VECTOR_BANKS_FROM = 5
-CUTS = (0, 256, 512, 768, 896, 1024)
+VECTOR_BANKS_FROM = 4
+CUTS = (0, 256, 512, 768, 1024)
 
 
 def tile_list_duplex_cancel_filter_kernel(
@@ -86,14 +85,20 @@ def tile_list_duplex_cancel_filter_kernel(
 
         nc.sync.dma_start(idx[:], offs)
         tab_rows = load_scale_rows(tab_scales, "tab_rows", nc.vector)
+        wrx_rows_raw = load_scale_rows(wrx_scales, "wrx_rows_raw", nc.gpsimd)
         v_rows = tile([P, J], U8, "v_rows")
         nc.vector.tensor_copy(v_rows[:], tab_rows[:].indirect(idx[:]))
+        wrx_rows = tile([P, H], U8, "wrx_rows")
+        nc.gpsimd.tensor_copy(
+            out=wrx_rows[:].rearrange("p (g t m) -> p g t m", t=LANES, m=P),
+            in_=wrx_rows_raw[:].rearrange("p (g m t) -> p g t m", t=LANES, m=P),
+        )
 
         base_lanes = base.rearrange("(p t) c -> p t c", t=LANES)
         xs_lanes = xs.rearrange("(p t) c -> p t c", t=LANES)
         page = [tile([P, T2], F32, f"page{t}", tag="row", bufs=ROW_RING) for t in range(LANES)]
-        xs_pieces = [(0, 0, FIRST_XS), (0, FIRST_XS, S), (1, 0, S)]
-        xs_pieces = xs_pieces + [(2, 0, S // 2), (2, S // 2, S), (3, 0, S)]
+        xs_pieces = [(0, 0, FIRST_XS), (0, FIRST_XS, S)]
+        xs_pieces = xs_pieces + [(t, 0, S) for t in range(1, LANES)]
         xs_tiles = [tile([P, hi - lo], F32, f"xs{t}_{lo}") for t, lo, hi in xs_pieces]
         wtx_raw = [tile([P, LANES, BANK], F32, f"wtx_raw{g}") for g in range(PASSES)]
         wrx_raw = tile([P, PASSES, 2 * H], U8, "wrx_raw")
@@ -109,24 +114,14 @@ def tile_list_duplex_cancel_filter_kernel(
             if lo == 0:
                 nc.sync.dma_start(out=page[t][:], in_=base_lanes[:, t, :])
             nc.sync.dma_start(out=xs_tile[:], in_=xs_lanes[:, t, lo:hi])
-            if t == 0 and hi == S:
-                wrx_rows_raw = load_scale_rows(wrx_scales, "wrx_rows_raw", nc.gpsimd)
-            if t == 1:
-                load_wtx(0)
-                nc.sync.dma_start(
-                    out=wrx_raw[:].bitcast(I32),
-                    in_=wrx_words.rearrange("a p c -> p a c").bitcast(I32),
-                )
-            if t == 2 and lo == 0:
-                load_wtx(1)
+            if t < PASSES and hi == S:
+                load_wtx(t)
+        nc.sync.dma_start(
+            out=wrx_raw[:].bitcast(I32), in_=wrx_words.rearrange("a p c -> p a c").bitcast(I32)
+        )
         wdem_planes = zeroed_plane(N, "wdem_planes")
         v_plane = [zeroed_plane(J, f"v_plane{a}") for a in range(PASSES)]
         wrx_plane = [zeroed_plane(H, f"wrx_plane{a}") for a in range(PASSES)]
-        wrx_rows = tile([P, H], U8, "wrx_rows")
-        nc.gpsimd.tensor_copy(
-            out=wrx_rows[:].rearrange("p (g t m) -> p g t m", t=LANES, m=P),
-            in_=wrx_rows_raw[:].rearrange("p (g m t) -> p g t m", t=LANES, m=P),
-        )
 
         tab = [tile([P, T], U32, f"tab{a}") for a in range(PASSES)]
         for a in range(PASSES):
@@ -160,19 +155,11 @@ def tile_list_duplex_cancel_filter_kernel(
                 func=ACT.Identity,
             )
 
-        wrx = tile([P, PASSES, 2 * H], U8, "wrx")
-        wrx_to = wrx[:].rearrange("p a c -> p (a c)").bitcast(U16)
-        wrx_from = wrx_raw[:].rearrange("p a c -> p (a c)").bitcast(U16)
-        nc.gpsimd.tensor_copy(
-            out=wrx_to.rearrange("p (h t m) -> p h t m", t=LANES, m=P),
-            in_=wrx_from.rearrange("p (h m t) -> p h t m", t=LANES, m=P),
-        )
-
         page_bf = tile([P, T2, LANES], BF16, "page_bf", tag="wtx_raw0")
-        split = T2 - GPSIMD_COLS
         for (t, lo, hi), xs_tile in zip(xs_pieces, xs_tiles):
             nc.vector.tensor_copy(page[t][:].indirect(entries(idx2, lo, hi)), xs_tile[:])
             if hi == S:
+                split = T2 - GPSIMD_COLS[t // 2]
                 step = BANK if t == LANES - 1 else split
                 for c0 in range(0, split, step):
                     c1 = min(c0 + step, split)
@@ -218,9 +205,17 @@ def tile_list_duplex_cancel_filter_kernel(
         quantise_wtx(0, 2 * P, BANK)
         v1 = [gather_v1(0, None)]
 
+        wrx = tile([P, PASSES, 2 * H], U8, "wrx", tag="wtx_bf0")
+        wrx_to = wrx[:].rearrange("p a c -> p (a c)").bitcast(U16)
+        wrx_from = wrx_raw[:].rearrange("p a c -> p (a c)").bitcast(U16)
+        nc.gpsimd.tensor_copy(
+            out=wrx_to.rearrange("p (h t m) -> p h t m", t=LANES, m=P),
+            in_=wrx_from.rearrange("p (h m t) -> p h t m", t=LANES, m=P),
+        )
+
         leak = [tile([P, 2, LANES, HALF], F32, f"leak{g}") for g in range(PASSES)]
         out_rows = out.rearrange("(n p) j -> p n j", p=P)
-        held_tags = {1: "wtx_bf0", ROW_TILES - 2: "wtx_bf1", ROW_TILES - 1: "tab1"}
+        held_tags = {1: "a1", ROW_TILES - 2: "wtx_bf1", ROW_TILES - 1: "tab1"}
         x_tags = ("xs3_0", "xs1_0", "wrx_raw", "wtx_raw1")
 
         def project_page(i):
@@ -266,8 +261,7 @@ def tile_list_duplex_cancel_filter_kernel(
                 nc.scalar.activation(out=y, in_=y, func=ACT.Identity, scale=cub_col, bias=1.0)
             else:
                 nc.gpsimd.tensor_scalar(y, y, cub_col, 1.0, ALU.mult, ALU.add)
-            engine = nc.vector if i == VECTOR_PRODUCT else nc.gpsimd
-            engine.tensor_tensor(y, y, x, ALU.mult)
+            nc.gpsimd.tensor_tensor(y, y, x, ALU.mult)
 
         def project_received(g, j0):
             cols = slice(j0, j0 + B_COLS)

@@ -31,10 +31,11 @@ A_BANKS = 3
 B_BANKS = 5
 ROW_RING = 6
 FIRST_XS = 256
-GPSIMD_COLS = (384, 640)
+GPSIMD_COLS = (256, 640)
 SCALAR_GAINS_FROM = 5
 VECTOR_BANKS_FROM = 4
-CUTS = (0, 256, 512, 768, 1024)
+Y_COLS = 256
+PIECES = J // Y_COLS
 
 
 def tile_list_duplex_cancel_filter_kernel(
@@ -55,7 +56,7 @@ def tile_list_duplex_cancel_filter_kernel(
 
         def zeroed_plane(width, name):
             plane = tile([P, width], U8, name)
-            nc.gpsimd.memset(plane[:].bitcast(I32), 0)
+            nc.vector.memset(plane[:].bitcast(I32), 0)
             return plane
 
         def load_scale_rows(scales, name, engine):
@@ -288,20 +289,24 @@ def tile_list_duplex_cancel_filter_kernel(
                 ALU.subtract,
             )
 
-        def filter_and_store(piece):
-            cols = slice(CUTS[piece], CUTS[piece + 1])
-            width = cols.stop - cols.start
-            last = cols.stop == J
-            resid_codes = tile([P, PASSES, width], U32, f"resid_codes{piece}")
-            resid_plane = tile([P, PASSES, width], U8, f"resid_plane{piece}")
+        def quantise_resid(piece, passes, tag=None):
+            count = passes.stop - passes.start
+            name = f"{piece}_{passes.start}"
+            resid_codes = tile([P, count, Y_COLS], U32, f"resid_codes{name}", tag=tag)
+            resid_plane = tile([P, count, Y_COLS], U8, f"resid_plane{name}")
             nc.vector.quantize_mx(
                 out=resid_codes[:].rearrange("p g c -> p (g c)").bitcast(FP8X4),
                 scales=resid_plane[:].rearrange("p g c -> p (g c)"),
-                in_=resid[piece].rearrange("p g c t -> p (g c t)"),
+                in_=resid[piece][:, passes].rearrange("p g c t -> p (g c t)"),
             )
-            staged = tile([P, N // P, width], F32, f"staged{piece}")
+            return [(resid_codes[:, g, :], resid_plane[:, g, :]) for g in range(count)]
+
+        def filter_and_store(piece, operands):
+            cols = slice(Y_COLS * piece, Y_COLS * (piece + 1))
+            last = piece == PIECES - 1
+            staged = tile([P, N // P, Y_COLS], F32, f"staged{piece}")
             for group in ((0,), (1,), (2,)) if last else ((0, 1), (2,)):
-                y = bank([P, len(group), width], "b_ring")
+                y = bank([P, len(group), Y_COLS], "b_ring")
                 for place, n in enumerate(group):
                     rows = slice(P * n, P * (n + 1))
                     for g in range(PASSES):
@@ -309,8 +314,7 @@ def tile_list_duplex_cancel_filter_kernel(
                             out=y[:, place, :],
                             lhsT=wdem[:, g, rows].bitcast(FP8X4),
                             lhsT_scale=wdem_planes[4 * g : P, rows],
-                            rhs=resid_codes[:, g, :].bitcast(FP8X4),
-                            rhs_scale=resid_plane[:, g, :],
+                            rhs=operands[g][0].bitcast(FP8X4), rhs_scale=operands[g][1],
                             start=(g == 0), stop=(g == PASSES - 1),
                         )
                 for place, n in enumerate(group):
@@ -327,13 +331,13 @@ def tile_list_duplex_cancel_filter_kernel(
             if not last:
                 nc.sync.dma_start(out=out_rows[:, :, cols], in_=staged[:])
 
-        both, halves = slice(0, 2), (slice(0, 1), slice(1, 2))
+        both_halves, halves = slice(0, 2), (slice(0, 1), slice(1, 2))
         a_tiles, x_tiles = [project_page(0)], []
         for i in range(SCALAR_GAINS_FROM):
             a_tiles.append(project_page(i + 1))
             x_tiles.append(gather_x(i))
-            square(i, both)
-            gain_and_product(i, both)
+            square(i, both_halves)
+            gain_and_product(i, both_halves)
             if i == 1:
                 v1.append(gather_v1(1, held_tags[1]))
 
@@ -342,8 +346,8 @@ def tile_list_duplex_cancel_filter_kernel(
         for i in range(SCALAR_GAINS_FROM, ROW_TILES):
             x_tiles.append(gather_x(i))
         for i in range(SCALAR_GAINS_FROM, ROW_TILES - 2):
-            square(i, both)
-            gain_and_product(i, both)
+            square(i, both_halves)
+            gain_and_product(i, both_halves)
         for i in range(ROW_TILES - 2, ROW_TILES):
             square(i, halves[0])
             square(i, halves[1])
@@ -351,24 +355,28 @@ def tile_list_duplex_cancel_filter_kernel(
         for i in range(ROW_TILES - 2, ROW_TILES):
             gain_and_product(i, halves[1])
 
-        values = PASSES * LANES
-        first = CUTS[1]
-        resid_first = tile([P, values * first], BF16, "resid_first", tag=held_tags[ROW_TILES - 2])
-        resid_rest = tile(
-            [P, values * (J - first)], BF16, "resid_rest", tag=held_tags[ROW_TILES - 1]
+        resid_first = tile(
+            [P, PASSES, Y_COLS, LANES], BF16, "resid_first", tag=held_tags[ROW_TILES - 2]
         )
-        resid = [resid_first[:]] + [
-            resid_rest[:, values * (lo - first) : values * (hi - first)]
-            for lo, hi in zip(CUTS[1:], CUTS[2:])
-        ]
-        resid = [r.rearrange("p (g c t) -> p g c t", g=PASSES, t=LANES) for r in resid]
+        resid_rest = tile(
+            [P, PIECES - 1, PASSES, Y_COLS, LANES], BF16, "resid_rest", tag=held_tags[ROW_TILES - 1]
+        )
+        resid = [resid_first[:]] + [resid_rest[:, piece] for piece in range(PIECES - 1)]
+        both_passes, first_pass, second_pass = slice(0, 2), slice(0, 1), slice(1, 2)
+        last_piece = PIECES - 1
         for g in range(PASSES):
             b_banks = [project_received(g, j0) for j0 in range(0, J, B_COLS)]
-            for piece in range(len(resid)):
-                for j0 in range(CUTS[piece], CUTS[piece + 1], B_COLS):
-                    lo = j0 - CUTS[piece]
+            for piece in range(PIECES):
+                for lo in range(0, Y_COLS, B_COLS):
+                    j0 = Y_COLS * piece + lo
                     subtract(g, j0, resid[piece][:, g, lo : lo + B_COLS, :], b_banks[j0 // B_COLS])
-                if g == PASSES - 1 and piece == 1:
-                    filter_and_store(0)
-                if g == PASSES - 1 and piece >= 1:
-                    filter_and_store(piece)
+                if g == 0 or piece == 0:
+                    continue
+                if piece == 1:
+                    filter_and_store(0, quantise_resid(0, both_passes))
+                if piece < last_piece:
+                    filter_and_store(piece, quantise_resid(piece, both_passes))
+                else:
+                    filter_and_store(piece, last_first_pass + quantise_resid(piece, second_pass))
+                if piece == last_piece - 1:
+                    last_first_pass = quantise_resid(last_piece, first_pass, f"x{ROW_TILES - 1}")

@@ -27,13 +27,11 @@ LINE = 4
 ROW_TILES = PASSES * LANES
 HALF = J // 2
 B_COLS = BANK // LANES
-A_BANKS = 3
-B_BANKS = 5
-ROW_RING = 6
+RING = 4
+ROW_RING = 4
 FIRST_XS = 256
-GPSIMD_COLS = (256, 640)
+GPSIMD_COLS = (256, 768)
 SCALAR_GAINS_FROM = 5
-VECTOR_BANKS_FROM = 4
 Y_COLS = 256
 PIECES = J // Y_COLS
 
@@ -52,7 +50,7 @@ def tile_list_duplex_cancel_filter_kernel(
             return sb.tile(shape, dtype, name=name, tag=tag or name, bufs=bufs, align_bytes=ALIGN)
 
         def bank(shape, tag):
-            return psum.tile(shape, F32, name=tag, bufs=A_BANKS if tag == "a_ring" else B_BANKS)
+            return psum.tile(shape, F32, name=tag, bufs=RING)
 
         def zeroed_plane(width, name):
             plane = tile([P, width], U8, name)
@@ -117,9 +115,11 @@ def tile_list_duplex_cancel_filter_kernel(
             nc.sync.dma_start(out=xs_tile[:], in_=xs_lanes[:, t, lo:hi])
             if t < PASSES and hi == S:
                 load_wtx(t)
-        nc.sync.dma_start(
-            out=wrx_raw[:].bitcast(I32), in_=wrx_words.rearrange("a p c -> p a c").bitcast(I32)
-        )
+            if t == 1:
+                nc.sync.dma_start(
+                    out=wrx_raw[:].bitcast(I32),
+                    in_=wrx_words.rearrange("a p c -> p a c").bitcast(I32),
+                )
         wdem_planes = zeroed_plane(N, "wdem_planes")
         v_plane = [zeroed_plane(J, f"v_plane{a}") for a in range(PASSES)]
         wrx_plane = [zeroed_plane(H, f"wrx_plane{a}") for a in range(PASSES)]
@@ -155,6 +155,14 @@ def tile_list_duplex_cancel_filter_kernel(
                 in_=wtx_raw[g][:].rearrange("p i (m t) -> p m i t", t=LANES),
                 func=ACT.Identity,
             )
+
+        wrx = tile([P, PASSES, 2 * H], U8, "wrx")
+        wrx_to = wrx[:].rearrange("p a c -> p (a c)").bitcast(U16)
+        wrx_from = wrx_raw[:].rearrange("p a c -> p (a c)").bitcast(U16)
+        nc.gpsimd.tensor_copy(
+            out=wrx_to.rearrange("p (h t m) -> p h t m", t=LANES, m=P),
+            in_=wrx_from.rearrange("p (h m t) -> p h t m", t=LANES, m=P),
+        )
 
         page_bf = tile([P, T2, LANES], BF16, "page_bf", tag="wtx_raw0")
         for (t, lo, hi), xs_tile in zip(xs_pieces, xs_tiles):
@@ -198,25 +206,17 @@ def tile_list_duplex_cancel_filter_kernel(
 
         page_pieces = [slice(c0, c0 + BANK) for c0 in (T2 - BANK, *range(0, T2 - BANK, BANK))]
         quantise_wtx(0, 0, P)
-        for cols in page_pieces[:-1]:
+        for cols in page_pieces:
             quantise_page(cols)
-        quantise_wtx(1, 0, BANK)
-        quantise_page(page_pieces[-1])
         quantise_wtx(0, P, 2 * P)
         quantise_wtx(0, 2 * P, BANK)
-        v1 = [gather_v1(0, None)]
+        quantise_wtx(1, 0, BANK)
 
-        wrx = tile([P, PASSES, 2 * H], U8, "wrx", tag="wtx_bf0")
-        wrx_to = wrx[:].rearrange("p a c -> p (a c)").bitcast(U16)
-        wrx_from = wrx_raw[:].rearrange("p a c -> p (a c)").bitcast(U16)
-        nc.gpsimd.tensor_copy(
-            out=wrx_to.rearrange("p (h t m) -> p h t m", t=LANES, m=P),
-            in_=wrx_from.rearrange("p (h m t) -> p h t m", t=LANES, m=P),
-        )
-
-        leak = [tile([P, 2, LANES, HALF], F32, f"leak{g}") for g in range(PASSES)]
+        leak0 = tile([P, LANES, J], F32, "leak0")
+        leak1 = tile([P, 2, LANES, HALF], F32, "leak1")
+        gains = tile([P, LANES - 1, J], F32, "gains", tag="wtx_raw0")
         out_rows = out.rearrange("(n p) j -> p n j", p=P)
-        held_tags = {1: "a1", ROW_TILES - 2: "wtx_bf1", ROW_TILES - 1: "tab1"}
+        held_tags = {3: "a3", 4: "a4", ROW_TILES - 2: "wtx_bf0", ROW_TILES - 1: "tab1"}
         x_tags = ("xs3_0", "xs1_0", "wrx_raw", "wtx_raw1")
 
         def project_page(i):
@@ -226,7 +226,7 @@ def tile_list_duplex_cancel_filter_kernel(
                 a_rows = tile([P, T2], F32, f"a{i}", tag="row", bufs=ROW_RING)
             g, t = divmod(i, LANES)
             for place, cols in enumerate(page_pieces):
-                acc = bank([P, BANK], "b_ring" if i < LANES and place >= A_BANKS else "a_ring")
+                acc = bank([P, BANK], "even" if i in (0, 2, 4) else "odd")
                 nc.tensor.matmul_mx(
                     out=acc[:],
                     lhsT=wtx_codes[:, P * i : P * (i + 1)].bitcast(FP8X4),
@@ -234,39 +234,52 @@ def tile_list_duplex_cancel_filter_kernel(
                     rhs=page_codes[:, cols].bitcast(FP8X4), rhs_scale=page_plane[:, cols],
                     start=True, stop=True,
                 )
-                if i >= VECTOR_BANKS_FROM and place == 0:
-                    nc.vector.tensor_copy(out=a_rows[:, cols], in_=acc[:])
-                else:
-                    nc.scalar.copy(out=a_rows[:, cols], in_=acc[:])
+                nc.scalar.copy(out=a_rows[:, cols], in_=acc[:])
             return a_rows
 
         def gather_x(i):
             x = tile([P, J], F32, f"x{i}", tag=x_tags[i] if i < len(x_tags) else None)
-            nc.vector.tensor_copy(x[:], a_tiles[i][:].indirect(idx3[:]))
+            step = HALF if i == 0 else J
+            for lo in range(0, J, step):
+                nc.vector.tensor_copy(
+                    x[:, lo : lo + step], a_tiles[i][:].indirect(entries(idx3, lo, lo + step))
+                )
             return x
 
         def leak_operands(i, halves):
             g, t = divmod(i, LANES)
             x = x_tiles[i][:].rearrange("p (h j) -> p h j", j=HALF)[:, halves, :]
-            return x, leak[g][:, halves, t, :]
+            if g == 0:
+                y = leak0[:, t, :].rearrange("p (h j) -> p h j", j=HALF)[:, halves, :]
+                return x, y, y
+            z = leak1[:, halves, t, :]
+            if t == LANES - 1:
+                return x, z, z
+            return x, gains[:, t, :].rearrange("p (h j) -> p h j", j=HALF)[:, halves, :], z
 
         def square(i, halves):
-            x, y = leak_operands(i, halves)
-            nc.scalar.activation(out=y, in_=x, func=ACT.Square)
+            x, y, z = leak_operands(i, halves)
+            if i == 0:
+                nc.gpsimd.tensor_tensor(y, x, x, ALU.mult)
+            else:
+                nc.scalar.activation(out=y, in_=x, func=ACT.Square)
 
-        def gain_and_product(i, halves):
-            x, y = leak_operands(i, halves)
+        def gain(i, halves):
+            y = leak_operands(i, halves)[1]
             g, t = divmod(i, LANES)
             cub_col = cub_cols[:, g, t : t + 1]
             if i >= SCALAR_GAINS_FROM:
                 nc.scalar.activation(out=y, in_=y, func=ACT.Identity, scale=cub_col, bias=1.0)
             else:
                 nc.gpsimd.tensor_scalar(y, y, cub_col, 1.0, ALU.mult, ALU.add)
-            nc.gpsimd.tensor_tensor(y, y, x, ALU.mult)
 
-        def project_received(g, j0):
+        def product(i, halves):
+            x, y, z = leak_operands(i, halves)
+            nc.gpsimd.tensor_tensor(z, y, x, ALU.mult)
+
+        def project_received(g, j0, tag):
             cols = slice(j0, j0 + B_COLS)
-            b = bank([P, LANES, B_COLS], "b_ring" if j0 < B_COLS * B_BANKS else "a_ring")
+            b = bank([P, LANES, B_COLS], tag)
             words = (v0[:, cols], v1[j0 // HALF][:, j0 % HALF : j0 % HALF + B_COLS])
             for t in range(LANES):
                 r0 = P * (LANES * g + t)
@@ -282,10 +295,11 @@ def tile_list_duplex_cancel_filter_kernel(
 
         def subtract(g, j0, resid_cols, b):
             half, lo = divmod(j0, HALF)
+            leak = leak0[:, :, j0 : j0 + B_COLS] if g == 0 else leak1[:, half, :, lo : lo + B_COLS]
             nc.vector.tensor_tensor(
                 resid_cols.rearrange("p (c i) t -> p c t i", i=LINE),
                 b[:].rearrange("p t (c i) -> p c t i", i=LINE),
-                leak[g][:, half, :, lo : lo + B_COLS].rearrange("p t (c i) -> p c t i", i=LINE),
+                leak.rearrange("p t (c i) -> p c t i", i=LINE),
                 ALU.subtract,
             )
 
@@ -306,7 +320,7 @@ def tile_list_duplex_cancel_filter_kernel(
             last = piece == PIECES - 1
             staged = tile([P, N // P, Y_COLS], F32, f"staged{piece}")
             for group in ((0,), (1,), (2,)) if last else ((0, 1), (2,)):
-                y = bank([P, len(group), Y_COLS], "b_ring")
+                y = bank([P, len(group), Y_COLS], "even" if piece == 2 else "odd")
                 for place, n in enumerate(group):
                     rows = slice(P * n, P * (n + 1))
                     for g in range(PASSES):
@@ -332,51 +346,72 @@ def tile_list_duplex_cancel_filter_kernel(
                 nc.sync.dma_start(out=out_rows[:, :, cols], in_=staged[:])
 
         both_halves, halves = slice(0, 2), (slice(0, 1), slice(1, 2))
-        a_tiles, x_tiles = [project_page(0)], []
-        for i in range(SCALAR_GAINS_FROM):
-            a_tiles.append(project_page(i + 1))
-            x_tiles.append(gather_x(i))
-            square(i, both_halves)
-            gain_and_product(i, both_halves)
-            if i == 1:
-                v1.append(gather_v1(1, held_tags[1]))
+        a_tiles, x_tiles, v1 = [], [], []
 
-        for i in range(SCALAR_GAINS_FROM + 1, ROW_TILES):
+        def row_tile(i):
             a_tiles.append(project_page(i))
-        for i in range(SCALAR_GAINS_FROM, ROW_TILES):
             x_tiles.append(gather_x(i))
-        for i in range(SCALAR_GAINS_FROM, ROW_TILES - 2):
-            square(i, both_halves)
-            gain_and_product(i, both_halves)
-        for i in range(ROW_TILES - 2, ROW_TILES):
-            square(i, halves[0])
-            square(i, halves[1])
-            gain_and_product(i, halves[0])
-        for i in range(ROW_TILES - 2, ROW_TILES):
-            gain_and_product(i, halves[1])
 
-        resid_first = tile(
-            [P, PASSES, Y_COLS, LANES], BF16, "resid_first", tag=held_tags[ROW_TILES - 2]
-        )
-        resid_rest = tile(
-            [P, PIECES - 1, PASSES, Y_COLS, LANES], BF16, "resid_rest", tag=held_tags[ROW_TILES - 1]
-        )
-        resid = [resid_first[:]] + [resid_rest[:, piece] for piece in range(PIECES - 1)]
+        def leak_of(i):
+            square(i, both_halves)
+            gain(i, both_halves)
+            product(i, both_halves)
+
+        def received(g, half, tag):
+            return [project_received(g, HALF * half + B_COLS * k, tag) for k in range(RING)]
+
+        def subtract_banks(g, half, banks, first=0, count=RING):
+            for k in range(first, first + count):
+                j0 = HALF * half + B_COLS * k
+                piece, lo = divmod(j0, Y_COLS)
+                subtract(g, j0, resid[piece][:, g, lo : lo + B_COLS, :], banks[k])
+
+        row_tile(0)
+        square(0, halves[0])
+        square(0, halves[1])
+        gain(0, both_halves)
+        product(0, both_halves)
+        for i in range(1, 4):
+            row_tile(i)
+        leak_of(1)
+        v1.append(gather_v1(0, held_tags[3]))
+        row_tile(4)
+        leak_of(2)
+        leak_of(3)
+        v1.append(gather_v1(1, held_tags[4]))
+        row_tile(5)
+        row_tile(6)
+        leak_of(4)
+        row_tile(7)
+        b00 = received(0, 0, "even")
+        resid_first = tile([P, 2, PASSES, Y_COLS, LANES], BF16, "resid_first", tag=held_tags[7])
+        resid = [resid_first[:, 0], resid_first[:, 1]]
+        subtract_banks(0, 0, b00)
+        b01 = received(0, 1, "even")
+        square(5, both_halves)
+        gain(5, both_halves)
+        product(5, both_halves)
+        square(6, both_halves)
+        square(7, halves[0])
+        gain(6, halves[0])
+        gain(7, halves[0])
+        square(7, halves[1])
+        gain(6, halves[1])
+        gain(7, halves[1])
+        for half in halves:
+            product(6, half)
+            product(7, half)
+        resid_rest = tile([P, 2, PASSES, Y_COLS, LANES], BF16, "resid_rest", tag=held_tags[6])
+        resid = resid + [resid_rest[:, 0], resid_rest[:, 1]]
+        b10 = received(1, 0, "odd")
+        subtract_banks(0, 1, b01)
+        b11 = received(1, 1, "even")
+        subtract_banks(1, 0, b10)
         both_passes, first_pass, second_pass = slice(0, 2), slice(0, 1), slice(1, 2)
-        last_piece = PIECES - 1
-        for g in range(PASSES):
-            b_banks = [project_received(g, j0) for j0 in range(0, J, B_COLS)]
-            for piece in range(PIECES):
-                for lo in range(0, Y_COLS, B_COLS):
-                    j0 = Y_COLS * piece + lo
-                    subtract(g, j0, resid[piece][:, g, lo : lo + B_COLS, :], b_banks[j0 // B_COLS])
-                if g == 0 or piece == 0:
-                    continue
-                if piece == 1:
-                    filter_and_store(0, quantise_resid(0, both_passes))
-                if piece < last_piece:
-                    filter_and_store(piece, quantise_resid(piece, both_passes))
-                else:
-                    filter_and_store(piece, last_first_pass + quantise_resid(piece, second_pass))
-                if piece == last_piece - 1:
-                    last_first_pass = quantise_resid(last_piece, first_pass, f"x{ROW_TILES - 1}")
+        for piece in (0, 1):
+            filter_and_store(piece, quantise_resid(piece, both_passes))
+        subtract_banks(1, 1, b11, 0, 2)
+        last_first_pass = quantise_resid(3, first_pass, f"x{ROW_TILES - 1}")
+        filter_and_store(2, quantise_resid(2, both_passes))
+        subtract_banks(1, 1, b11, 2, 2)
+        filter_and_store(3, last_first_pass + quantise_resid(3, second_pass))

@@ -30,8 +30,8 @@ B_COLS = BANK // LANES
 RING = 4
 ROW_RING = 4
 FIRST_XS = 256
-GPSIMD_COLS = (256, 768)
-SCALAR_GAINS_FROM = 5
+GPSIMD_COLS = 768
+SCALAR_GAINS_FROM = 4
 Y_COLS = 256
 PIECES = J // Y_COLS
 
@@ -115,11 +115,9 @@ def tile_list_duplex_cancel_filter_kernel(
             nc.sync.dma_start(out=xs_tile[:], in_=xs_lanes[:, t, lo:hi])
             if t < PASSES and hi == S:
                 load_wtx(t)
-            if t == 1:
-                nc.sync.dma_start(
-                    out=wrx_raw[:].bitcast(I32),
-                    in_=wrx_words.rearrange("a p c -> p a c").bitcast(I32),
-                )
+        nc.sync.dma_start(
+            out=wrx_raw[:].bitcast(I32), in_=wrx_words.rearrange("a p c -> p a c").bitcast(I32)
+        )
         wdem_planes = zeroed_plane(N, "wdem_planes")
         v_plane = [zeroed_plane(J, f"v_plane{a}") for a in range(PASSES)]
         wrx_plane = [zeroed_plane(H, f"wrx_plane{a}") for a in range(PASSES)]
@@ -156,26 +154,19 @@ def tile_list_duplex_cancel_filter_kernel(
                 func=ACT.Identity,
             )
 
-        wrx = tile([P, PASSES, 2 * H], U8, "wrx")
-        wrx_to = wrx[:].rearrange("p a c -> p (a c)").bitcast(U16)
-        wrx_from = wrx_raw[:].rearrange("p a c -> p (a c)").bitcast(U16)
-        nc.gpsimd.tensor_copy(
-            out=wrx_to.rearrange("p (h t m) -> p h t m", t=LANES, m=P),
-            in_=wrx_from.rearrange("p (h m t) -> p h t m", t=LANES, m=P),
-        )
-
         page_bf = tile([P, T2, LANES], BF16, "page_bf", tag="wtx_raw0")
         for (t, lo, hi), xs_tile in zip(xs_pieces, xs_tiles):
             nc.vector.tensor_copy(page[t][:].indirect(entries(idx2, lo, hi)), xs_tile[:])
             if hi == S:
-                split = T2 - GPSIMD_COLS[t // 2]
+                split = T2 - GPSIMD_COLS if t >= 2 else T2
                 step = BANK if t == LANES - 1 else split
                 for c0 in range(0, split, step):
                     c1 = min(c0 + step, split)
                     nc.scalar.copy(out=page_bf[:, c0:c1, t], in_=page[t][:, c0:c1])
-                nc.gpsimd.tensor_scalar(
-                    page_bf[:, split:, t], page[t][:, split:], 1.0, 0.0, ALU.mult, ALU.add
-                )
+                if split < T2:
+                    nc.gpsimd.tensor_scalar(
+                        page_bf[:, split:, t], page[t][:, split:], 1.0, 0.0, ALU.mult, ALU.add
+                    )
 
         v0 = tile([P, J], U32, "v0")
         nc.vector.tensor_copy(v0[:], tab[0][:].indirect(idx[:]))
@@ -212,9 +203,17 @@ def tile_list_duplex_cancel_filter_kernel(
         quantise_wtx(0, 2 * P, BANK)
         quantise_wtx(1, 0, BANK)
 
+        wrx = tile([P, PASSES, 2 * H], U8, "wrx", tag="wtx_bf1")
+        wrx_to = wrx[:].rearrange("p a c -> p (a c)").bitcast(U16)
+        wrx_from = wrx_raw[:].rearrange("p a c -> p (a c)").bitcast(U16)
+        nc.gpsimd.tensor_copy(
+            out=wrx_to.rearrange("p (h t m) -> p h t m", t=LANES, m=P),
+            in_=wrx_from.rearrange("p (h m t) -> p h t m", t=LANES, m=P),
+        )
+
         leak0 = tile([P, LANES, J], F32, "leak0")
         leak1 = tile([P, 2, LANES, HALF], F32, "leak1")
-        gains = tile([P, LANES - 1, J], F32, "gains", tag="wtx_raw0")
+        gains = tile([P, 2, J], F32, "gains", tag="wtx_raw0")
         out_rows = out.rearrange("(n p) j -> p n j", p=P)
         held_tags = {3: "a3", 4: "a4", ROW_TILES - 2: "wtx_bf0", ROW_TILES - 1: "tab1"}
         x_tags = ("xs3_0", "xs1_0", "wrx_raw", "wtx_raw1")
@@ -234,26 +233,30 @@ def tile_list_duplex_cancel_filter_kernel(
                     rhs=page_codes[:, cols].bitcast(FP8X4), rhs_scale=page_plane[:, cols],
                     start=True, stop=True,
                 )
-                nc.scalar.copy(out=a_rows[:, cols], in_=acc[:])
+                if i == ROW_TILES - 1 and place < 2:
+                    nc.vector.tensor_copy(out=a_rows[:, cols], in_=acc[:])
+                else:
+                    nc.scalar.copy(out=a_rows[:, cols], in_=acc[:])
             return a_rows
 
+        x_last = tile([P, 2, J], F32, "x_last")
+
         def gather_x(i):
-            x = tile([P, J], F32, f"x{i}", tag=x_tags[i] if i < len(x_tags) else None)
-            step = HALF if i == 0 else J
-            for lo in range(0, J, step):
-                nc.vector.tensor_copy(
-                    x[:, lo : lo + step], a_tiles[i][:].indirect(entries(idx3, lo, lo + step))
-                )
+            if i < ROW_TILES - 2:
+                x = tile([P, J], F32, f"x{i}", tag=x_tags[i] if i < len(x_tags) else None)[:]
+            else:
+                x = x_last[:, i - (ROW_TILES - 2), :]
+            nc.vector.tensor_copy(x, a_tiles[i][:].indirect(idx3[:]))
             return x
 
         def leak_operands(i, halves):
             g, t = divmod(i, LANES)
-            x = x_tiles[i][:].rearrange("p (h j) -> p h j", j=HALF)[:, halves, :]
+            x = x_tiles[i].rearrange("p (h j) -> p h j", j=HALF)[:, halves, :]
             if g == 0:
                 y = leak0[:, t, :].rearrange("p (h j) -> p h j", j=HALF)[:, halves, :]
                 return x, y, y
             z = leak1[:, halves, t, :]
-            if t == LANES - 1:
+            if t >= 2:
                 return x, z, z
             return x, gains[:, t, :].rearrange("p (h j) -> p h j", j=HALF)[:, halves, :], z
 
@@ -367,10 +370,7 @@ def tile_list_duplex_cancel_filter_kernel(
                 subtract(g, j0, resid[piece][:, g, lo : lo + B_COLS, :], banks[k])
 
         row_tile(0)
-        square(0, halves[0])
-        square(0, halves[1])
-        gain(0, both_halves)
-        product(0, both_halves)
+        leak_of(0)
         for i in range(1, 4):
             row_tile(i)
         leak_of(1)
@@ -398,9 +398,9 @@ def tile_list_duplex_cancel_filter_kernel(
         square(7, halves[1])
         gain(6, halves[1])
         gain(7, halves[1])
-        for half in halves:
-            product(6, half)
-            product(7, half)
+        for half in range(2):
+            y = leak1[:, half, 2:, :]
+            nc.gpsimd.tensor_tensor(y, y, x_last[:, :, HALF * half : HALF * (half + 1)], ALU.mult)
         resid_rest = tile([P, 2, PASSES, Y_COLS, LANES], BF16, "resid_rest", tag=held_tags[6])
         resid = resid + [resid_rest[:, 0], resid_rest[:, 1]]
         b10 = received(1, 0, "odd")
@@ -411,7 +411,7 @@ def tile_list_duplex_cancel_filter_kernel(
         for piece in (0, 1):
             filter_and_store(piece, quantise_resid(piece, both_passes))
         subtract_banks(1, 1, b11, 0, 2)
-        last_first_pass = quantise_resid(3, first_pass, f"x{ROW_TILES - 1}")
+        last_first_pass = quantise_resid(3, first_pass, "x_last")
         filter_and_store(2, quantise_resid(2, both_passes))
         subtract_banks(1, 1, b11, 2, 2)
         filter_and_store(3, last_first_pass + quantise_resid(3, second_pass))

@@ -30,7 +30,7 @@ B_COLS = BANK // LANES
 RING = 4
 ROW_RING = 4
 FIRST_XS = 256
-GPSIMD_COLS = 768
+GPSIMD_COLS = (256, 768)
 SCALAR_GAINS_FROM = 4
 Y_COLS = 256
 PIECES = J // Y_COLS
@@ -158,15 +158,14 @@ def tile_list_duplex_cancel_filter_kernel(
         for (t, lo, hi), xs_tile in zip(xs_pieces, xs_tiles):
             nc.vector.tensor_copy(page[t][:].indirect(entries(idx2, lo, hi)), xs_tile[:])
             if hi == S:
-                split = T2 - GPSIMD_COLS if t >= 2 else T2
+                split = T2 - GPSIMD_COLS[t // 2]
                 step = BANK if t == LANES - 1 else split
                 for c0 in range(0, split, step):
                     c1 = min(c0 + step, split)
                     nc.scalar.copy(out=page_bf[:, c0:c1, t], in_=page[t][:, c0:c1])
-                if split < T2:
-                    nc.gpsimd.tensor_scalar(
-                        page_bf[:, split:, t], page[t][:, split:], 1.0, 0.0, ALU.mult, ALU.add
-                    )
+                nc.gpsimd.tensor_scalar(
+                    page_bf[:, split:, t], page[t][:, split:], 1.0, 0.0, ALU.mult, ALU.add
+                )
 
         v0 = tile([P, J], U32, "v0")
         nc.vector.tensor_copy(v0[:], tab[0][:].indirect(idx[:]))

@@ -232,7 +232,7 @@ def tile_list_duplex_cancel_filter_kernel(
                     rhs=page_codes[:, cols].bitcast(FP8X4), rhs_scale=page_plane[:, cols],
                     start=True, stop=True,
                 )
-                if i == ROW_TILES - 1 and place < 2:
+                if i == ROW_TILES - 1 and place >= 2:
                     nc.vector.tensor_copy(out=a_rows[:, cols], in_=acc[:])
                 else:
                     nc.scalar.copy(out=a_rows[:, cols], in_=acc[:])
@@ -322,7 +322,7 @@ def tile_list_duplex_cancel_filter_kernel(
             last = piece == PIECES - 1
             staged = tile([P, N // P, Y_COLS], F32, f"staged{piece}")
             for group in ((0,), (1,), (2,)) if last else ((0, 1), (2,)):
-                y = bank([P, len(group), Y_COLS], "even" if piece == 2 else "odd")
+                y = bank([P, len(group), Y_COLS], "odd" if piece == 2 else "even")
                 for place, n in enumerate(group):
                     rows = slice(P * n, P * (n + 1))
                     for g in range(PASSES):
@@ -383,10 +383,11 @@ def tile_list_duplex_cancel_filter_kernel(
         leak_of(4)
         row_tile(7)
         b00 = received(0, 0, "even")
-        resid_first = tile([P, 2, PASSES, Y_COLS, LANES], BF16, "resid_first", tag=held_tags[7])
-        resid = [resid_first[:, 0], resid_first[:, 1]]
+        b01 = received(0, 1, "odd")
+        resid_all = tile([P, PIECES, PASSES, Y_COLS, LANES], BF16, "resid", tag=held_tags[7])
+        resid = [resid_all[:, piece] for piece in range(PIECES)]
         subtract_banks(0, 0, b00)
-        b01 = received(0, 1, "even")
+        b10 = received(1, 0, "even")
         square(5, both_halves)
         gain(5, both_halves)
         product(5, both_halves)
@@ -400,11 +401,8 @@ def tile_list_duplex_cancel_filter_kernel(
         for half in range(2):
             y = leak1[:, half, 2:, :]
             nc.gpsimd.tensor_tensor(y, y, x_last[:, :, HALF * half : HALF * (half + 1)], ALU.mult)
-        resid_rest = tile([P, 2, PASSES, Y_COLS, LANES], BF16, "resid_rest", tag=held_tags[6])
-        resid = resid + [resid_rest[:, 0], resid_rest[:, 1]]
-        b10 = received(1, 0, "odd")
         subtract_banks(0, 1, b01)
-        b11 = received(1, 1, "even")
+        b11 = received(1, 1, "odd")
         subtract_banks(1, 0, b10)
         both_passes, first_pass, second_pass = slice(0, 2), slice(0, 1), slice(1, 2)
         for piece in (0, 1):

@@ -30,7 +30,7 @@ B_COLS = BANK // LANES
 RING = 4
 ROW_RING = 4
 FIRST_XS = 256
-GPSIMD_COLS = (256, 768)
+GPSIMD_COLS = (256, 704)
 SCALAR_GAINS_FROM = 4
 Y_COLS = 256
 PIECES = J // Y_COLS
@@ -49,8 +49,8 @@ def tile_list_duplex_cancel_filter_kernel(
         def tile(shape, dtype, name, tag=None, bufs=1):
             return sb.tile(shape, dtype, name=name, tag=tag or name, bufs=bufs, align_bytes=ALIGN)
 
-        def bank(shape, tag):
-            return psum.tile(shape, F32, name=tag, bufs=RING)
+        def bank(shape, number):
+            return psum.tile(shape, F32, name=f"bank{number}")
 
         def zeroed_plane(width, name):
             plane = tile([P, width], U8, name)
@@ -188,12 +188,6 @@ def tile_list_duplex_cancel_filter_kernel(
                 in_=page_bf[:, cols, :].rearrange("p c t -> p (c t)"),
             )
 
-        def gather_v1(half, tag):
-            words = tile([P, HALF], U32, f"v1_{half}", tag=tag)
-            lo = HALF * half
-            nc.vector.tensor_copy(words[:], tab[1][:].indirect(entries(idx, lo, lo + HALF)))
-            return words
-
         page_pieces = [slice(c0, c0 + BANK) for c0 in (T2 - BANK, *range(0, T2 - BANK, BANK))]
         quantise_wtx(0, 0, P)
         for cols in page_pieces:
@@ -214,7 +208,7 @@ def tile_list_duplex_cancel_filter_kernel(
         leak1 = tile([P, 2, LANES, HALF], F32, "leak1")
         gains = tile([P, 2, J], F32, "gains", tag="wtx_raw0")
         out_rows = out.rearrange("(n p) j -> p n j", p=P)
-        held_tags = {3: "a3", 4: "a4", ROW_TILES - 2: "wtx_bf0", ROW_TILES - 1: "tab1"}
+        held_tags = {2: "a2", 4: "a4", ROW_TILES - 2: "wtx_bf0", ROW_TILES - 1: "tab1"}
         x_tags = ("xs3_0", "xs1_0", "wrx_raw", "wtx_raw1")
 
         def project_page(i):
@@ -224,7 +218,7 @@ def tile_list_duplex_cancel_filter_kernel(
                 a_rows = tile([P, T2], F32, f"a{i}", tag="row", bufs=ROW_RING)
             g, t = divmod(i, LANES)
             for place, cols in enumerate(page_pieces):
-                acc = bank([P, BANK], "even" if i in (0, 2, 4) else "odd")
+                acc = bank([P, BANK], place if i in (0, 2, 4) else RING + place)
                 nc.tensor.matmul_mx(
                     out=acc[:],
                     lhsT=wtx_codes[:, P * i : P * (i + 1)].bitcast(FP8X4),
@@ -282,7 +276,7 @@ def tile_list_duplex_cancel_filter_kernel(
         def project_received(g, j0, tag):
             cols = slice(j0, j0 + B_COLS)
             b = bank([P, LANES, B_COLS], tag)
-            words = (v0[:, cols], v1[j0 // HALF][:, j0 % HALF : j0 % HALF + B_COLS])
+            words = (v0[:, cols], v1[:, cols])
             for t in range(LANES):
                 r0 = P * (LANES * g + t)
                 for a in range(PASSES):
@@ -322,7 +316,7 @@ def tile_list_duplex_cancel_filter_kernel(
             last = piece == PIECES - 1
             staged = tile([P, N // P, Y_COLS], F32, f"staged{piece}")
             for group in ((0,), (1,), (2,)) if last else ((0, 1), (2,)):
-                y = bank([P, len(group), Y_COLS], "odd" if piece == 2 else "even")
+                y = bank([P, len(group), Y_COLS], y_banks[piece][group[0] if last else group[0] // 2])
                 for place, n in enumerate(group):
                     rows = slice(P * n, P * (n + 1))
                     for g in range(PASSES):
@@ -348,7 +342,7 @@ def tile_list_duplex_cancel_filter_kernel(
                 nc.sync.dma_start(out=out_rows[:, :, cols], in_=staged[:])
 
         both_halves, halves = slice(0, 2), (slice(0, 1), slice(1, 2))
-        a_tiles, x_tiles, v1 = [], [], []
+        a_tiles, x_tiles = [], []
 
         def row_tile(i):
             a_tiles.append(project_page(i))
@@ -360,7 +354,7 @@ def tile_list_duplex_cancel_filter_kernel(
             product(i, both_halves)
 
         def received(g, half, tag):
-            return [project_received(g, HALF * half + B_COLS * k, tag) for k in range(RING)]
+            return [project_received(g, HALF * half + B_COLS * k, tag[k]) for k in range(RING)]
 
         def subtract_banks(g, half, banks, first=0, count=RING):
             for k in range(first, first + count):
@@ -373,21 +367,21 @@ def tile_list_duplex_cancel_filter_kernel(
         for i in range(1, 4):
             row_tile(i)
         leak_of(1)
-        v1.append(gather_v1(0, held_tags[3]))
+        v1 = tile([P, J], U32, "v1", tag=held_tags[2])
+        nc.vector.tensor_copy(v1[:], tab[1][:].indirect(idx[:]))
         row_tile(4)
         leak_of(2)
-        leak_of(3)
-        v1.append(gather_v1(1, held_tags[4]))
         row_tile(5)
+        leak_of(3)
         row_tile(6)
         leak_of(4)
         row_tile(7)
-        b00 = received(0, 0, "even")
-        b01 = received(0, 1, "odd")
+        b00 = received(0, 0, (0, 1, 2, 3))
+        b01 = received(0, 1, (4, 5, 6, 7))
         resid_all = tile([P, PIECES, PASSES, Y_COLS, LANES], BF16, "resid", tag=held_tags[7])
         resid = [resid_all[:, piece] for piece in range(PIECES)]
         subtract_banks(0, 0, b00)
-        b10 = received(1, 0, "even")
+        b10 = received(1, 0, (0, 1, 2, 3))
         square(5, both_halves)
         gain(5, both_halves)
         product(5, both_halves)
@@ -402,8 +396,9 @@ def tile_list_duplex_cancel_filter_kernel(
             y = leak1[:, half, 2:, :]
             nc.gpsimd.tensor_tensor(y, y, x_last[:, :, HALF * half : HALF * (half + 1)], ALU.mult)
         subtract_banks(0, 1, b01)
-        b11 = received(1, 1, "odd")
         subtract_banks(1, 0, b10)
+        b11 = received(1, 1, (4, 5, 0, 1))
+        y_banks = ((6, 7), (2, 3), (4, 5), (6, 7, 2))
         both_passes, first_pass, second_pass = slice(0, 2), slice(0, 1), slice(1, 2)
         for piece in (0, 1):
             filter_and_store(piece, quantise_resid(piece, both_passes))

@@ -32,6 +32,7 @@ ROW_RING = 4
 FIRST_XS = 256
 GPSIMD_COLS = (256, 704)
 SCALAR_GAINS_FROM = 4
+FIRST_V1 = 256
 Y_COLS = 256
 PIECES = J // Y_COLS
 
@@ -84,14 +85,8 @@ def tile_list_duplex_cancel_filter_kernel(
 
         nc.sync.dma_start(idx[:], offs)
         tab_rows = load_scale_rows(tab_scales, "tab_rows", nc.vector)
-        wrx_rows_raw = load_scale_rows(wrx_scales, "wrx_rows_raw", nc.gpsimd)
         v_rows = tile([P, J], U8, "v_rows")
         nc.vector.tensor_copy(v_rows[:], tab_rows[:].indirect(idx[:]))
-        wrx_rows = tile([P, H], U8, "wrx_rows")
-        nc.gpsimd.tensor_copy(
-            out=wrx_rows[:].rearrange("p (g t m) -> p g t m", t=LANES, m=P),
-            in_=wrx_rows_raw[:].rearrange("p (g m t) -> p g t m", t=LANES, m=P),
-        )
 
         base_lanes = base.rearrange("(p t) c -> p t c", t=LANES)
         xs_lanes = xs.rearrange("(p t) c -> p t c", t=LANES)
@@ -108,15 +103,23 @@ def tile_list_duplex_cancel_filter_kernel(
                 in_=wtx[:, BANK * g : BANK * (g + 1)].rearrange("(p i) c -> p i c", i=LANES),
             )
 
-        nc.sync.dma_start(idx2[:], offs2)
         for (t, lo, hi), xs_tile in zip(xs_pieces, xs_tiles):
             if lo == 0:
                 nc.sync.dma_start(out=page[t][:], in_=base_lanes[:, t, :])
+            if hi == FIRST_XS:
+                nc.sync.dma_start(idx2[:], offs2)
             nc.sync.dma_start(out=xs_tile[:], in_=xs_lanes[:, t, lo:hi])
+            if hi == FIRST_XS:
+                wrx_rows_raw = load_scale_rows(wrx_scales, "wrx_rows_raw", nc.gpsimd)
             if t < PASSES and hi == S:
                 load_wtx(t)
         nc.sync.dma_start(
             out=wrx_raw[:].bitcast(I32), in_=wrx_words.rearrange("a p c -> p a c").bitcast(I32)
+        )
+        wrx_rows = tile([P, H], U8, "wrx_rows")
+        nc.gpsimd.tensor_copy(
+            out=wrx_rows[:].rearrange("p (g t m) -> p g t m", t=LANES, m=P),
+            in_=wrx_rows_raw[:].rearrange("p (g m t) -> p g t m", t=LANES, m=P),
         )
         wdem_planes = zeroed_plane(N, "wdem_planes")
         v_plane = [zeroed_plane(J, f"v_plane{a}") for a in range(PASSES)]
@@ -195,6 +198,8 @@ def tile_list_duplex_cancel_filter_kernel(
         quantise_wtx(0, P, 2 * P)
         quantise_wtx(0, 2 * P, BANK)
         quantise_wtx(1, 0, BANK)
+        v1_first = tile([P, FIRST_V1], U32, "v1_first", tag="xs2_0")
+        nc.vector.tensor_copy(v1_first[:], tab[1][:].indirect(entries(idx, 0, FIRST_V1)))
 
         wrx = tile([P, PASSES, 2 * H], U8, "wrx", tag="wtx_bf1")
         wrx_to = wrx[:].rearrange("p a c -> p (a c)").bitcast(U16)
@@ -211,13 +216,15 @@ def tile_list_duplex_cancel_filter_kernel(
         held_tags = {2: "a2", 4: "a4", ROW_TILES - 2: "wtx_bf0", ROW_TILES - 1: "tab1"}
         x_tags = ("xs3_0", "xs1_0", "wrx_raw", "wtx_raw1")
 
-        def project_page(i):
+        def project_page(i, midway=None):
             if i in held_tags:
                 a_rows = tile([P, T2], F32, f"a{i}", tag=held_tags[i])
             else:
                 a_rows = tile([P, T2], F32, f"a{i}", tag="row", bufs=ROW_RING)
             g, t = divmod(i, LANES)
             for place, cols in enumerate(page_pieces):
+                if place == 2 and midway is not None:
+                    midway()
                 acc = bank([P, BANK], place if i in (0, 2, 4) else RING + place)
                 nc.tensor.matmul_mx(
                     out=acc[:],
@@ -226,7 +233,7 @@ def tile_list_duplex_cancel_filter_kernel(
                     rhs=page_codes[:, cols].bitcast(FP8X4), rhs_scale=page_plane[:, cols],
                     start=True, stop=True,
                 )
-                if i == ROW_TILES - 1 and place >= 2:
+                if (i == ROW_TILES - 1 and place >= 2) or (i == 3 and place == 0):
                     nc.vector.tensor_copy(out=a_rows[:, cols], in_=acc[:])
                 else:
                     nc.scalar.copy(out=a_rows[:, cols], in_=acc[:])
@@ -255,7 +262,7 @@ def tile_list_duplex_cancel_filter_kernel(
 
         def square(i, halves):
             x, y, z = leak_operands(i, halves)
-            if i == 0:
+            if i == 0 and halves.start == 0:
                 nc.gpsimd.tensor_tensor(y, x, x, ALU.mult)
             else:
                 nc.scalar.activation(out=y, in_=x, func=ACT.Square)
@@ -276,7 +283,10 @@ def tile_list_duplex_cancel_filter_kernel(
         def project_received(g, j0, tag):
             cols = slice(j0, j0 + B_COLS)
             b = bank([P, LANES, B_COLS], tag)
-            words = (v0[:, cols], v1[:, cols])
+            if j0 < FIRST_V1:
+                words = (v0[:, cols], v1_first[:, cols])
+            else:
+                words = (v0[:, cols], v1_rest[:, j0 - FIRST_V1 : j0 - FIRST_V1 + B_COLS])
             for t in range(LANES):
                 r0 = P * (LANES * g + t)
                 for a in range(PASSES):
@@ -344,8 +354,8 @@ def tile_list_duplex_cancel_filter_kernel(
         both_halves, halves = slice(0, 2), (slice(0, 1), slice(1, 2))
         a_tiles, x_tiles = [], []
 
-        def row_tile(i):
-            a_tiles.append(project_page(i))
+        def row_tile(i, midway=None):
+            a_tiles.append(project_page(i, midway))
             x_tiles.append(gather_x(i))
 
         def leak_of(i):
@@ -363,12 +373,15 @@ def tile_list_duplex_cancel_filter_kernel(
                 subtract(g, j0, resid[piece][:, g, lo : lo + B_COLS, :], banks[k])
 
         row_tile(0)
-        leak_of(0)
-        for i in range(1, 4):
-            row_tile(i)
+        square(0, halves[0])
+        row_tile(1)
+        row_tile(2, lambda: square(0, halves[1]))
+        gain(0, both_halves)
+        product(0, both_halves)
+        row_tile(3)
         leak_of(1)
-        v1 = tile([P, J], U32, "v1", tag=held_tags[2])
-        nc.vector.tensor_copy(v1[:], tab[1][:].indirect(idx[:]))
+        v1_rest = tile([P, J - FIRST_V1], U32, "v1_rest", tag=held_tags[2])
+        nc.vector.tensor_copy(v1_rest[:], tab[1][:].indirect(entries(idx, FIRST_V1, J)))
         row_tile(4)
         leak_of(2)
         row_tile(5)

@@ -27,12 +27,14 @@ LINE = 4
 ROW_TILES = PASSES * LANES
 HALF = J // 2
 B_COLS = BANK // LANES
-RING = 4
+LOW_BANKS, HIGH_BANKS = (0, 1, 2, 3), (4, 5, 6, 7)
 ROW_RING = 4
 FIRST_XS = 256
 GPSIMD_COLS = (256, 704)
-SCALAR_GAINS_FROM = 4
 FIRST_V1 = 256
+SCALAR_GAINS_FROM = 4
+SQUARE_LAG = 2
+VECTOR_BANKS = ((ROW_TILES - 1, 2), (ROW_TILES - 1, 3))
 Y_COLS = 256
 PIECES = J // Y_COLS
 
@@ -198,7 +200,7 @@ def tile_list_duplex_cancel_filter_kernel(
         quantise_wtx(0, P, 2 * P)
         quantise_wtx(0, 2 * P, BANK)
         quantise_wtx(1, 0, BANK)
-        v1_first = tile([P, FIRST_V1], U32, "v1_first", tag="xs2_0")
+        v1_first = tile([P, FIRST_V1], U32, "v1_first")
         nc.vector.tensor_copy(v1_first[:], tab[1][:].indirect(entries(idx, 0, FIRST_V1)))
 
         wrx = tile([P, PASSES, 2 * H], U8, "wrx", tag="wtx_bf1")
@@ -211,21 +213,25 @@ def tile_list_duplex_cancel_filter_kernel(
 
         leak0 = tile([P, LANES, J], F32, "leak0")
         leak1 = tile([P, 2, LANES, HALF], F32, "leak1")
-        gains = tile([P, 2, J], F32, "gains", tag="wtx_raw0")
+        gain_rows = tile([P, 2, J], F32, "gain_rows", tag="wtx_raw0")
+        x_last = tile([P, 2, J], F32, "x_last")
         out_rows = out.rearrange("(n p) j -> p n j", p=P)
-        held_tags = {2: "a2", 4: "a4", ROW_TILES - 2: "wtx_bf0", ROW_TILES - 1: "tab1"}
+        held_tags = {2: "a2", ROW_TILES - 1: "tab1"}
         x_tags = ("xs3_0", "xs1_0", "wrx_raw", "wtx_raw1")
+        both_halves, halves = slice(0, 2), (slice(0, 1), slice(1, 2))
+        x_tiles = []
 
-        def project_page(i, midway=None):
+        def row_tile(i, between=None):
             if i in held_tags:
                 a_rows = tile([P, T2], F32, f"a{i}", tag=held_tags[i])
             else:
                 a_rows = tile([P, T2], F32, f"a{i}", tag="row", bufs=ROW_RING)
             g, t = divmod(i, LANES)
+            banks = HIGH_BANKS if i % 2 else LOW_BANKS
             for place, cols in enumerate(page_pieces):
-                if place == 2 and midway is not None:
-                    midway()
-                acc = bank([P, BANK], place if i in (0, 2, 4) else RING + place)
+                if between is not None and place == between[0]:
+                    between[1]()
+                acc = bank([P, BANK], banks[place])
                 nc.tensor.matmul_mx(
                     out=acc[:],
                     lhsT=wtx_codes[:, P * i : P * (i + 1)].bitcast(FP8X4),
@@ -233,42 +239,36 @@ def tile_list_duplex_cancel_filter_kernel(
                     rhs=page_codes[:, cols].bitcast(FP8X4), rhs_scale=page_plane[:, cols],
                     start=True, stop=True,
                 )
-                if (i == ROW_TILES - 1 and place >= 2) or (i == 3 and place == 0):
+                if (i, place) in VECTOR_BANKS:
                     nc.vector.tensor_copy(out=a_rows[:, cols], in_=acc[:])
                 else:
                     nc.scalar.copy(out=a_rows[:, cols], in_=acc[:])
-            return a_rows
-
-        x_last = tile([P, 2, J], F32, "x_last")
-
-        def gather_x(i):
             if i < ROW_TILES - 2:
                 x = tile([P, J], F32, f"x{i}", tag=x_tags[i] if i < len(x_tags) else None)[:]
             else:
                 x = x_last[:, i - (ROW_TILES - 2), :]
-            nc.vector.tensor_copy(x, a_tiles[i][:].indirect(idx3[:]))
-            return x
+            nc.vector.tensor_copy(x, a_rows[:].indirect(idx3[:]))
+            x_tiles.append(x)
 
-        def leak_operands(i, halves):
+        def by_halves(row, part):
+            return row.rearrange("p (h j) -> p h j", j=HALF)[:, part, :]
+
+        def leak_place(i, part):
             g, t = divmod(i, LANES)
-            x = x_tiles[i].rearrange("p (h j) -> p h j", j=HALF)[:, halves, :]
-            if g == 0:
-                y = leak0[:, t, :].rearrange("p (h j) -> p h j", j=HALF)[:, halves, :]
-                return x, y, y
-            z = leak1[:, halves, t, :]
-            if t >= 2:
-                return x, z, z
-            return x, gains[:, t, :].rearrange("p (h j) -> p h j", j=HALF)[:, halves, :], z
+            return by_halves(leak0[:, t, :], part) if g == 0 else leak1[:, part, t, :]
 
-        def square(i, halves):
-            x, y, z = leak_operands(i, halves)
-            if i == 0 and halves.start == 0:
-                nc.gpsimd.tensor_tensor(y, x, x, ALU.mult)
-            else:
-                nc.scalar.activation(out=y, in_=x, func=ACT.Square)
+        def gain_place(i, part):
+            if LANES <= i < ROW_TILES - 2:
+                return by_halves(gain_rows[:, i - LANES, :], part)
+            return leak_place(i, part)
 
-        def gain(i, halves):
-            y = leak_operands(i, halves)[1]
+        def square(i, part):
+            nc.scalar.activation(
+                out=gain_place(i, part), in_=by_halves(x_tiles[i], part), func=ACT.Square
+            )
+
+        def gain(i, part):
+            y = gain_place(i, part)
             g, t = divmod(i, LANES)
             cub_col = cub_cols[:, g, t : t + 1]
             if i >= SCALAR_GAINS_FROM:
@@ -276,38 +276,51 @@ def tile_list_duplex_cancel_filter_kernel(
             else:
                 nc.gpsimd.tensor_scalar(y, y, cub_col, 1.0, ALU.mult, ALU.add)
 
-        def product(i, halves):
-            x, y, z = leak_operands(i, halves)
-            nc.gpsimd.tensor_tensor(z, y, x, ALU.mult)
-
-        def project_received(g, j0, tag):
-            cols = slice(j0, j0 + B_COLS)
-            b = bank([P, LANES, B_COLS], tag)
-            if j0 < FIRST_V1:
-                words = (v0[:, cols], v1_first[:, cols])
-            else:
-                words = (v0[:, cols], v1_rest[:, j0 - FIRST_V1 : j0 - FIRST_V1 + B_COLS])
-            for t in range(LANES):
-                r0 = P * (LANES * g + t)
-                for a in range(PASSES):
-                    nc.tensor.matmul_mx(
-                        out=b[:, t, :],
-                        lhsT=wrx[:, a, 2 * r0 : 2 * (r0 + P)].bitcast(FP4X4),
-                        lhsT_scale=wrx_plane[a][:, r0 : r0 + P],
-                        rhs=words[a].bitcast(FP8X4), rhs_scale=v_plane[a][:, cols],
-                        start=(a == 0), stop=(a == PASSES - 1),
-                    )
-            return b
-
-        def subtract(g, j0, resid_cols, b):
-            half, lo = divmod(j0, HALF)
-            leak = leak0[:, :, j0 : j0 + B_COLS] if g == 0 else leak1[:, half, :, lo : lo + B_COLS]
-            nc.vector.tensor_tensor(
-                resid_cols.rearrange("p (c i) t -> p c t i", i=LINE),
-                b[:].rearrange("p t (c i) -> p c t i", i=LINE),
-                leak.rearrange("p t (c i) -> p c t i", i=LINE),
-                ALU.subtract,
+        def product(i):
+            nc.gpsimd.tensor_tensor(
+                leak_place(i, both_halves), gain_place(i, both_halves),
+                by_halves(x_tiles[i], both_halves), ALU.mult,
             )
+
+        def project_received(g, half, numbers):
+            banks = []
+            for quarter, number in enumerate(numbers):
+                j0 = HALF * half + B_COLS * quarter
+                cols = slice(j0, j0 + B_COLS)
+                if j0 < FIRST_V1:
+                    words = (v0[:, cols], v1_first[:, cols])
+                else:
+                    words = (v0[:, cols], v1_rest[:, j0 - FIRST_V1 : j0 - FIRST_V1 + B_COLS])
+                b = bank([P, LANES, B_COLS], number)
+                for t in range(LANES):
+                    r0 = P * (LANES * g + t)
+                    for a in range(PASSES):
+                        nc.tensor.matmul_mx(
+                            out=b[:, t, :],
+                            lhsT=wrx[:, a, 2 * r0 : 2 * (r0 + P)].bitcast(FP4X4),
+                            lhsT_scale=wrx_plane[a][:, r0 : r0 + P],
+                            rhs=words[a].bitcast(FP8X4), rhs_scale=v_plane[a][:, cols],
+                            start=(a == 0), stop=(a == PASSES - 1),
+                        )
+                banks.append((j0, b))
+            return banks
+
+        def subtract(g, banks):
+            for j0, b in banks:
+                half, in_half = divmod(j0, HALF)
+                piece, in_piece = divmod(j0, Y_COLS)
+                if g == 0:
+                    leak = leak0[:, :, j0 : j0 + B_COLS]
+                else:
+                    leak = leak1[:, half, :, in_half : in_half + B_COLS]
+                nc.vector.tensor_tensor(
+                    resid[:, piece, g, in_piece : in_piece + B_COLS, :].rearrange(
+                        "p (c i) t -> p c t i", i=LINE
+                    ),
+                    b[:].rearrange("p t (c i) -> p c t i", i=LINE),
+                    leak.rearrange("p t (c i) -> p c t i", i=LINE),
+                    ALU.subtract,
+                )
 
         def quantise_resid(piece, passes, tag=None):
             count = passes.stop - passes.start
@@ -317,16 +330,18 @@ def tile_list_duplex_cancel_filter_kernel(
             nc.vector.quantize_mx(
                 out=resid_codes[:].rearrange("p g c -> p (g c)").bitcast(FP8X4),
                 scales=resid_plane[:].rearrange("p g c -> p (g c)"),
-                in_=resid[piece][:, passes].rearrange("p g c t -> p (g c t)"),
+                in_=resid[:, piece, passes].rearrange("p g c t -> p (g c t)"),
             )
             return [(resid_codes[:, g, :], resid_plane[:, g, :]) for g in range(count)]
 
-        def filter_and_store(piece, operands):
+        def filter_and_store(piece, operands, numbers):
             cols = slice(Y_COLS * piece, Y_COLS * (piece + 1))
             last = piece == PIECES - 1
+            store_by_tiles = piece >= PIECES - 2
             staged = tile([P, N // P, Y_COLS], F32, f"staged{piece}")
-            for group in ((0,), (1,), (2,)) if last else ((0, 1), (2,)):
-                y = bank([P, len(group), Y_COLS], y_banks[piece][group[0] if last else group[0] // 2])
+            groups = ((0,), (1,), (2,)) if last else ((0, 1), (2,))
+            for group, number in zip(groups, numbers):
+                y = bank([P, len(group), Y_COLS], number)
                 for place, n in enumerate(group):
                     rows = slice(P * n, P * (n + 1))
                     for g in range(PASSES):
@@ -345,78 +360,58 @@ def tile_list_duplex_cancel_filter_kernel(
                         nc.scalar.activation(
                             out=staged[:, n, :], in_=y[:, place, :], func=ACT.Identity, bias=bias
                         )
-                    if last:
-                        queue = nc.scalar if n == 2 else nc.sync
+                    if store_by_tiles:
+                        queue = nc.scalar if last and n == 2 else nc.sync
                         queue.dma_start(out=out_rows[:, n, cols], in_=staged[:, n, :])
-            if not last:
+            if not store_by_tiles:
                 nc.sync.dma_start(out=out_rows[:, :, cols], in_=staged[:])
 
-        both_halves, halves = slice(0, 2), (slice(0, 1), slice(1, 2))
-        a_tiles, x_tiles = [], []
+        row_tile(0)
+        x_first = by_halves(x_tiles[0], halves[0])
+        nc.gpsimd.tensor_tensor(gain_place(0, halves[0]), x_first, x_first, ALU.mult)
+        row_tile(1)
+        row_tile(2, between=(2, lambda: square(0, halves[1])))
+        gain(0, both_halves)
+        product(0)
 
-        def row_tile(i, midway=None):
-            a_tiles.append(project_page(i, midway))
-            x_tiles.append(gather_x(i))
-
-        def leak_of(i):
+        for i in range(1, SCALAR_GAINS_FROM):
+            row_tile(i + SQUARE_LAG)
             square(i, both_halves)
             gain(i, both_halves)
-            product(i, both_halves)
+            product(i)
+            if i == 1:
+                v1_rest = tile([P, J - FIRST_V1], U32, "v1_rest", tag=held_tags[2])
+                nc.vector.tensor_copy(v1_rest[:], tab[1][:].indirect(entries(idx, FIRST_V1, J)))
 
-        def received(g, half, tag):
-            return [project_received(g, HALF * half + B_COLS * k, tag[k]) for k in range(RING)]
-
-        def subtract_banks(g, half, banks, first=0, count=RING):
-            for k in range(first, first + count):
-                j0 = HALF * half + B_COLS * k
-                piece, lo = divmod(j0, Y_COLS)
-                subtract(g, j0, resid[piece][:, g, lo : lo + B_COLS, :], banks[k])
-
-        row_tile(0)
-        square(0, halves[0])
-        row_tile(1)
-        row_tile(2, lambda: square(0, halves[1]))
-        gain(0, both_halves)
-        product(0, both_halves)
-        row_tile(3)
-        leak_of(1)
-        v1_rest = tile([P, J - FIRST_V1], U32, "v1_rest", tag=held_tags[2])
-        nc.vector.tensor_copy(v1_rest[:], tab[1][:].indirect(entries(idx, FIRST_V1, J)))
-        row_tile(4)
-        leak_of(2)
-        row_tile(5)
-        leak_of(3)
-        row_tile(6)
-        leak_of(4)
-        row_tile(7)
-        b00 = received(0, 0, (0, 1, 2, 3))
-        b01 = received(0, 1, (4, 5, 6, 7))
-        resid_all = tile([P, PIECES, PASSES, Y_COLS, LANES], BF16, "resid", tag=held_tags[7])
-        resid = [resid_all[:, piece] for piece in range(PIECES)]
-        subtract_banks(0, 0, b00)
-        b10 = received(1, 0, (0, 1, 2, 3))
-        square(5, both_halves)
-        gain(5, both_halves)
-        product(5, both_halves)
-        square(6, both_halves)
-        square(7, halves[0])
-        gain(6, halves[0])
-        gain(7, halves[0])
-        square(7, halves[1])
-        gain(6, halves[1])
-        gain(7, halves[1])
+        row_tile(ROW_TILES - 2)
+        square(4, both_halves)
+        row_tile(ROW_TILES - 1, between=(1, lambda: gain(4, both_halves)))
+        product(4)
+        b_first = [project_received(0, 0, LOW_BANKS), project_received(0, 1, HIGH_BANKS)]
+        resid = tile(
+            [P, PIECES, PASSES, Y_COLS, LANES], BF16, "resid", tag=held_tags[ROW_TILES - 1]
+        )
+        subtract(0, b_first[0])
+        b_second = [project_received(1, 0, LOW_BANKS)]
+        for step in (square, gain):
+            for half in halves:
+                step(5, half)
+        product(5)
         for half in range(2):
+            for step in (square, gain):
+                for i in range(ROW_TILES - 2, ROW_TILES):
+                    step(i, halves[half])
             y = leak1[:, half, 2:, :]
             nc.gpsimd.tensor_tensor(y, y, x_last[:, :, HALF * half : HALF * (half + 1)], ALU.mult)
-        subtract_banks(0, 1, b01)
-        subtract_banks(1, 0, b10)
-        b11 = received(1, 1, (4, 5, 0, 1))
-        y_banks = ((6, 7), (2, 3), (4, 5), (6, 7, 2))
+        subtract(0, b_first[1])
+        subtract(1, b_second[0])
+        b_second.append(project_received(1, 1, HIGH_BANKS[:2] + LOW_BANKS[:2]))
+
         both_passes, first_pass, second_pass = slice(0, 2), slice(0, 1), slice(1, 2)
-        for piece in (0, 1):
-            filter_and_store(piece, quantise_resid(piece, both_passes))
-        subtract_banks(1, 1, b11, 0, 2)
-        last_first_pass = quantise_resid(3, first_pass, "x_last")
-        filter_and_store(2, quantise_resid(2, both_passes))
-        subtract_banks(1, 1, b11, 2, 2)
-        filter_and_store(3, last_first_pass + quantise_resid(3, second_pass))
+        filter_and_store(0, quantise_resid(0, both_passes), HIGH_BANKS[2:])
+        filter_and_store(1, quantise_resid(1, both_passes), LOW_BANKS[2:])
+        subtract(1, b_second[1][:3])
+        filter_and_store(2, quantise_resid(2, both_passes), HIGH_BANKS[:2])
+        subtract(1, b_second[1][3:])
+        last_operands = quantise_resid(3, first_pass, "x_last") + quantise_resid(3, second_pass)
+        filter_and_store(3, last_operands, HIGH_BANKS[2:] + LOW_BANKS[2:3])

@@ -34,7 +34,7 @@ GPSIMD_COLS = (256, 704)
 FIRST_V1 = 256
 SCALAR_GAINS_FROM = 4
 SQUARE_LAG = 2
-VECTOR_BANKS = ((ROW_TILES - 1, 2), (ROW_TILES - 1, 3))
+VECTOR_BANKS = ((3, 0), (ROW_TILES - 1, 2), (ROW_TILES - 1, 3))
 Y_COLS = 256
 PIECES = J // Y_COLS
 

@@ -339,7 +339,7 @@ def tile_list_duplex_cancel_filter_kernel(
             last = piece == PIECES - 1
             store_by_tiles = piece >= PIECES - 2
             staged = tile([P, N // P, Y_COLS], F32, f"staged{piece}")
-            groups = ((0,), (1,), (2,)) if last else ((0, 1), (2,))
+            groups = ((0,), (1,), (2,)) if last else ((0,), (1, 2)) if piece == 0 else ((0, 1), (2,))
             for group, number in zip(groups, numbers):
                 y = bank([P, len(group), Y_COLS], number)
                 for place, n in enumerate(group):
@@ -360,11 +360,14 @@ def tile_list_duplex_cancel_filter_kernel(
                         nc.scalar.activation(
                             out=staged[:, n, :], in_=y[:, place, :], func=ACT.Identity, bias=bias
                         )
+                    if piece == 0 and n == 0:
+                        nc.sync.dma_start(out=out_rows[:, 0, cols], in_=staged[:, 0, :])
                     if store_by_tiles:
                         queue = nc.scalar if last and n == 2 else nc.sync
                         queue.dma_start(out=out_rows[:, n, cols], in_=staged[:, n, :])
             if not store_by_tiles:
-                nc.sync.dma_start(out=out_rows[:, :, cols], in_=staged[:])
+                first = 1 if piece == 0 else 0
+                nc.sync.dma_start(out=out_rows[:, first:, cols], in_=staged[:, first:, :])
 
         row_tile(0)
         x_first = by_halves(x_tiles[0], halves[0])

@@ -176,14 +176,25 @@ def tile_list_duplex_cancel_filter_kernel(
         nc.vector.tensor_copy(v0[:], tab[0][:].indirect(idx[:]))
         codes = tile([P, T2 + H], U32, "codes", tag="tab0")
         page_codes, wtx_codes = codes[:, :T2], codes[:, T2:]
-        wtx_plane = [tile([P, BANK], U8, f"wtx_plane{g}") for g in range(PASSES)]
+        plane_starts = (0, LANES, LANES + 1, ROW_TILES)
+        wtx_plane = [
+            tile([P, P * (hi - lo)], U8, f"wtx_plane{lo}")
+            for lo, hi in zip(plane_starts, plane_starts[1:])
+        ]
+
+        def wtx_scales(first, end):
+            part = max(u for u, lo in enumerate(plane_starts) if lo <= first)
+            lo = plane_starts[part]
+            return wtx_plane[part][:, P * (first - lo) : P * (end - lo)]
+
         page_plane = tile([P, T2], U8, "page_plane")
 
-        def quantise_wtx(g, lo, hi):
+        def quantise_wtx(first, end):
+            g, t = divmod(first, LANES)
             nc.vector.quantize_mx(
-                out=wtx_codes[:, BANK * g + lo : BANK * g + hi].bitcast(FP8X4),
-                scales=wtx_plane[g][:, lo:hi],
-                in_=wtx_bf[g][:, LANES * lo : LANES * hi],
+                out=wtx_codes[:, P * first : P * end].bitcast(FP8X4),
+                scales=wtx_scales(first, end),
+                in_=wtx_bf[g][:, LANES * P * t : LANES * P * (t + end - first)],
             )
 
         def quantise_page(cols):
@@ -194,12 +205,12 @@ def tile_list_duplex_cancel_filter_kernel(
             )
 
         page_pieces = [slice(c0, c0 + BANK) for c0 in (T2 - BANK, *range(0, T2 - BANK, BANK))]
-        quantise_wtx(0, 0, P)
+        quantise_wtx(0, 1)
         for cols in page_pieces:
             quantise_page(cols)
-        quantise_wtx(0, P, 2 * P)
-        quantise_wtx(0, 2 * P, BANK)
-        quantise_wtx(1, 0, BANK)
+        quantise_wtx(1, LANES)
+        quantise_wtx(LANES, LANES + 1)
+        quantise_wtx(LANES + 1, ROW_TILES)
         v1_first = tile([P, FIRST_V1], U32, "v1_first")
         nc.vector.tensor_copy(v1_first[:], tab[1][:].indirect(entries(idx, 0, FIRST_V1)))
 
@@ -215,8 +226,9 @@ def tile_list_duplex_cancel_filter_kernel(
         leak1 = tile([P, 2, LANES, HALF], F32, "leak1")
         gain_rows = tile([P, 2, J], F32, "gain_rows", tag="wtx_raw0")
         x_last = tile([P, 2, J], F32, "x_last")
+        square_apart = tile([P, HALF], F32, "square_apart")
         out_rows = out.rearrange("(n p) j -> p n j", p=P)
-        held_tags = {2: "a2", ROW_TILES - 1: "tab1"}
+        held_tags = {ROW_TILES - 1: "tab1"}
         x_tags = ("xs3_0", "xs1_0", "wrx_raw", "wtx_raw1")
         both_halves, halves = slice(0, 2), (slice(0, 1), slice(1, 2))
         x_tiles = []
@@ -226,7 +238,6 @@ def tile_list_duplex_cancel_filter_kernel(
                 a_rows = tile([P, T2], F32, f"a{i}", tag=held_tags[i])
             else:
                 a_rows = tile([P, T2], F32, f"a{i}", tag="row", bufs=ROW_RING)
-            g, t = divmod(i, LANES)
             banks = HIGH_BANKS if i % 2 else LOW_BANKS
             for place, cols in enumerate(page_pieces):
                 if between is not None and place == between[0]:
@@ -235,7 +246,7 @@ def tile_list_duplex_cancel_filter_kernel(
                 nc.tensor.matmul_mx(
                     out=acc[:],
                     lhsT=wtx_codes[:, P * i : P * (i + 1)].bitcast(FP8X4),
-                    lhsT_scale=wtx_plane[g][:, P * t : P * (t + 1)],
+                    lhsT_scale=wtx_scales(i, i + 1),
                     rhs=page_codes[:, cols].bitcast(FP8X4), rhs_scale=page_plane[:, cols],
                     start=True, stop=True,
                 )
@@ -262,9 +273,14 @@ def tile_list_duplex_cancel_filter_kernel(
                 return by_halves(gain_rows[:, i - LANES, :], part)
             return leak_place(i, part)
 
+        def square_place(i, part):
+            if (i, part) == (5, halves[0]):
+                return by_halves(square_apart[:], part)
+            return gain_place(i, part)
+
         def square(i, part):
             nc.scalar.activation(
-                out=gain_place(i, part), in_=by_halves(x_tiles[i], part), func=ACT.Square
+                out=square_place(i, part), in_=by_halves(x_tiles[i], part), func=ACT.Square
             )
 
         def gain(i, part):
@@ -272,7 +288,9 @@ def tile_list_duplex_cancel_filter_kernel(
             g, t = divmod(i, LANES)
             cub_col = cub_cols[:, g, t : t + 1]
             if i >= SCALAR_GAINS_FROM:
-                nc.scalar.activation(out=y, in_=y, func=ACT.Identity, scale=cub_col, bias=1.0)
+                nc.scalar.activation(
+                    out=y, in_=square_place(i, part), func=ACT.Identity, scale=cub_col, bias=1.0
+                )
             else:
                 nc.gpsimd.tensor_scalar(y, y, cub_col, 1.0, ALU.mult, ALU.add)
 
@@ -382,8 +400,8 @@ def tile_list_duplex_cancel_filter_kernel(
             square(i, both_halves)
             gain(i, both_halves)
             product(i)
-            if i == 1:
-                v1_rest = tile([P, J - FIRST_V1], U32, "v1_rest", tag=held_tags[2])
+            if i == 2:
+                v1_rest = tile([P, J - FIRST_V1], U32, "v1_rest", tag="wtx_plane4")
                 nc.vector.tensor_copy(v1_rest[:], tab[1][:].indirect(entries(idx, FIRST_V1, J)))
 
         row_tile(ROW_TILES - 2)
@@ -391,14 +409,12 @@ def tile_list_duplex_cancel_filter_kernel(
         row_tile(ROW_TILES - 1, between=(1, lambda: gain(4, both_halves)))
         product(4)
         b_first = [project_received(0, 0, LOW_BANKS), project_received(0, 1, HIGH_BANKS)]
-        resid = tile(
-            [P, PIECES, PASSES, Y_COLS, LANES], BF16, "resid", tag=held_tags[ROW_TILES - 1]
-        )
-        subtract(0, b_first[0])
-        b_second = [project_received(1, 0, LOW_BANKS)]
         for step in (square, gain):
             for half in halves:
                 step(5, half)
+        resid = tile([P, PIECES, PASSES, Y_COLS, LANES], BF16, "resid", tag="square_apart")
+        subtract(0, b_first[0])
+        b_second = [project_received(1, 0, LOW_BANKS)]
         product(5)
         for half in range(2):
             for step in (square, gain):

@@ -34,7 +34,7 @@ GPSIMD_COLS = (256, 704)
 FIRST_V1 = 256
 SCALAR_GAINS_FROM = 4
 SQUARE_LAG = 2
-VECTOR_BANKS = ((3, 0), (ROW_TILES - 1, 2), (ROW_TILES - 1, 3))
+VECTOR_COLS = {(3, 0): BANK, (4, 3): BANK // 4, (7, 2): BANK, (7, 3): BANK}
 Y_COLS = 256
 PIECES = J // Y_COLS
 
@@ -250,15 +250,20 @@ def tile_list_duplex_cancel_filter_kernel(
                     rhs=page_codes[:, cols].bitcast(FP8X4), rhs_scale=page_plane[:, cols],
                     start=True, stop=True,
                 )
-                if (i, place) in VECTOR_BANKS:
-                    nc.vector.tensor_copy(out=a_rows[:, cols], in_=acc[:])
-                else:
-                    nc.scalar.copy(out=a_rows[:, cols], in_=acc[:])
+                share = VECTOR_COLS.get((i, place), 0)
+                if share:
+                    nc.vector.tensor_copy(out=a_rows[:, cols][:, :share], in_=acc[:, :share])
+                if share < BANK:
+                    nc.scalar.copy(out=a_rows[:, cols][:, share:], in_=acc[:, share:])
             if i < ROW_TILES - 2:
                 x = tile([P, J], F32, f"x{i}", tag=x_tags[i] if i < len(x_tags) else None)[:]
             else:
                 x = x_last[:, i - (ROW_TILES - 2), :]
-            nc.vector.tensor_copy(x, a_rows[:].indirect(idx3[:]))
+            step = HALF if i in (0, ROW_TILES - 1) else J
+            for lo in range(0, J, step):
+                nc.vector.tensor_copy(
+                    x[:, lo : lo + step], a_rows[:].indirect(entries(idx3, lo, lo + step))
+                )
             x_tiles.append(x)
 
         def by_halves(row, part):
@@ -390,14 +395,18 @@ def tile_list_duplex_cancel_filter_kernel(
         row_tile(0)
         x_first = by_halves(x_tiles[0], halves[0])
         nc.gpsimd.tensor_tensor(gain_place(0, halves[0]), x_first, x_first, ALU.mult)
+        gain(0, halves[0])
         row_tile(1)
         row_tile(2, between=(2, lambda: square(0, halves[1])))
-        gain(0, both_halves)
+        gain(0, halves[1])
         product(0)
 
         for i in range(1, SCALAR_GAINS_FROM):
-            row_tile(i + SQUARE_LAG)
-            square(i, both_halves)
+            if i == 1:
+                row_tile(i + SQUARE_LAG, between=(3, lambda: square(1, both_halves)))
+            else:
+                row_tile(i + SQUARE_LAG)
+                square(i, both_halves)
             gain(i, both_halves)
             product(i)
             if i == 2:

@@ -31,10 +31,10 @@ LOW_BANKS, HIGH_BANKS = (0, 1, 2, 3), (4, 5, 6, 7)
 ROW_RING = 4
 FIRST_XS = 256
 GPSIMD_COLS = (256, 704)
-FIRST_V1 = 256
+FIRST_V1 = 384
 SCALAR_GAINS_FROM = 4
 SQUARE_LAG = 2
-VECTOR_COLS = {(3, 0): BANK, (4, 3): BANK // 4, (7, 2): BANK, (7, 3): BANK}
+VECTOR_COLS = {(3, 0): BANK, (4, 3): BANK // 2, (7, 2): BANK, (7, 3): BANK}
 Y_COLS = 256
 PIECES = J // Y_COLS
 
@@ -62,7 +62,7 @@ def tile_list_duplex_cancel_filter_kernel(
 
         def load_scale_rows(scales, name, engine):
             rows = tile([P, scales.shape[2]], U8, name)
-            nc.sync.dma_start(
+            nc.scalar.dma_start(
                 out=rows[0:32, :].bitcast(I32), in_=scales.rearrange("a q c -> (a q) c").bitcast(I32)
             )
             engine.memset(rows[32:64, :].bitcast(I32), 0)

from contextlib import ExitStack

import concourse.mybir as mybir

K, K2, H, N, T, T2, S, J = 1024, 512, 1024, 384, 2048, 2048, 1024, 1024
FLOPS = 2 * (K2 * H * T2 + K * H * J + H * N * J)

F32 = mybir.dt.float32
BF16 = mybir.dt.bfloat16
I32 = mybir.dt.int32
U32 = mybir.dt.uint32
U16 = mybir.dt.uint16
U8 = mybir.dt.uint8
FP8X4 = mybir.dt.float8_e4m3fn_x4
FP4X4 = mybir.dt.float4_e2m1fn_x4
ACT = mybir.ActivationFunctionType
ALU = mybir.AluOpType

P = 128
LANES = 4
PASSES = 2
BANK = 512
QUADRANT = 32
BLOCKS = 16
ALIGN = 64
LINE = 4
ROW_TILES = PASSES * LANES
HALF = J // 2
B_COLS = BANK // LANES
LOW_BANKS, HIGH_BANKS = (0, 1, 2, 3), (4, 5, 6, 7)
ROW_RING = 4
FIRST_XS = 256
GPSIMD_COLS = (256, 704)
FIRST_V1 = 384
SCALAR_GAINS_FROM = 4
SQUARE_LAG = 2
VECTOR_COLS = {(3, 0): BANK, (4, 3): BANK // 2, (7, 2): BANK, (7, 3): BANK}
Y_COLS = 256
PIECES = J // Y_COLS


def tile_list_duplex_cancel_filter_kernel(
    tc, tab_words, tab_scales, offs, offs2, offs3, xs, base, wtx, cub,
    wrx_words, wrx_scales, wdem_words, wdem_scales, bdem, out,
):
    nc = tc.nc
    with ExitStack() as ctx:
        lists = ctx.enter_context(tc.tile_pool(name="lists", bufs=1))
        sb = ctx.enter_context(tc.tile_pool(name="sb", bufs=1))
        psum = ctx.enter_context(tc.psum_pool(name="psum", bufs=1))

        def tile(shape, dtype, name, tag=None, bufs=1):
            return sb.tile(shape, dtype, name=name, tag=tag or name, bufs=bufs, align_bytes=ALIGN)

        def bank(shape, number):
            return psum.tile(shape, F32, name=f"bank{number}")

        def zeroed_plane(width, name):
            plane = tile([P, width], U8, name)
            nc.vector.memset(plane[:].bitcast(I32), 0)
            return plane

        def load_scale_rows(scales, name, engine):
            rows = tile([P, scales.shape[2]], U8, name)
            nc.scalar.dma_start(
                out=rows[0:32, :].bitcast(I32), in_=scales.rearrange("a q c -> (a q) c").bitcast(I32)
            )
            engine.memset(rows[32:64, :].bitcast(I32), 0)
            engine.memset(rows[64:128, :].bitcast(I32), 0)
            return rows

        def spread_scale_rows(planes, rows):
            for a in range(PASSES):
                for quad in range(P // QUADRANT):
                    first = BLOCKS * a + 4 * quad
                    nc.sync.dma_start(
                        out=planes[a][QUADRANT * quad : QUADRANT * quad + 4, :].bitcast(I32),
                        in_=rows[first : first + 4, :].bitcast(I32),
                    )

        def entries(offsets, lo, hi):
            return offsets[:, lo // 16 : hi // 16]

        idx = lists.tile([P, J // 16], U16, name="idx")
        idx2 = lists.tile([P, S // 16], U16, name="idx2")
        idx3 = lists.tile([P, J // 16], U16, name="idx3")

        nc.sync.dma_start(idx[:], offs)
        tab_rows = load_scale_rows(tab_scales, "tab_rows", nc.vector)
        v_rows = tile([P, J], U8, "v_rows")
        nc.vector.tensor_copy(v_rows[:], tab_rows[:].indirect(idx[:]))

        base_lanes = base.rearrange("(p t) c -> p t c", t=LANES)
        xs_lanes = xs.rearrange("(p t) c -> p t c", t=LANES)
        page = [tile([P, T2], F32, f"page{t}", tag="row", bufs=ROW_RING) for t in range(LANES)]
        xs_pieces = [(0, 0, FIRST_XS), (0, FIRST_XS, S)]
        xs_pieces = xs_pieces + [(t, 0, S) for t in range(1, LANES)]
        xs_tiles = [tile([P, hi - lo], F32, f"xs{t}_{lo}") for t, lo, hi in xs_pieces]
        wtx_raw = [tile([P, LANES, BANK], F32, f"wtx_raw{g}") for g in range(PASSES)]
        wrx_raw = tile([P, PASSES, 2 * H], U8, "wrx_raw")

        def load_wtx(g):
            nc.sync.dma_start(
                out=wtx_raw[g][:],
                in_=wtx[:, BANK * g : BANK * (g + 1)].rearrange("(p i) c -> p i c", i=LANES),
            )

        for (t, lo, hi), xs_tile in zip(xs_pieces, xs_tiles):
            if lo == 0:
                nc.sync.dma_start(out=page[t][:], in_=base_lanes[:, t, :])
            if hi == FIRST_XS:
                nc.sync.dma_start(idx2[:], offs2)
            nc.sync.dma_start(out=xs_tile[:], in_=xs_lanes[:, t, lo:hi])
            if hi == FIRST_XS:
                wrx_rows_raw = load_scale_rows(wrx_scales, "wrx_rows_raw", nc.gpsimd)
            if t < PASSES and hi == S:
                load_wtx(t)
        nc.sync.dma_start(
            out=wrx_raw[:].bitcast(I32), in_=wrx_words.rearrange("a p c -> p a c").bitcast(I32)
        )
        wrx_rows = tile([P, H], U8, "wrx_rows")
        nc.gpsimd.tensor_copy(
            out=wrx_rows[:].rearrange("p (g t m) -> p g t m", t=LANES, m=P),
            in_=wrx_rows_raw[:].rearrange("p (g m t) -> p g t m", t=LANES, m=P),
        )
        wdem_planes = zeroed_plane(N, "wdem_planes")
        v_plane = [zeroed_plane(J, f"v_plane{a}") for a in range(PASSES)]
        wrx_plane = [zeroed_plane(H, f"wrx_plane{a}") for a in range(PASSES)]

        tab = [tile([P, T], U32, f"tab{a}") for a in range(PASSES)]
        for a in range(PASSES):
            nc.sync.dma_start(
                out=tab[a][:].bitcast(I32),
                in_=tab_words[a].rearrange("p n i -> p (n i)").bitcast(I32),
            )
        nc.sync.dma_start(idx3[:], offs3)
        cub_cols = tile([P, PASSES, LANES], F32, "cub_cols")
        nc.sync.dma_start(out=cub_cols[:], in_=cub.rearrange("(g p t) -> p g t", g=PASSES, t=LANES))
        wdem = tile([P, PASSES, N], U32, "wdem")
        nc.sync.dma_start(
            out=wdem[:].bitcast(I32), in_=wdem_words.rearrange("a p c i -> p a (c i)").bitcast(I32)
        )
        for quad in range(P // QUADRANT):
            nc.sync.dma_start(
                out=wdem_planes[QUADRANT * quad : QUADRANT * quad + 4 * PASSES, :].bitcast(I32),
                in_=wdem_scales[:, 4 * quad : 4 * quad + 4, :].bitcast(I32),
            )
        bias_cols = tile([P, N // P], F32, "bias_cols")
        with nc.allow_non_contiguous_dma(reason="one bias value to a partition"):
            nc.sync.dma_start(out=bias_cols[:], in_=bdem.rearrange("(n p) -> p n", p=P))
        spread_scale_rows(v_plane, v_rows)
        spread_scale_rows(wrx_plane, wrx_rows)

        wtx_bf = [tile([P, LANES * BANK], BF16, f"wtx_bf{g}") for g in range(PASSES)]
        for g in range(PASSES):
            nc.scalar.activation(
                out=wtx_bf[g][:].rearrange("p (t m i) -> p m i t", t=LANES, i=LANES),
                in_=wtx_raw[g][:].rearrange("p i (m t) -> p m i t", t=LANES),
                func=ACT.Identity,
            )

        page_bf = tile([P, T2, LANES], BF16, "page_bf", tag="wtx_raw0")
        for (t, lo, hi), xs_tile in zip(xs_pieces, xs_tiles):
            nc.vector.tensor_copy(page[t][:].indirect(entries(idx2, lo, hi)), xs_tile[:])
            if hi == S:
                split = T2 - GPSIMD_COLS[t // 2]
                step = BANK if t == LANES - 1 else split
                for c0 in range(0, split, step):
                    c1 = min(c0 + step, split)
                    nc.scalar.copy(out=page_bf[:, c0:c1, t], in_=page[t][:, c0:c1])
                nc.gpsimd.tensor_scalar(
                    page_bf[:, split:, t], page[t][:, split:], 1.0, 0.0, ALU.mult, ALU.add
                )

        v0 = tile([P, J], U32, "v0")
        nc.vector.tensor_copy(v0[:], tab[0][:].indirect(idx[:]))
        codes = tile([P, T2 + H], U32, "codes", tag="tab0")
        page_codes, wtx_codes = codes[:, :T2], codes[:, T2:]
        plane_starts = (0, LANES, LANES + 1, ROW_TILES)
        wtx_plane = [
            tile([P, P * (hi - lo)], U8, f"wtx_plane{lo}")
            for lo, hi in zip(plane_starts, plane_starts[1:])
        ]

        def wtx_scales(first, end):
            part = max(u for u, lo in enumerate(plane_starts) if lo <= first)
            lo = plane_starts[part]
            return wtx_plane[part][:, P * (first - lo) : P * (end - lo)]

        page_plane = tile([P, T2], U8, "page_plane")

        def quantise_wtx(first, end):
            g, t = divmod(first, LANES)
            nc.vector.quantize_mx(
                out=wtx_codes[:, P * first : P * end].bitcast(FP8X4),
                scales=wtx_scales(first, end),
                in_=wtx_bf[g][:, LANES * P * t : LANES * P * (t + end - first)],
            )

        def quantise_page(cols):
            nc.vector.quantize_mx(
                out=page_codes[:, cols].bitcast(FP8X4),
                scales=page_plane[:, cols],
                in_=page_bf[:, cols, :].rearrange("p c t -> p (c t)"),
            )

        page_pieces = [slice(c0, c0 + BANK) for c0 in (T2 - BANK, *range(0, T2 - BANK, BANK))]
        quantise_wtx(0, 1)
        for cols in page_pieces:
            quantise_page(cols)
        quantise_wtx(1, LANES)
        quantise_wtx(LANES, LANES + 1)
        quantise_wtx(LANES + 1, ROW_TILES)
        v1_first = tile([P, FIRST_V1], U32, "v1_first")
        nc.vector.tensor_copy(v1_first[:], tab[1][:].indirect(entries(idx, 0, FIRST_V1)))

        wrx = tile([P, PASSES, 2 * H], U8, "wrx", tag="wtx_bf1")
        wrx_to = wrx[:].rearrange("p a c -> p (a c)").bitcast(U16)
        wrx_from = wrx_raw[:].rearrange("p a c -> p (a c)").bitcast(U16)
        nc.gpsimd.tensor_copy(
            out=wrx_to.rearrange("p (h t m) -> p h t m", t=LANES, m=P),
            in_=wrx_from.rearrange("p (h m t) -> p h t m", t=LANES, m=P),
        )

        leak0 = tile([P, LANES, J], F32, "leak0")
        leak1 = tile([P, 2, LANES, HALF], F32, "leak1")
        gain_rows = tile([P, 2, J], F32, "gain_rows", tag="wtx_raw0")
        x_last = tile([P, 2, J], F32, "x_last")
        square_apart = tile([P, HALF], F32, "square_apart")
        out_rows = out.rearrange("(n p) j -> p n j", p=P)
        held_tags = {ROW_TILES - 1: "tab1"}
        x_tags = ("xs3_0", "xs1_0", "wrx_raw", "wtx_raw1")
        both_halves, halves = slice(0, 2), (slice(0, 1), slice(1, 2))
        x_tiles = []

        def row_tile(i, between=None):
            if i in held_tags:
                a_rows = tile([P, T2], F32, f"a{i}", tag=held_tags[i])
            else:
                a_rows = tile([P, T2], F32, f"a{i}", tag="row", bufs=ROW_RING)
            banks = HIGH_BANKS if i % 2 else LOW_BANKS
            for place, cols in enumerate(page_pieces):
                if between is not None and place == between[0]:
                    between[1]()
                acc = bank([P, BANK], banks[place])
                nc.tensor.matmul_mx(
                    out=acc[:],
                    lhsT=wtx_codes[:, P * i : P * (i + 1)].bitcast(FP8X4),
                    lhsT_scale=wtx_scales(i, i + 1),
                    rhs=page_codes[:, cols].bitcast(FP8X4), rhs_scale=page_plane[:, cols],
                    start=True, stop=True,
                )
                share = VECTOR_COLS.get((i, place), 0)
                if share:
                    nc.vector.tensor_copy(out=a_rows[:, cols][:, :share], in_=acc[:, :share])
                if share < BANK:
                    nc.scalar.copy(out=a_rows[:, cols][:, share:], in_=acc[:, share:])
            if i < ROW_TILES - 2:
                x = tile([P, J], F32, f"x{i}", tag=x_tags[i] if i < len(x_tags) else None)[:]
            else:
                x = x_last[:, i - (ROW_TILES - 2), :]
            step = HALF if i in (0, ROW_TILES - 1) else J
            for lo in range(0, J, step):
                nc.vector.tensor_copy(
                    x[:, lo : lo + step], a_rows[:].indirect(entries(idx3, lo, lo + step))
                )
            x_tiles.append(x)

        def by_halves(row, part):
            return row.rearrange("p (h j) -> p h j", j=HALF)[:, part, :]

        def leak_place(i, part):
            g, t = divmod(i, LANES)
            return by_halves(leak0[:, t, :], part) if g == 0 else leak1[:, part, t, :]

        def gain_place(i, part):
            if LANES <= i < ROW_TILES - 2:
                return by_halves(gain_rows[:, i - LANES, :], part)
            return leak_place(i, part)

        def square_place(i, part):
            if (i, part) == (5, halves[0]):
                return by_halves(square_apart[:], part)
            return gain_place(i, part)

        def square(i, part):
            nc.scalar.activation(
                out=square_place(i, part), in_=by_halves(x_tiles[i], part), func=ACT.Square
            )

        def gain(i, part):
            y = gain_place(i, part)
            g, t = divmod(i, LANES)
            cub_col = cub_cols[:, g, t : t + 1]
            if i >= SCALAR_GAINS_FROM:
                nc.scalar.activation(
                    out=y, in_=square_place(i, part), func=ACT.Identity, scale=cub_col, bias=1.0
                )
            else:
                nc.gpsimd.tensor_scalar(y, y, cub_col, 1.0, ALU.mult, ALU.add)

        def product(i):
            nc.gpsimd.tensor_tensor(
                leak_place(i, both_halves), gain_place(i, both_halves),
                by_halves(x_tiles[i], both_halves), ALU.mult,
            )

        def project_received(g, half, numbers):
            banks = []
            for quarter, number in enumerate(numbers):
                j0 = HALF * half + B_COLS * quarter
                cols = slice(j0, j0 + B_COLS)
                if j0 < FIRST_V1:
                    words = (v0[:, cols], v1_first[:, cols])
                else:
                    words = (v0[:, cols], v1_rest[:, j0 - FIRST_V1 : j0 - FIRST_V1 + B_COLS])
                b = bank([P, LANES, B_COLS], number)
                for t in range(LANES):
                    r0 = P * (LANES * g + t)
                    for a in range(PASSES):
                        nc.tensor.matmul_mx(
                            out=b[:, t, :],
                            lhsT=wrx[:, a, 2 * r0 : 2 * (r0 + P)].bitcast(FP4X4),
                            lhsT_scale=wrx_plane[a][:, r0 : r0 + P],
                            rhs=words[a].bitcast(FP8X4), rhs_scale=v_plane[a][:, cols],
                            start=(a == 0), stop=(a == PASSES - 1),
                        )
                banks.append((j0, b))
            return banks

        def subtract(g, banks):
            for j0, b in banks:
                half, in_half = divmod(j0, HALF)
                piece, in_piece = divmod(j0, Y_COLS)
                if g == 0:
                    leak = leak0[:, :, j0 : j0 + B_COLS]
                else:
                    leak = leak1[:, half, :, in_half : in_half + B_COLS]
                nc.vector.tensor_tensor(
                    resid[:, piece, g, in_piece : in_piece + B_COLS, :].rearrange(
                        "p (c i) t -> p c t i", i=LINE
                    ),
                    b[:].rearrange("p t (c i) -> p c t i", i=LINE),
                    leak.rearrange("p t (c i) -> p c t i", i=LINE),
                    ALU.subtract,
                )

        def quantise_resid(piece, passes, tag=None):
            count = passes.stop - passes.start
            name = f"{piece}_{passes.start}"
            resid_codes = tile([P, count, Y_COLS], U32, f"resid_codes{name}", tag=tag)
            resid_plane = tile([P, count, Y_COLS], U8, f"resid_plane{name}")
            nc.vector.quantize_mx(
                out=resid_codes[:].rearrange("p g c -> p (g c)").bitcast(FP8X4),
                scales=resid_plane[:].rearrange("p g c -> p (g c)"),
                in_=resid[:, piece, passes].rearrange("p g c t -> p (g c t)"),
            )
            return [(resid_codes[:, g, :], resid_plane[:, g, :]) for g in range(count)]

        def filter_and_store(piece, operands, numbers):
            cols = slice(Y_COLS * piece, Y_COLS * (piece + 1))
            last = piece == PIECES - 1
            store_by_tiles = piece >= PIECES - 2
            staged = tile([P, N // P, Y_COLS], F32, f"staged{piece}")
            groups = ((0,), (1,), (2,)) if last else ((0,), (1, 2)) if piece == 0 else ((0, 1), (2,))
            for group, number in zip(groups, numbers):
                y = bank([P, len(group), Y_COLS], number)
                for place, n in enumerate(group):
                    rows = slice(P * n, P * (n + 1))
                    for g in range(PASSES):
                        nc.tensor.matmul_mx(
                            out=y[:, place, :],
                            lhsT=wdem[:, g, rows].bitcast(FP8X4),
                            lhsT_scale=wdem_planes[4 * g : P, rows],
                            rhs=operands[g][0].bitcast(FP8X4), rhs_scale=operands[g][1],
                            start=(g == 0), stop=(g == PASSES - 1),
                        )
                for place, n in enumerate(group):
                    bias = bias_cols[:, n : n + 1]
                    if last and n == 1:
                        nc.vector.tensor_scalar(staged[:, n, :], y[:, place, :], bias, None, ALU.add)
                    else:
                        nc.scalar.activation(
                            out=staged[:, n, :], in_=y[:, place, :], func=ACT.Identity, bias=bias
                        )
                    if piece == 0 and n == 0:
                        nc.sync.dma_start(out=out_rows[:, 0, cols], in_=staged[:, 0, :])
                    if store_by_tiles:
                        queue = nc.scalar if last and n == 2 else nc.sync
                        queue.dma_start(out=out_rows[:, n, cols], in_=staged[:, n, :])
            if not store_by_tiles:
                first = 1 if piece == 0 else 0
                nc.sync.dma_start(out=out_rows[:, first:, cols], in_=staged[:, first:, :])

        row_tile(0)
        x_first = by_halves(x_tiles[0], halves[0])
        nc.gpsimd.tensor_tensor(gain_place(0, halves[0]), x_first, x_first, ALU.mult)
        gain(0, halves[0])
        row_tile(1)
        row_tile(2, between=(2, lambda: square(0, halves[1])))
        gain(0, halves[1])
        product(0)

        for i in range(1, SCALAR_GAINS_FROM):
            if i == 1:
                row_tile(i + SQUARE_LAG, between=(3, lambda: square(1, both_halves)))
            else:
                row_tile(i + SQUARE_LAG)
                square(i, both_halves)
            gain(i, both_halves)
            product(i)
            if i == 2:
                v1_rest = tile([P, J - FIRST_V1], U32, "v1_rest", tag="wtx_plane4")
                nc.vector.tensor_copy(v1_rest[:], tab[1][:].indirect(entries(idx, FIRST_V1, J)))

        row_tile(ROW_TILES - 2)
        square(4, both_halves)
        row_tile(ROW_TILES - 1, between=(1, lambda: gain(4, both_halves)))
        product(4)
        b_first = [project_received(0, 0, LOW_BANKS), project_received(0, 1, HIGH_BANKS)]
        for step in (square, gain):
            for half in halves:
                step(5, half)
        resid = tile([P, PIECES, PASSES, Y_COLS, LANES], BF16, "resid", tag="square_apart")
        subtract(0, b_first[0])
        b_second = [project_received(1, 0, LOW_BANKS)]
        product(5)
        for half in range(2):
            for step in (square, gain):
                for i in range(ROW_TILES - 2, ROW_TILES):
                    step(i, halves[half])
            y = leak1[:, half, 2:, :]
            nc.gpsimd.tensor_tensor(y, y, x_last[:, :, HALF * half : HALF * (half + 1)], ALU.mult)
        subtract(0, b_first[1])
        subtract(1, b_second[0])
        b_second.append(project_received(1, 1, HIGH_BANKS[:2] + LOW_BANKS[:2]))

        both_passes, first_pass, second_pass = slice(0, 2), slice(0, 1), slice(1, 2)
        filter_and_store(0, quantise_resid(0, both_passes), HIGH_BANKS[2:])
        filter_and_store(1, quantise_resid(1, both_passes), LOW_BANKS[2:])
        subtract(1, b_second[1][:3])
        filter_and_store(2, quantise_resid(2, both_passes), HIGH_BANKS[:2])
        subtract(1, b_second[1][3:])
        last_operands = quantise_resid(3, first_pass, "x_last") + quantise_resid(3, second_pass)
        filter_and_store(3, last_operands, HIGH_BANKS[2:] + LOW_BANKS[2:3])
